import numpy as np
import ml_dtypes


def mxq(x, axis, fmt="e4m3"):
    dtype, down = {"e4m3": (ml_dtypes.float8_e4m3fn, 7), "e5m2": (ml_dtypes.float8_e5m2, 14)}[fmt]
    v = np.moveaxis(np.asarray(x, np.float32).astype(ml_dtypes.bfloat16).astype(np.float64), axis, -1)
    blocks = v.reshape(v.shape[:-1] + (-1, 32))
    amax = np.abs(blocks).max(-1, keepdims=True)
    byte = np.maximum(np.where(amax > 0, np.frexp(amax)[1] - 1 + 127, 0) - down, 1)
    scale = np.exp2(byte - 127.0)
    codes = (blocks / scale).astype(np.float32).astype(dtype).astype(np.float64)
    return np.moveaxis((codes * scale).reshape(v.shape), -1, axis)


WIDE = False


def mx_kscale(k):
    if not WIDE:
        return np.ones(k)
    levels = np.array([10, -10, 5, -5, 0])
    if k % 512:
        return np.exp2(np.random.permutation(np.resize(levels, k // 32))).repeat(32)
    a = np.empty((k // 512, 16))
    for p in range(k // 512):
        a[p, :8] = np.random.permutation(np.resize(levels, 8))
        for g in range(8):
            far = levels[np.abs(levels - a[p, g]) >= 10]
            a[p, g + 8] = far[np.random.randint(len(far))]
    return np.exp2(a.ravel()).repeat(32)


def f64(x):
    return np.asarray(x).astype(np.float64)


def striped(idx):
    return np.tile(idx.reshape(-1, 16).T, (8, 1)).astype(np.uint16)


def unstriped(offs):
    return offs[:16].T.reshape(-1).astype(np.int64)


E2M1 = np.array([0.0, 0.5, 1.0, 1.5, 2.0, 3.0, 4.0, 6.0, -0.0, -0.5, -1.0, -1.5, -2.0, -3.0, -4.0, -6.0])


def pack_weight(w, fmt):
    k, n = w.shape
    w = f64(np.asarray(w, np.float32).astype(ml_dtypes.bfloat16)).reshape(k // 32, 32, n)
    amax = np.abs(w).max(1)
    if fmt == "e4m3":
        byte = np.frexp(amax)[1] - 1 + 127 - 7
    else:
        mant, ex = np.frexp(amax / 6.0)
        byte = np.where(mant > 0.5, ex, ex - 1) + 127
    byte = np.clip(np.where(amax > 0, byte, 1), 1, 254)
    scaled = (w * np.exp2(127.0 - byte)[:, None, :]).reshape(k, n).astype(np.float32)
    by_word = np.ascontiguousarray(scaled.reshape(k // 512, 128, 4, n).transpose(0, 1, 3, 2))
    if fmt == "e4m3":
        words = by_word.astype(ml_dtypes.float8_e4m3fn).view(np.uint8)
    else:
        c = by_word.astype(ml_dtypes.float4_e2m1fn).view(np.uint8) & 0xF
        words = (c[..., 0::2] | (c[..., 1::2] << 4)).reshape(k // 512, 128, 2 * n)
    return np.ascontiguousarray(words), np.ascontiguousarray(byte.astype(np.uint8).reshape(k // 512, 16, n))


def unpack_weight(words, scales, fmt):
    g, _, n = scales.shape
    words = np.ascontiguousarray(words).reshape(g, 128, n, -1)
    if fmt == "e4m3":
        vals = words.view(ml_dtypes.float8_e4m3fn).astype(np.float64)
    else:
        nib = np.empty((g, 128, n, 4), np.uint8)
        nib[..., 0::2] = words & 0xF
        nib[..., 1::2] = words >> 4
        vals = E2M1[nib]
    vals = vals * np.repeat(np.exp2(scales.astype(np.float64) - 127.0), 8, axis=1)[..., None]
    return vals.transpose(0, 1, 3, 2).reshape(g * 512, n)


def silu(v):
    return v / (1.0 + np.exp(-np.maximum(v, -700.0)))


K, T, E, C, N = 2560, 384, 12, 128, 256
TOP = 4
K8 = 1024


def by_expert(wq, xq):
    return np.concatenate([wq[e].T @ xq[:, e * C:(e + 1) * C] for e in range(E)], axis=1)


def setup_inputs():
    n = np.random.standard_normal
    s = mx_kscale(K)[:, None]
    deal = np.repeat(np.arange(E), C).reshape(TOP, T)[:, np.random.permutation(T)]
    deal = np.take_along_axis(deal, np.argsort(np.random.rand(TOP, T), axis=0), axis=0)
    for _ in range(8):
        s_, t_ = np.random.permutation(T).reshape(2, -1); r = np.random.randint(TOP, size=T // 2); x, y = deal[r, s_].copy(), deal[r, t_].copy()
        ok = ~((deal[:, s_] == y).any(0) | (deal[:, t_] == x).any(0)); deal[r[ok], s_[ok]] = y[ok]; deal[r[ok], t_[ok]] = x[ok]
    order = np.lexsort((np.random.rand(TOP * T), deal.reshape(-1)))
    slot_token = order % T; pos = np.empty(TOP * T, np.int64); pos[order] = np.arange(TOP * T); pos = pos.reshape(TOP, T)
    g = np.random.uniform(0.5, 1.5, (TOP, T)); g = g / g.sum(0)
    w = n((E, K, N)) / np.sqrt(K) / s[None]
    w8 = [pack_weight(m[:K8], "e4m3") for m in w]
    w4 = [pack_weight(m[K8:], "e2m1") for m in w]
    return {
        "xT": (n((K, T)) * s).astype(np.float32),
        "w8_words": np.stack([m[0] for m in w8]),
        "w8_scales": np.stack([m[1] for m in w8]),
        "w4_words": np.stack([m[0] for m in w4]),
        "w4_scales": np.stack([m[1] for m in w4]),
        "b": (0.3 * n((N, E))).astype(np.float32),
        "gate": np.stack([np.tile(r, (N, 1)) for r in g]).astype(np.float32),
        "offs": striped(slot_token),
        "pos1": striped(pos[0]),
        "pos2": striped(pos[1]),
        "pos3": striped(pos[2]),
        "pos4": striped(pos[3]),
    }


def reference(xT, w8_words, w8_scales, w4_words, w4_scales, b, gate, offs, pos1, pos2, pos3, pos4):
    idx = unstriped(offs)
    w = np.stack([np.concatenate([unpack_weight(w8_words[e], w8_scales[e], "e4m3"), unpack_weight(w4_words[e], w4_scales[e], "e2m1")]) for e in range(E)])
    xq = mxq(f64(xT)[:, idx], 0, "e4m3")
    y = by_expert(w, xq)
    y = silu(y + np.repeat(f64(b), C, axis=1))
    return sum(f64(gate[r]) * y[:, unstriped(p)] for r, p in enumerate((pos1, pos2, pos3, pos4)))

@@ -1,0 +1,246 @@
+from contextlib import ExitStack
+
+import concourse.mybir as mybir
+
+K, T, E, C, N, TOP = 2560, 384, 12, 128, 256, 4
+S = E * C
+P = 128
+PASSES, PASSES8 = 5, 2
+PASSES4 = PASSES - PASSES8
+HALVES = N // P
+FLOPS = 2 * S * K * N
+BYTES = 4 * K * T + E * N * (PASSES8 * (512 + 16) + PASSES4 * (256 + 16)) + 4 * N * E + 4 * TOP * T + 2 * P * (S + TOP * T) // 16 + 4 * N * T
+
+F32 = mybir.dt.float32
+BF16 = mybir.dt.bfloat16
+I32 = mybir.dt.int32
+U32 = mybir.dt.uint32
+U16 = mybir.dt.uint16
+U8 = mybir.dt.uint8
+FP8X4 = mybir.dt.float8_e4m3fn_x4
+FP4X4 = mybir.dt.float4_e2m1fn_x4
+COPY = mybir.ActivationFunctionType.Copy
+SILU = mybir.ActivationFunctionType.Silu
+MULT = mybir.AluOpType.mult
+ADD = mybir.AluOpType.add
+
+WINDOW = 1024
+PAD = WINDOW - T
+PLANE_WINDOW = 1536
+W8_ROW = 4
+PLANE_ROW = (4, 12, 0, 8, 0)
+PACK_OF = (0, 0, 0, 0, 1)
+PACKS = 2
+SHIFTED = 3
+EARLY = 2
+BATCHES = ((0, 4), (4, 8), (8, 12))
+
+
+def tile_moe_tk_lin_silu_kernel(tc, xT, w8_words, w8_scales, w4_words, w4_scales, b, gate, offs, pos1, pos2, pos3, pos4, out):
+    nc = tc.nc
+    with ExitStack() as ctx:
+        lists = ctx.enter_context(tc.tile_pool(name="lists", bufs=1))
+        keep = ctx.enter_context(tc.tile_pool(name="keep", bufs=1))
+        psum = ctx.enter_context(tc.psum_pool(name="psum", bufs=8))
+
+        offs_sb = lists.tile([P, S // 16], U16, name="offs_sb")
+        pos_sb = [lists.tile([P, T // 16], U16, name=f"pos_sb{r}") for r in range(TOP)]
+
+        words = keep.tile([P, PASSES * T + PAD], I32, name="words", align_bytes=64)
+        planes = keep.tile([P, (PACKS - 1) * T + PLANE_WINDOW], U8, name="planes", align_bytes=64)
+        w8 = keep.tile([P, E * PASSES8, 4 * N], U8, name="w8", align_bytes=64)
+        w4 = keep.tile([P, E * PASSES4, 2 * N], U8, name="w4", align_bytes=64)
+        w8s = keep.tile([P, E * PASSES8, N], U8, name="w8s", align_bytes=64)
+        w4s = keep.tile([P, E * PASSES4, N], U8, name="w4s", align_bytes=64)
+        bias = keep.tile([P, HALVES, E], F32, name="bias")
+        gates = keep.tile([P, TOP, T], F32, name="gates")
+        raw = [keep.tile([P, 4, T], F32, name=f"raw{a}") for a in range(PASSES)]
+        grouped = [keep.tile([P, T, 4], BF16, name=f"grouped{a}", align_bytes=64) for a in range(PASSES)]
+        early_words = [keep.tile([P, S], U32, name=f"early_words{a}", align_bytes=64) for a in range(EARLY)]
+        slot_planes = [keep.tile([P, S], U8, name=f"slot_planes{q}", align_bytes=64) for q in range(PACKS)]
+        shifted = keep.tile([P, S], U8, name="shifted", align_bytes=64)
+        y = [keep.tile([P, S], F32, name=f"y{h}") for h in range(HALVES)]
+        dummy = keep.tile([P, 1], F32, name="dummy")
+
+        x_rows = xT.rearrange("(a p j) t -> a p j t", p=P, j=4)
+        nc.sync.dma_start(out=raw[0][:, :, 0:256], in_=x_rows[0][:, :, 0:256])
+        nc.sync.dma_start(out=raw[0][:, :, 256:T], in_=x_rows[0][:, :, 256:T])
+        nc.sync.dma_start(offs_sb[:], offs)
+
+        nc.vector.memset(dummy[:], 0.0)
+        nc.scalar.activation(dummy[:], dummy[:], SILU)
+        nc.vector.memset(planes[:].bitcast(I32), 0)
+        nc.vector.memset(words[:, PASSES * T :], 0)
+        nc.vector.memset(w8s[:].rearrange("p e n -> p (e n)").bitcast(I32), 0)
+        nc.vector.memset(w4s[:].rearrange("p e n -> p (e n)").bitcast(I32), 0)
+        nc.vector.memset(shifted[:].bitcast(I32), 0)
+
+        w8_rows = w8_words.rearrange("e a p n r -> p (e a) (n r)").bitcast(I32)
+        w4_rows = w4_words.rearrange("e a p n -> p (e a) n").bitcast(I32)
+        w8s_rows = w8_scales.rearrange("e a q n -> q (e a) n").bitcast(I32)
+        w4s_rows = w4_scales.rearrange("e a q n -> q (e a) n").bitcast(I32)
+        def load_w8(e0, e1):
+            rows = slice(e0 * PASSES8, e1 * PASSES8)
+            nc.sync.dma_start(out=w8[:, rows].bitcast(I32), in_=w8_rows[:, rows])
+
+        def load_w4(e0, e1):
+            rows = slice(e0 * PASSES4, e1 * PASSES4)
+            nc.sync.dma_start(out=w4[:, rows].bitcast(I32), in_=w4_rows[:, rows])
+
+        for r in range(4):
+            nc.gpsimd.dma_start(out=w8s[W8_ROW + r : P : 32].bitcast(I32), in_=w8s_rows[r:16:4])
+        for r in range(4):
+            nc.gpsimd.dma_start(out=w4s[r:P:32].bitcast(I32), in_=w4s_rows[r:16:4])
+        for a in range(1, PASSES):
+            nc.sync.dma_start(out=raw[a][:], in_=x_rows[a])
+        load_w8(0, 4)
+        load_w4(0, 4)
+        nc.sync.dma_start(out=bias[:], in_=b.rearrange("(h p) e -> p h e", p=P))
+        load_w8(4, 8)
+        load_w4(4, 8)
+        for r, pos in enumerate((pos1, pos2, pos3, pos4)):
+            nc.sync.dma_start(pos_sb[r][:], pos)
+        load_w8(8, 12)
+        load_w4(8, 12)
+        for r in range(TOP):
+            nc.sync.dma_start(out=gates[:, r, :], in_=gate[r, 0:P, :])
+
+        def interleave_scalar(a, t0, t1):
+            nc.scalar.activation(grouped[a][:, t0:t1, :], raw[a][:, :, t0:t1].rearrange("p j t -> p t j"), COPY)
+
+        def interleave_vector(a, t0, t1):
+            nc.vector.tensor_copy(out=grouped[a][:, t0:t1, :], in_=raw[a][:, :, t0:t1].rearrange("p j t -> p t j"))
+
+        def word_column(a):
+            return (PASSES - 1 - a) * T
+
+        def plane_column(q):
+            return (PACKS - 1 - q) * T
+
+        def quantise(a):
+            for t0, t1 in ((0, 256), (256, T)):
+                w0, s0 = word_column(a), plane_column(PACK_OF[a])
+                nc.vector.quantize_mx(
+                    out=words[:, w0 + t0 : w0 + t1].bitcast(FP8X4),
+                    scales=planes[PLANE_ROW[a] : P, s0 + t0 : s0 + t1],
+                    in_=grouped[a][:, t0:t1, :].rearrange("p t j -> p (t j)"),
+                )
+
+        def gather_words(a, dst, j0, j1):
+            w0 = word_column(a)
+            nc.vector.tensor_copy(
+                out=dst,
+                in_=words[:, w0 : w0 + WINDOW].bitcast(U32).indirect(offs_sb[:, j0 // 16 : j1 // 16]),
+            )
+
+        def gather_planes(q, j0, j1):
+            s0 = plane_column(q)
+            nc.vector.tensor_copy(
+                out=slot_planes[q][:, j0:j1],
+                in_=planes[:, s0 : s0 + (WINDOW if j1 - j0 <= 512 else PLANE_WINDOW)].indirect(offs_sb[:, j0 // 16 : j1 // 16]),
+            )
+
+        def shift_planes(j0, j1):
+            k = PLANE_ROW[SHIFTED]
+            nc.gpsimd.dma_start(
+                out=shifted[0:100, j0:j1].bitcast(I32),
+                in_=slot_planes[PACK_OF[SHIFTED]][k : k + 100, j0:j1].bitcast(I32),
+            )
+
+        def multiply(acc, a, e, h, moving):
+            cols = slice(e * C, (e + 1) * C)
+            if a < PASSES8:
+                i = e * PASSES8 + a
+                lhsT = w8[:, i, 4 * P * h : 4 * P * (h + 1)].bitcast(FP8X4)
+                lhsT_scale = w8s[W8_ROW:P, i, P * h : P * (h + 1)]
+            else:
+                i = e * PASSES4 + a - PASSES8
+                lhsT = w4[:, i, 2 * P * h : 2 * P * (h + 1)].bitcast(FP4X4)
+                lhsT_scale = w4s[:, i, P * h : P * (h + 1)]
+            nc.tensor.matmul_mx(
+                out=acc[:],
+                lhsT=lhsT,
+                lhsT_scale=lhsT_scale,
+                rhs=moving.bitcast(FP8X4),
+                rhs_scale=shifted[:, cols] if a == SHIFTED else slot_planes[PACK_OF[a]][PLANE_ROW[a] : P, cols],
+                start=(a == 0),
+                stop=(a == PASSES - 1),
+            )
+
+        interleave_scalar(0, 0, 128)
+        interleave_vector(0, 128, 256)
+        interleave_vector(0, 256, T)
+        for a in range(1, PASSES):
+            interleave_scalar(a, 0, T)
+        quantise(0)
+        for a in range(EARLY):
+            for j in range(0, S, S // 2):
+                gather_words(a, early_words[a][:, j : j + S // 2], j, j + S // 2)
+            quantise(a + 1)
+        quantise(3)
+
+        for e0, e1 in BATCHES:
+            j0, j1 = e0 * C, e1 * C
+            if e0 == BATCHES[1][0]:
+                gather_planes(0, j0, S)
+                shift_planes(j0, S)
+            if e0 > 0:
+                gather_planes(1, j0, j1)
+            batch_words = {a: early_words[a][:, j0:j1] for a in range(EARLY)}
+            for a in range(EARLY, PASSES):
+                tile = keep.tile([P, j1 - j0], U32, name=f"batch_words{a}", align_bytes=64)
+                batch_words[a] = tile[:]
+            gather_words(2, batch_words[2], j0, j1)
+            if e0 == 0:
+                gather_planes(0, j0, j1)
+                shift_planes(j0, j1)
+                quantise(4)
+            gather_words(3, batch_words[3], j0, j1)
+            if e0 == 0:
+                gather_planes(1, j0, j1)
+            accs = {}
+            for e in range(e0, e1):
+                for h in range(HALVES):
+                    accs[e, h] = psum.tile([P, C], F32, name="acc")
+            for a in range(PASSES - 1):
+                for e in range(e0, e1):
+                    for h in range(HALVES):
+                        multiply(accs[e, h], a, e, h, batch_words[a][:, (e - e0) * C : (e - e0 + 1) * C])
+            for f0, f1 in ((e0, e1),) if e1 < E else ((e0, e0 + 2), (e0 + 2, e0 + 3), (e0 + 3, e1)):
+                gather_words(4, batch_words[4][:, (f0 - e0) * C : (f1 - e0) * C], f0 * C, f1 * C)
+                for e in range(f0, f1):
+                    for h in range(HALVES):
+                        multiply(accs[e, h], 4, e, h, batch_words[4][:, (e - e0) * C : (e - e0 + 1) * C])
+                        nc.scalar.activation(y[h][:, e * C : (e + 1) * C], accs[e, h][:], SILU, bias=bias[:, h, e : e + 1])
+
+        part = [[keep.tile([P, T], F32, name=f"part{h}_{r}") for r in range(TOP)] for h in range(HALVES)]
+        low = [keep.tile([P, T], F32, name=f"low{h}") for h in range(HALVES)]
+        three = [keep.tile([P, T], F32, name=f"three{h}") for h in range(HALVES)]
+        total = [keep.tile([P, T], F32, name=f"total{h}") for h in range(HALVES)]
+
+        def pick(h, r):
+            nc.vector.tensor_tensor(part[h][r][:], y[h][:].indirect(pos_sb[r][:]), gates[:, r, :], MULT)
+
+        def add(dst, a, b, t0=0, t1=T):
+            nc.vector.tensor_tensor(dst[:, t0:t1], a[:, t0:t1], b[:, t0:t1], ADD)
+
+        def store(h, t0=0, t1=T):
+            nc.sync.dma_start(out=out[h * P : (h + 1) * P, t0:t1], in_=total[h][:, t0:t1])
+
+        pick(0, 0)
+        pick(0, 1)
+        pick(0, 2)
+        add(low[0], part[0][0], part[0][1])
+        pick(0, 3)
+        add(three[0], low[0], part[0][2])
+        pick(1, 0)
+        add(total[0], three[0], part[0][3])
+        store(0)
+        pick(1, 1)
+        pick(1, 2)
+        add(low[1], part[1][0], part[1][1])
+        pick(1, 3)
+        add(three[1], low[1], part[1][2])
+        for t0 in (0, T // 2):
+            add(total[1], three[1], part[1][3], t0, t0 + T // 2)
+            store(1, t0, t0 + T // 2)

@@ -1,6 +1,7 @@
 from contextlib import ExitStack
 
 import concourse.mybir as mybir
+from concourse.masks import make_identity
 
 K, T, E, C, N, TOP = 2560, 384, 12, 128, 256, 4
 S = E * C
@@ -24,16 +25,17 @@ SILU = mybir.ActivationFunctionType.Silu
 MULT = mybir.AluOpType.mult
 ADD = mybir.AluOpType.add
 
-WINDOW = 1024
-PAD = WINDOW - T
-PLANE_WINDOW = 1536
 W8_ROW = 4
 PLANE_ROW = (4, 12, 0, 8, 0)
-PACK_OF = (0, 0, 0, 0, 1)
-PACKS = 2
 SHIFTED = 3
 EARLY = 2
-BATCHES = ((0, 4), (4, 8), (8, 12))
+BATCHES = ((0, 4), (4, 8), (8, 10), (10, 12))
+NARROW = 704
+WIDE = 1024
+WORD_COLUMN = (3 * T, 2 * T, T, 0, 3 * T + NARROW)
+WORD_COLUMNS = WORD_COLUMN[4] + NARROW
+PLANE_COLUMNS = 2 * NARROW
+CHUNKS = T // P
 
 
 def tile_moe_tk_lin_silu_kernel(tc, xT, w8_words, w8_scales, w4_words, w4_scales, b, gate, offs, pos1, pos2, pos3, pos4, out):
@@ -46,20 +48,20 @@ def tile_moe_tk_lin_silu_kernel(tc, xT, w8_words, w8_scales, w4_words, w4_scales
         offs_sb = lists.tile([P, S // 16], U16, name="offs_sb")
         pos_sb = [lists.tile([P, T // 16], U16, name=f"pos_sb{r}") for r in range(TOP)]
 
-        words = keep.tile([P, PASSES * T + PAD], I32, name="words", align_bytes=64)
-        planes = keep.tile([P, (PACKS - 1) * T + PLANE_WINDOW], U8, name="planes", align_bytes=64)
+        words = keep.tile([P, WORD_COLUMNS], I32, name="words", align_bytes=64)
+        planes = keep.tile([P, PLANE_COLUMNS], U8, name="planes", align_bytes=64)
         w8 = keep.tile([P, E * PASSES8, 4 * N], U8, name="w8", align_bytes=64)
         w4 = keep.tile([P, E * PASSES4, 2 * N], U8, name="w4", align_bytes=64)
-        w8s = keep.tile([P, E * PASSES8, N], U8, name="w8s", align_bytes=64)
-        w4s = keep.tile([P, E * PASSES4, N], U8, name="w4s", align_bytes=64)
+        ws = keep.tile([P, E * PASSES4, N], U8, name="ws", align_bytes=64)
         bias = keep.tile([P, HALVES, E], F32, name="bias")
         gates = keep.tile([P, TOP, T], F32, name="gates")
         raw = [keep.tile([P, 4, T], F32, name=f"raw{a}") for a in range(PASSES)]
         grouped = [keep.tile([P, T, 4], BF16, name=f"grouped{a}", align_bytes=64) for a in range(PASSES)]
-        early_words = [keep.tile([P, S], U32, name=f"early_words{a}", align_bytes=64) for a in range(EARLY)]
-        slot_planes = [keep.tile([P, S], U8, name=f"slot_planes{q}", align_bytes=64) for q in range(PACKS)]
+        slot_words = [keep.tile([P, S], U32, name=f"slot_words{a}", align_bytes=64) for a in range(PASSES)]
+        slot_planes = [keep.tile([P, S], U8, name=f"slot_planes{q}", align_bytes=64) for q in range(2)]
         shifted = keep.tile([P, S], U8, name="shifted", align_bytes=64)
         y = [keep.tile([P, S], F32, name=f"y{h}") for h in range(HALVES)]
+        ident = keep.tile([P, P], F32, name="ident")
         dummy = keep.tile([P, 1], F32, name="dummy")
 
         x_rows = xT.rearrange("(a p j) t -> a p j t", p=P, j=4)
@@ -69,16 +71,17 @@ def tile_moe_tk_lin_silu_kernel(tc, xT, w8_words, w8_scales, w4_words, w4_scales
 
         nc.vector.memset(dummy[:], 0.0)
         nc.scalar.activation(dummy[:], dummy[:], SILU)
+        nc.vector.memset(ws[:].rearrange("p e n -> p (e n)").bitcast(I32), 0)
         nc.vector.memset(planes[:].bitcast(I32), 0)
-        nc.vector.memset(words[:, PASSES * T :], 0)
-        nc.vector.memset(w8s[:].rearrange("p e n -> p (e n)").bitcast(I32), 0)
-        nc.vector.memset(w4s[:].rearrange("p e n -> p (e n)").bitcast(I32), 0)
+        nc.vector.memset(words[:, WORD_COLUMN[0] + T : WORD_COLUMN[4]], 0)
+        nc.vector.memset(words[:, WORD_COLUMN[4] + T :], 0)
         nc.vector.memset(shifted[:].bitcast(I32), 0)
 
         w8_rows = w8_words.rearrange("e a p n r -> p (e a) (n r)").bitcast(I32)
         w4_rows = w4_words.rearrange("e a p n -> p (e a) n").bitcast(I32)
         w8s_rows = w8_scales.rearrange("e a q n -> q (e a) n").bitcast(I32)
         w4s_rows = w4_scales.rearrange("e a q n -> q (e a) n").bitcast(I32)
+
         def load_w8(e0, e1):
             rows = slice(e0 * PASSES8, e1 * PASSES8)
             nc.sync.dma_start(out=w8[:, rows].bitcast(I32), in_=w8_rows[:, rows])
@@ -88,20 +91,20 @@ def tile_moe_tk_lin_silu_kernel(tc, xT, w8_words, w8_scales, w4_words, w4_scales
             nc.sync.dma_start(out=w4[:, rows].bitcast(I32), in_=w4_rows[:, rows])
 
         for r in range(4):
-            nc.gpsimd.dma_start(out=w8s[W8_ROW + r : P : 32].bitcast(I32), in_=w8s_rows[r:16:4])
+            nc.gpsimd.dma_start(out=ws[W8_ROW + r : P : 32, 0 : E * PASSES8].bitcast(I32), in_=w8s_rows[r:16:4])
         for r in range(4):
-            nc.gpsimd.dma_start(out=w4s[r:P:32].bitcast(I32), in_=w4s_rows[r:16:4])
+            nc.gpsimd.dma_start(out=ws[r:P:32].bitcast(I32), in_=w4s_rows[r:16:4])
+        make_identity(nc, ident[:])
         for a in range(1, PASSES):
             nc.sync.dma_start(out=raw[a][:], in_=x_rows[a])
-        load_w8(0, 4)
-        load_w4(0, 4)
-        nc.sync.dma_start(out=bias[:], in_=b.rearrange("(h p) e -> p h e", p=P))
-        load_w8(4, 8)
-        load_w4(4, 8)
-        for r, pos in enumerate((pos1, pos2, pos3, pos4)):
-            nc.sync.dma_start(pos_sb[r][:], pos)
-        load_w8(8, 12)
-        load_w4(8, 12)
+        for e0, e1 in BATCHES:
+            load_w8(e0, e1)
+            load_w4(e0, e1)
+            if e0 == 0:
+                nc.sync.dma_start(out=bias[:], in_=b.rearrange("(h p) e -> p h e", p=P))
+            if e0 == BATCHES[1][0]:
+                for r, pos in enumerate((pos1, pos2, pos3, pos4)):
+                    nc.sync.dma_start(pos_sb[r][:], pos)
         for r in range(TOP):
             nc.sync.dma_start(out=gates[:, r, :], in_=gate[r, 0:P, :])
 
@@ -111,61 +114,63 @@ def tile_moe_tk_lin_silu_kernel(tc, xT, w8_words, w8_scales, w4_words, w4_scales
         def interleave_vector(a, t0, t1):
             nc.vector.tensor_copy(out=grouped[a][:, t0:t1, :], in_=raw[a][:, :, t0:t1].rearrange("p j t -> p t j"))
 
-        def word_column(a):
-            return (PASSES - 1 - a) * T
-
-        def plane_column(q):
-            return (PACKS - 1 - q) * T
+        def plane_column(a):
+            return NARROW if a == PASSES - 1 else 0
 
         def quantise(a):
             for t0, t1 in ((0, 256), (256, T)):
-                w0, s0 = word_column(a), plane_column(PACK_OF[a])
+                w0, s0 = WORD_COLUMN[a], plane_column(a)
                 nc.vector.quantize_mx(
                     out=words[:, w0 + t0 : w0 + t1].bitcast(FP8X4),
                     scales=planes[PLANE_ROW[a] : P, s0 + t0 : s0 + t1],
                     in_=grouped[a][:, t0:t1, :].rearrange("p t j -> p (t j)"),
                 )
 
-        def gather_words(a, dst, j0, j1):
-            w0 = word_column(a)
+        def gather_words(a, j0, j1, last):
+            w0 = WORD_COLUMN[a]
+            w1 = WORD_COLUMNS if last else w0 + (NARROW if j1 - j0 <= 512 else WIDE)
+            w1 = min(w1, w0 + 8 * (j1 - j0))
             nc.vector.tensor_copy(
-                out=dst,
-                in_=words[:, w0 : w0 + WINDOW].bitcast(U32).indirect(offs_sb[:, j0 // 16 : j1 // 16]),
+                out=slot_words[a][:, j0:j1],
+                in_=words[:, w0:w1].bitcast(U32).indirect(offs_sb[:, j0 // 16 : j1 // 16]),
             )
 
         def gather_planes(q, j0, j1):
-            s0 = plane_column(q)
+            s0 = q * NARROW
             nc.vector.tensor_copy(
                 out=slot_planes[q][:, j0:j1],
-                in_=planes[:, s0 : s0 + (WINDOW if j1 - j0 <= 512 else PLANE_WINDOW)].indirect(offs_sb[:, j0 // 16 : j1 // 16]),
+                in_=planes[:, s0 : (s0 + NARROW if j1 - j0 <= 512 else PLANE_COLUMNS)].indirect(offs_sb[:, j0 // 16 : j1 // 16]),
             )
 
         def shift_planes(j0, j1):
             k = PLANE_ROW[SHIFTED]
             nc.gpsimd.dma_start(
-                out=shifted[0:100, j0:j1].bitcast(I32),
-                in_=slot_planes[PACK_OF[SHIFTED]][k : k + 100, j0:j1].bitcast(I32),
+                out=shifted[0:112, j0:j1].bitcast(I32),
+                in_=slot_planes[0][k : k + 112, j0:j1].bitcast(I32),
             )
 
-        def multiply(acc, a, e, h, moving):
+        def multiply(acc, a, e, h):
             cols = slice(e * C, (e + 1) * C)
             if a < PASSES8:
                 i = e * PASSES8 + a
                 lhsT = w8[:, i, 4 * P * h : 4 * P * (h + 1)].bitcast(FP8X4)
-                lhsT_scale = w8s[W8_ROW:P, i, P * h : P * (h + 1)]
+                lhsT_scale = ws[W8_ROW:P, i, P * h : P * (h + 1)]
             else:
                 i = e * PASSES4 + a - PASSES8
                 lhsT = w4[:, i, 2 * P * h : 2 * P * (h + 1)].bitcast(FP4X4)
-                lhsT_scale = w4s[:, i, P * h : P * (h + 1)]
+                lhsT_scale = ws[:, i, P * h : P * (h + 1)]
             nc.tensor.matmul_mx(
-                out=acc[:],
+                out=acc[:, 0:C],
                 lhsT=lhsT,
                 lhsT_scale=lhsT_scale,
-                rhs=moving.bitcast(FP8X4),
-                rhs_scale=shifted[:, cols] if a == SHIFTED else slot_planes[PACK_OF[a]][PLANE_ROW[a] : P, cols],
+                rhs=slot_words[a][:, cols].bitcast(FP8X4),
+                rhs_scale=shifted[:, cols] if a == SHIFTED else slot_planes[a // 4][PLANE_ROW[a] : P, cols],
                 start=(a == 0),
                 stop=(a == PASSES - 1),
             )
+
+        def activate(acc, e, h):
+            nc.scalar.activation(y[h][:, e * C : (e + 1) * C], acc[:, 0:C], SILU, bias=bias[:, h, e : e + 1])
 
         interleave_scalar(0, 0, 128)
         interleave_vector(0, 128, 256)
@@ -174,73 +179,70 @@ def tile_moe_tk_lin_silu_kernel(tc, xT, w8_words, w8_scales, w4_words, w4_scales
             interleave_scalar(a, 0, T)
         quantise(0)
         for a in range(EARLY):
-            for j in range(0, S, S // 2):
-                gather_words(a, early_words[a][:, j : j + S // 2], j, j + S // 2)
+            step = 512 if a == 0 else S // 2
+            for j in range(0, S, step):
+                gather_words(a, j, j + step, False)
             quantise(a + 1)
-        quantise(3)
 
+        late = []
         for e0, e1 in BATCHES:
             j0, j1 = e0 * C, e1 * C
-            if e0 == BATCHES[1][0]:
-                gather_planes(0, j0, S)
-                shift_planes(j0, S)
-            if e0 > 0:
-                gather_planes(1, j0, j1)
-            batch_words = {a: early_words[a][:, j0:j1] for a in range(EARLY)}
-            for a in range(EARLY, PASSES):
-                tile = keep.tile([P, j1 - j0], U32, name=f"batch_words{a}", align_bytes=64)
-                batch_words[a] = tile[:]
-            gather_words(2, batch_words[2], j0, j1)
             if e0 == 0:
+                gather_words(2, j0, j1, False)
+                quantise(3)
                 gather_planes(0, j0, j1)
                 shift_planes(j0, j1)
+                gather_words(3, j0, j1, False)
                 quantise(4)
-            gather_words(3, batch_words[3], j0, j1)
-            if e0 == 0:
                 gather_planes(1, j0, j1)
-            accs = {}
-            for e in range(e0, e1):
-                for h in range(HALVES):
-                    accs[e, h] = psum.tile([P, C], F32, name="acc")
-            for a in range(PASSES - 1):
-                for e in range(e0, e1):
-                    for h in range(HALVES):
-                        multiply(accs[e, h], a, e, h, batch_words[a][:, (e - e0) * C : (e - e0 + 1) * C])
-            for f0, f1 in ((e0, e1),) if e1 < E else ((e0, e0 + 2), (e0 + 2, e0 + 3), (e0 + 3, e1)):
-                gather_words(4, batch_words[4][:, (f0 - e0) * C : (f1 - e0) * C], f0 * C, f1 * C)
-                for e in range(f0, f1):
-                    for h in range(HALVES):
-                        multiply(accs[e, h], 4, e, h, batch_words[4][:, (e - e0) * C : (e - e0 + 1) * C])
-                        nc.scalar.activation(y[h][:, e * C : (e + 1) * C], accs[e, h][:], SILU, bias=bias[:, h, e : e + 1])
+            else:
+                if e0 == BATCHES[1][0]:
+                    gather_planes(0, j0, S)
+                    shift_planes(j0, S)
+                gather_words(2, j0, j1, True)
+                gather_words(3, j0, j1, True)
+                if e0 <= BATCHES[2][0]:
+                    gather_planes(1, j0, j0 + 512)
+            gather_words(4, j0, j1, True)
+            for h in range(HALVES):
+                accs = {e: psum.tile([P, T], F32, name="bank") for e in range(e0, e1)}
+                for a in range(PASSES):
+                    for e in range(e0, e1):
+                        multiply(accs[e], a, e, h)
+                        if a == PASSES - 1:
+                            activate(accs[e], e, h)
 
         part = [[keep.tile([P, T], F32, name=f"part{h}_{r}") for r in range(TOP)] for h in range(HALVES)]
-        low = [keep.tile([P, T], F32, name=f"low{h}") for h in range(HALVES)]
-        three = [keep.tile([P, T], F32, name=f"three{h}") for h in range(HALVES)]
+        turned = [keep.tile([P, T], F32, name=f"turned{h}") for h in range(HALVES)]
+        three = keep.tile([P, T], F32, name="three")
         total = [keep.tile([P, T], F32, name=f"total{h}") for h in range(HALVES)]
 
         def pick(h, r):
             nc.vector.tensor_tensor(part[h][r][:], y[h][:].indirect(pos_sb[r][:]), gates[:, r, :], MULT)
 
-        def add(dst, a, b, t0=0, t1=T):
-            nc.vector.tensor_tensor(dst[:, t0:t1], a[:, t0:t1], b[:, t0:t1], ADD)
+        def sum_on_tensor(h, count):
+            banks = [psum.tile([P, T], F32, name="bank") for c in range(CHUNKS)]
+            for r in range(count):
+                for c in range(CHUNKS):
+                    nc.tensor.matmul(banks[c][:, 0:P], part[h][r][:, c * P : (c + 1) * P], ident[:], start=(r == 0), stop=(r == count - 1), is_transpose=True)
+            back = psum.tile([P, T], F32, name="bank")
+            for c in range(CHUNKS):
+                nc.scalar.copy(turned[h][:, c * P : (c + 1) * P], banks[c][:, 0:P])
+                nc.tensor.transpose(back[:, c * P : (c + 1) * P], turned[h][:, c * P : (c + 1) * P], ident[:])
+            return back
 
-        def store(h, t0=0, t1=T):
+        def store(h, t0, t1):
             nc.sync.dma_start(out=out[h * P : (h + 1) * P, t0:t1], in_=total[h][:, t0:t1])
 
-        pick(0, 0)
-        pick(0, 1)
-        pick(0, 2)
-        add(low[0], part[0][0], part[0][1])
-        pick(0, 3)
-        add(three[0], low[0], part[0][2])
-        pick(1, 0)
-        add(total[0], three[0], part[0][3])
-        store(0)
-        pick(1, 1)
-        pick(1, 2)
-        add(low[1], part[1][0], part[1][1])
-        pick(1, 3)
-        add(three[1], low[1], part[1][2])
+        for h in range(HALVES):
+            for r in range(TOP):
+                pick(h, r)
+        back = sum_on_tensor(0, TOP)
+        nc.scalar.copy(total[0][:], back[:])
+        store(0, 0, T)
+        back = sum_on_tensor(1, 2)
         for t0 in (0, T // 2):
-            add(total[1], three[1], part[1][3], t0, t0 + T // 2)
+            nc.vector.tensor_tensor(three[:, t0 : t0 + T // 2], part[1][2][:, t0 : t0 + T // 2], back[:, t0 : t0 + T // 2], ADD)
+        for t0 in (0, T // 2):
+            nc.vector.tensor_tensor(total[1][:, t0 : t0 + T // 2], three[:, t0 : t0 + T // 2], part[1][3][:, t0 : t0 + T // 2], ADD)
             store(1, t0, t0 + T // 2)

@@ -90,13 +90,13 @@ def tile_moe_tk_lin_silu_kernel(tc, xT, w8_words, w8_scales, w4_words, w4_scales
             rows = slice(e0 * PASSES4, e1 * PASSES4)
             nc.sync.dma_start(out=w4[:, rows].bitcast(I32), in_=w4_rows[:, rows])
 
-        for r in range(4):
-            nc.gpsimd.dma_start(out=ws[W8_ROW + r : P : 32, 0 : E * PASSES8].bitcast(I32), in_=w8s_rows[r:16:4])
-        for r in range(4):
-            nc.gpsimd.dma_start(out=ws[r:P:32].bitcast(I32), in_=w4s_rows[r:16:4])
         make_identity(nc, ident[:])
         for a in range(1, PASSES):
             nc.sync.dma_start(out=raw[a][:], in_=x_rows[a])
+        for r in range(4):
+            nc.sync.dma_start(out=ws[W8_ROW + r : P : 32, 0 : E * PASSES8].bitcast(I32), in_=w8s_rows[r:16:4])
+        for r in range(4):
+            nc.sync.dma_start(out=ws[r:P:32].bitcast(I32), in_=w4s_rows[r:16:4])
         for e0, e1 in BATCHES:
             load_w8(e0, e1)
             load_w4(e0, e1)

@@ -32,9 +32,11 @@ EARLY = 2
 BATCHES = ((0, 4), (4, 8), (8, 10), (10, 12))
 NARROW = 704
 WIDE = 1024
-WORD_COLUMN = (3 * T, 2 * T, T, 0, 3 * T + NARROW)
+WORD_COLUMN = (3 * T, 2 * T, 0, T, 3 * T + NARROW)
 WORD_COLUMNS = WORD_COLUMN[4] + NARROW
 PLANE_COLUMNS = 2 * NARROW
+LATE = 7
+BANKS = 8
 CHUNKS = T // P
 
 
@@ -43,7 +45,7 @@ def tile_moe_tk_lin_silu_kernel(tc, xT, w8_words, w8_scales, w4_words, w4_scales
     with ExitStack() as ctx:
         lists = ctx.enter_context(tc.tile_pool(name="lists", bufs=1))
         keep = ctx.enter_context(tc.tile_pool(name="keep", bufs=1))
-        psum = ctx.enter_context(tc.psum_pool(name="psum", bufs=8))
+        psum = ctx.enter_context(tc.psum_pool(name="psum", bufs=1))
 
         offs_sb = lists.tile([P, S // 16], U16, name="offs_sb")
         pos_sb = [lists.tile([P, T // 16], U16, name=f"pos_sb{r}") for r in range(TOP)]
@@ -55,11 +57,10 @@ def tile_moe_tk_lin_silu_kernel(tc, xT, w8_words, w8_scales, w4_words, w4_scales
         ws = keep.tile([P, E * PASSES4, N], U8, name="ws", align_bytes=64)
         bias = keep.tile([P, HALVES, E], F32, name="bias")
         gates = keep.tile([P, TOP, T], F32, name="gates")
-        raw = [keep.tile([P, 4, T], F32, name=f"raw{a}") for a in range(PASSES)]
+        raw = [keep.tile([P, 4, T], F32, name=f"raw{a}", align_bytes=64) for a in range(PASSES)]
         grouped = [keep.tile([P, T, 4], BF16, name=f"grouped{a}", align_bytes=64) for a in range(PASSES)]
         slot_words = [keep.tile([P, S], U32, name=f"slot_words{a}", align_bytes=64) for a in range(PASSES)]
         slot_planes = [keep.tile([P, S], U8, name=f"slot_planes{q}", align_bytes=64) for q in range(2)]
-        shifted = keep.tile([P, S], U8, name="shifted", align_bytes=64)
         y = [keep.tile([P, S], F32, name=f"y{h}") for h in range(HALVES)]
         ident = keep.tile([P, P], F32, name="ident")
         dummy = keep.tile([P, 1], F32, name="dummy")
@@ -75,7 +76,6 @@ def tile_moe_tk_lin_silu_kernel(tc, xT, w8_words, w8_scales, w4_words, w4_scales
         nc.vector.memset(planes[:].bitcast(I32), 0)
         nc.vector.memset(words[:, WORD_COLUMN[0] + T : WORD_COLUMN[4]], 0)
         nc.vector.memset(words[:, WORD_COLUMN[4] + T :], 0)
-        nc.vector.memset(shifted[:].bitcast(I32), 0)
 
         w8_rows = w8_words.rearrange("e a p n r -> p (e a) (n r)").bitcast(I32)
         w4_rows = w4_words.rearrange("e a p n -> p (e a) n").bitcast(I32)
@@ -90,21 +90,36 @@ def tile_moe_tk_lin_silu_kernel(tc, xT, w8_words, w8_scales, w4_words, w4_scales
             rows = slice(e0 * PASSES4, e1 * PASSES4)
             nc.sync.dma_start(out=w4[:, rows].bitcast(I32), in_=w4_rows[:, rows])
 
-        make_identity(nc, ident[:])
-        for a in range(1, PASSES):
+        def load_x(a):
             nc.sync.dma_start(out=raw[a][:], in_=x_rows[a])
-        for r in range(4):
-            nc.sync.dma_start(out=ws[W8_ROW + r : P : 32, 0 : E * PASSES8].bitcast(I32), in_=w8s_rows[r:16:4])
-        for r in range(4):
-            nc.sync.dma_start(out=ws[r:P:32].bitcast(I32), in_=w4s_rows[r:16:4])
-        for e0, e1 in BATCHES:
+
+        def load_scales8(e0, e1):
+            for r in range(4):
+                nc.sync.dma_start(out=ws[W8_ROW + r : P : 32, e0 * PASSES4 : e0 * PASSES4 + (e1 - e0) * PASSES8].bitcast(I32), in_=w8s_rows[r:16:4, e0 * PASSES8 : e1 * PASSES8])
+
+        def load_scales4(e0, e1):
+            for r in range(4):
+                nc.sync.dma_start(out=ws[r:P:32, e0 * PASSES4 : e1 * PASSES4].bitcast(I32), in_=w4s_rows[r:16:4, e0 * PASSES4 : e1 * PASSES4])
+
+        make_identity(nc, ident[:])
+        first = BATCHES[0][1]
+        load_x(1)
+        load_scales8(0, first)
+        load_x(2)
+        load_x(3)
+        load_scales4(0, first)
+        load_w8(0, first)
+        load_x(4)
+        nc.sync.dma_start(out=bias[:], in_=b.rearrange("(h p) e -> p h e", p=P))
+        load_w4(0, first)
+        load_scales8(first, E)
+        for e0, e1 in BATCHES[1:]:
             load_w8(e0, e1)
+            if e0 == first:
+                load_scales4(first, E)
             load_w4(e0, e1)
-            if e0 == 0:
-                nc.sync.dma_start(out=bias[:], in_=b.rearrange("(h p) e -> p h e", p=P))
-            if e0 == BATCHES[1][0]:
-                for r, pos in enumerate((pos1, pos2, pos3, pos4)):
-                    nc.sync.dma_start(pos_sb[r][:], pos)
+        for r, pos in enumerate((pos1, pos2, pos3, pos4)):
+            nc.sync.dma_start(pos_sb[r][:], pos)
         for r in range(TOP):
             nc.sync.dma_start(out=gates[:, r, :], in_=gate[r, 0:P, :])
 
@@ -139,12 +154,12 @@ def tile_moe_tk_lin_silu_kernel(tc, xT, w8_words, w8_scales, w4_words, w4_scales
             s0 = q * NARROW
             nc.vector.tensor_copy(
                 out=slot_planes[q][:, j0:j1],
-                in_=planes[:, s0 : (s0 + NARROW if j1 - j0 <= 512 else PLANE_COLUMNS)].indirect(offs_sb[:, j0 // 16 : j1 // 16]),
+                in_=planes[:, s0 : s0 + NARROW].indirect(offs_sb[:, j0 // 16 : j1 // 16]),
             )
 
         def shift_planes(j0, j1):
             k = PLANE_ROW[SHIFTED]
-            nc.gpsimd.dma_start(
+            nc.scalar.dma_start(
                 out=shifted[0:112, j0:j1].bitcast(I32),
                 in_=slot_planes[0][k : k + 112, j0:j1].bitcast(I32),
             )
@@ -154,7 +169,7 @@ def tile_moe_tk_lin_silu_kernel(tc, xT, w8_words, w8_scales, w4_words, w4_scales
             if a < PASSES8:
                 i = e * PASSES8 + a
                 lhsT = w8[:, i, 4 * P * h : 4 * P * (h + 1)].bitcast(FP8X4)
-                lhsT_scale = ws[W8_ROW:P, i, P * h : P * (h + 1)]
+                lhsT_scale = ws[W8_ROW:P, i if e < BATCHES[1][0] else i + BATCHES[1][0], P * h : P * (h + 1)]
             else:
                 i = e * PASSES4 + a - PASSES8
                 lhsT = w4[:, i, 2 * P * h : 2 * P * (h + 1)].bitcast(FP4X4)
@@ -177,6 +192,7 @@ def tile_moe_tk_lin_silu_kernel(tc, xT, w8_words, w8_scales, w4_words, w4_scales
         interleave_vector(0, 256, T)
         for a in range(1, PASSES):
             interleave_scalar(a, 0, T)
+        shifted = keep.tile([P, S], U8, name="shifted", tag=f"raw{PASSES - 1}", align_bytes=64)
         quantise(0)
         for a in range(EARLY):
             step = 512 if a == 0 else S // 2
@@ -184,33 +200,41 @@ def tile_moe_tk_lin_silu_kernel(tc, xT, w8_words, w8_scales, w4_words, w4_scales
                 gather_words(a, j, j + step, False)
             quantise(a + 1)
 
-        late = []
+        def bank(i):
+            return psum.tile([P, T], F32, name=f"bank{i}")
+
+        turn = 0
         for e0, e1 in BATCHES:
             j0, j1 = e0 * C, e1 * C
             if e0 == 0:
-                gather_words(2, j0, j1, False)
                 quantise(3)
-                gather_planes(0, j0, j1)
-                shift_planes(j0, j1)
+                for j in range(0, S, 512):
+                    gather_planes(0, j, j + 512)
+                shift_planes(0, S)
+                gather_words(2, j0, j1, False)
                 gather_words(3, j0, j1, False)
                 quantise(4)
                 gather_planes(1, j0, j1)
             else:
-                if e0 == BATCHES[1][0]:
-                    gather_planes(0, j0, S)
-                    shift_planes(j0, S)
                 gather_words(2, j0, j1, True)
                 gather_words(3, j0, j1, True)
                 if e0 <= BATCHES[2][0]:
                     gather_planes(1, j0, j0 + 512)
             gather_words(4, j0, j1, True)
             for h in range(HALVES):
-                accs = {e: psum.tile([P, T], F32, name="bank") for e in range(e0, e1)}
+                experts = range(e0, e1 if h == 0 else min(e1, LATE))
+                accs = {e: bank((turn + e - e0) % BANKS) for e in experts}
+                turn += len(experts)
                 for a in range(PASSES):
-                    for e in range(e0, e1):
+                    for e in experts:
                         multiply(accs[e], a, e, h)
                         if a == PASSES - 1:
                             activate(accs[e], e, h)
+        for e in range(LATE, E):
+            acc = bank((turn - 3 + (e - LATE) % 3) % BANKS)
+            for a in range(PASSES):
+                multiply(acc, a, e, 1)
+            activate(acc, e, 1)
 
         part = [[keep.tile([P, T], F32, name=f"part{h}_{r}") for r in range(TOP)] for h in range(HALVES)]
         turned = [keep.tile([P, T], F32, name=f"turned{h}") for h in range(HALVES)]
@@ -221,11 +245,11 @@ def tile_moe_tk_lin_silu_kernel(tc, xT, w8_words, w8_scales, w4_words, w4_scales
             nc.vector.tensor_tensor(part[h][r][:], y[h][:].indirect(pos_sb[r][:]), gates[:, r, :], MULT)
 
         def sum_on_tensor(h, count):
-            banks = [psum.tile([P, T], F32, name="bank") for c in range(CHUNKS)]
+            banks = [bank((turn - 3 + 3 * h + c) % BANKS) for c in range(CHUNKS)]
             for r in range(count):
                 for c in range(CHUNKS):
                     nc.tensor.matmul(banks[c][:, 0:P], part[h][r][:, c * P : (c + 1) * P], ident[:], start=(r == 0), stop=(r == count - 1), is_transpose=True)
-            back = psum.tile([P, T], F32, name="bank")
+            back = bank((turn + 3 + h) % BANKS)
             for c in range(CHUNKS):
                 nc.scalar.copy(turned[h][:, c * P : (c + 1) * P], banks[c][:, 0:P])
                 nc.tensor.transpose(back[:, c * P : (c + 1) * P], turned[h][:, c * P : (c + 1) * P], ident[:])

@@ -26,16 +26,14 @@ MULT = mybir.AluOpType.mult
 ADD = mybir.AluOpType.add
 
 W8_ROW = 4
-PLANE_ROW = (4, 12, 0, 8, 0)
-SHIFTED = 3
-EARLY = 2
+PLANE_ROW = (4, 12, 0, 8, 16)
+ORDER = (4, 0, 1, 2, 3)
 BATCHES = ((0, 4), (4, 8), (8, 10), (10, 12))
 NARROW = 704
 WIDE = 1024
-WORD_COLUMN = (3 * T, 2 * T, 0, T, 3 * T + NARROW)
-WORD_COLUMNS = WORD_COLUMN[4] + NARROW
-PLANE_COLUMNS = 2 * NARROW
-LATE = 7
+WORD_COLUMN = (3 * T, 0, T, 2 * T, 4 * T)
+WORD_COLUMNS = 4 * T + NARROW
+LATE = 8
 BANKS = 8
 CHUNKS = T // P
 
@@ -51,7 +49,8 @@ def tile_moe_tk_lin_silu_kernel(tc, xT, w8_words, w8_scales, w4_words, w4_scales
         pos_sb = [lists.tile([P, T // 16], U16, name=f"pos_sb{r}") for r in range(TOP)]
 
         words = keep.tile([P, WORD_COLUMNS], I32, name="words", align_bytes=64)
-        planes = keep.tile([P, PLANE_COLUMNS], U8, name="planes", align_bytes=64)
+        planes = keep.tile([P, 2 * T], U8, name="planes", align_bytes=64)
+        packed = keep.tile([P, NARROW], U8, name="packed", align_bytes=64)
         w8 = keep.tile([P, E * PASSES8, 4 * N], U8, name="w8", align_bytes=64)
         w4 = keep.tile([P, E * PASSES4, 2 * N], U8, name="w4", align_bytes=64)
         ws = keep.tile([P, E * PASSES4, N], U8, name="ws", align_bytes=64)
@@ -60,35 +59,37 @@ def tile_moe_tk_lin_silu_kernel(tc, xT, w8_words, w8_scales, w4_words, w4_scales
         raw = [keep.tile([P, 4, T], F32, name=f"raw{a}", align_bytes=64) for a in range(PASSES)]
         grouped = [keep.tile([P, T, 4], BF16, name=f"grouped{a}", align_bytes=64) for a in range(PASSES)]
         slot_words = [keep.tile([P, S], U32, name=f"slot_words{a}", align_bytes=64) for a in range(PASSES)]
-        slot_planes = [keep.tile([P, S], U8, name=f"slot_planes{q}", align_bytes=64) for q in range(2)]
+        slot_planes = keep.tile([P, S], U8, name="slot_planes", align_bytes=64)
         y = [keep.tile([P, S], F32, name=f"y{h}") for h in range(HALVES)]
+        gate_rows = keep.tile([P, T], F32, name="gate_rows")
+        gate_cols = keep.tile([P, CHUNKS, TOP], F32, name="gate_cols")
         ident = keep.tile([P, P], F32, name="ident")
         dummy = keep.tile([P, 1], F32, name="dummy")
 
         x_rows = xT.rearrange("(a p j) t -> a p j t", p=P, j=4)
-        nc.sync.dma_start(out=raw[0][:, :, 0:256], in_=x_rows[0][:, :, 0:256])
-        nc.sync.dma_start(out=raw[0][:, :, 256:T], in_=x_rows[0][:, :, 256:T])
+        nc.sync.dma_start(out=raw[ORDER[0]][:], in_=x_rows[ORDER[0]])
         nc.sync.dma_start(offs_sb[:], offs)
 
         nc.vector.memset(dummy[:], 0.0)
         nc.scalar.activation(dummy[:], dummy[:], SILU)
         nc.vector.memset(ws[:].rearrange("p e n -> p (e n)").bitcast(I32), 0)
         nc.vector.memset(planes[:].bitcast(I32), 0)
-        nc.vector.memset(words[:, WORD_COLUMN[0] + T : WORD_COLUMN[4]], 0)
-        nc.vector.memset(words[:, WORD_COLUMN[4] + T :], 0)
+        nc.vector.memset(gate_rows[:], 0.0)
+        nc.vector.memset(packed[:].bitcast(I32), 0)
+        nc.vector.memset(words[:, PASSES * T :], 0)
 
         w8_rows = w8_words.rearrange("e a p n r -> p (e a) (n r)").bitcast(I32)
         w4_rows = w4_words.rearrange("e a p n -> p (e a) n").bitcast(I32)
         w8s_rows = w8_scales.rearrange("e a q n -> q (e a) n").bitcast(I32)
         w4s_rows = w4_scales.rearrange("e a q n -> q (e a) n").bitcast(I32)
 
-        def load_w8(e0, e1):
-            rows = slice(e0 * PASSES8, e1 * PASSES8)
-            nc.sync.dma_start(out=w8[:, rows].bitcast(I32), in_=w8_rows[:, rows])
+        def load_w8(e0, e1, h0=0, h1=HALVES):
+            rows, cols = slice(e0 * PASSES8, e1 * PASSES8), slice(h0 * P, h1 * P)
+            nc.sync.dma_start(out=w8[:].bitcast(I32)[:, rows, cols], in_=w8_rows[:, rows, cols])
 
-        def load_w4(e0, e1):
-            rows = slice(e0 * PASSES4, e1 * PASSES4)
-            nc.sync.dma_start(out=w4[:, rows].bitcast(I32), in_=w4_rows[:, rows])
+        def load_w4(e0, e1, h0=0, h1=HALVES):
+            rows, cols = slice(e0 * PASSES4, e1 * PASSES4), slice(h0 * P // 2, h1 * P // 2)
+            nc.sync.dma_start(out=w4[:].bitcast(I32)[:, rows, cols], in_=w4_rows[:, rows, cols])
 
         def load_x(a):
             nc.sync.dma_start(out=raw[a][:], in_=x_rows[a])
@@ -102,26 +103,29 @@ def tile_moe_tk_lin_silu_kernel(tc, xT, w8_words, w8_scales, w4_words, w4_scales
                 nc.sync.dma_start(out=ws[r:P:32, e0 * PASSES4 : e1 * PASSES4].bitcast(I32), in_=w4s_rows[r:16:4, e0 * PASSES4 : e1 * PASSES4])
 
         make_identity(nc, ident[:])
-        first = BATCHES[0][1]
-        load_x(1)
-        load_scales8(0, first)
-        load_x(2)
-        load_x(3)
-        load_scales4(0, first)
-        load_w8(0, first)
-        load_x(4)
-        nc.sync.dma_start(out=bias[:], in_=b.rearrange("(h p) e -> p h e", p=P))
-        load_w4(0, first)
-        load_scales8(first, E)
-        for e0, e1 in BATCHES[1:]:
-            load_w8(e0, e1)
-            if e0 == first:
-                load_scales4(first, E)
-            load_w4(e0, e1)
-        for r, pos in enumerate((pos1, pos2, pos3, pos4)):
-            nc.sync.dma_start(pos_sb[r][:], pos)
-        for r in range(TOP):
-            nc.sync.dma_start(out=gates[:, r, :], in_=gate[r, 0:P, :])
+        for a in ORDER[1:-1]:
+            load_x(a)
+        nc.sync.dma_start(out=gate_rows[0:TOP, :], in_=gate[:, 0, :])
+        load_x(ORDER[-1])
+        load_scales8(0, E)
+        load_scales4(0, E)
+        for e0 in (0, 2):
+            load_w8(e0, e0 + 2)
+        for e0 in (0, 2):
+            load_w4(e0, e0 + 2)
+        for e0 in range(BATCHES[1][0], LATE):
+            load_w8(e0, e0 + 1)
+            load_w4(e0, e0 + 1)
+            if e0 == BATCHES[1][0]:
+                nc.sync.dma_start(out=bias[:], in_=b.rearrange("(h p) e -> p h e", p=P))
+                for r, pos in enumerate((pos1, pos2, pos3, pos4)):
+                    nc.sync.dma_start(pos_sb[r][:], pos)
+        for e0, e1 in BATCHES[2:]:
+            load_w8(e0, e1, 0, 1)
+            load_w4(e0, e1, 0, 1)
+        for e0, e1 in BATCHES[2:]:
+            load_w8(e0, e1, 1, 2)
+            load_w4(e0, e1, 1, 2)
 
         def interleave_scalar(a, t0, t1):
             nc.scalar.activation(grouped[a][:, t0:t1, :], raw[a][:, :, t0:t1].rearrange("p j t -> p t j"), COPY)
@@ -129,47 +133,34 @@ def tile_moe_tk_lin_silu_kernel(tc, xT, w8_words, w8_scales, w4_words, w4_scales
         def interleave_vector(a, t0, t1):
             nc.vector.tensor_copy(out=grouped[a][:, t0:t1, :], in_=raw[a][:, :, t0:t1].rearrange("p j t -> p t j"))
 
-        def plane_column(a):
-            return NARROW if a == PASSES - 1 else 0
-
         def quantise(a):
             for t0, t1 in ((0, 256), (256, T)):
-                w0, s0 = WORD_COLUMN[a], plane_column(a)
+                w0, s0, k = WORD_COLUMN[a], T if a == ORDER[0] else 0, 0 if a == ORDER[0] else PLANE_ROW[a]
                 nc.vector.quantize_mx(
                     out=words[:, w0 + t0 : w0 + t1].bitcast(FP8X4),
-                    scales=planes[PLANE_ROW[a] : P, s0 + t0 : s0 + t1],
+                    scales=planes[k:P, s0 + t0 : s0 + t1],
                     in_=grouped[a][:, t0:t1, :].rearrange("p t j -> p (t j)"),
                 )
 
-        def gather_words(a, j0, j1, last):
-            w0 = WORD_COLUMN[a]
-            w1 = WORD_COLUMNS if last else w0 + (NARROW if j1 - j0 <= 512 else WIDE)
-            w1 = min(w1, w0 + 8 * (j1 - j0))
+        def gather_words(a, j0, j1, w1):
             nc.vector.tensor_copy(
                 out=slot_words[a][:, j0:j1],
-                in_=words[:, w0:w1].bitcast(U32).indirect(offs_sb[:, j0 // 16 : j1 // 16]),
+                in_=words[:, WORD_COLUMN[a] : w1].bitcast(U32).indirect(offs_sb[:, j0 // 16 : j1 // 16]),
             )
 
-        def gather_planes(q, j0, j1):
-            s0 = q * NARROW
-            nc.vector.tensor_copy(
-                out=slot_planes[q][:, j0:j1],
-                in_=planes[:, s0 : s0 + NARROW].indirect(offs_sb[:, j0 // 16 : j1 // 16]),
-            )
+        def gather_planes(j0, j1):
+            nc.vector.tensor_copy(out=slot_planes[:, j0:j1], in_=packed[:].indirect(offs_sb[:, j0 // 16 : j1 // 16]))
 
-        def shift_planes(j0, j1):
-            k = PLANE_ROW[SHIFTED]
-            nc.scalar.dma_start(
-                out=shifted[0:112, j0:j1].bitcast(I32),
-                in_=slot_planes[0][k : k + 112, j0:j1].bitcast(I32),
-            )
+        def shift_plane(a):
+            k = PLANE_ROW[a]
+            nc.gpsimd.dma_start(out=shifted[a][0:112, :].bitcast(I32), in_=slot_planes[k : k + 112, :].bitcast(I32))
 
         def multiply(acc, a, e, h):
             cols = slice(e * C, (e + 1) * C)
             if a < PASSES8:
                 i = e * PASSES8 + a
                 lhsT = w8[:, i, 4 * P * h : 4 * P * (h + 1)].bitcast(FP8X4)
-                lhsT_scale = ws[W8_ROW:P, i if e < BATCHES[1][0] else i + BATCHES[1][0], P * h : P * (h + 1)]
+                lhsT_scale = ws[W8_ROW:P, i, P * h : P * (h + 1)]
             else:
                 i = e * PASSES4 + a - PASSES8
                 lhsT = w4[:, i, 2 * P * h : 2 * P * (h + 1)].bitcast(FP4X4)
@@ -179,48 +170,55 @@ def tile_moe_tk_lin_silu_kernel(tc, xT, w8_words, w8_scales, w4_words, w4_scales
                 lhsT=lhsT,
                 lhsT_scale=lhsT_scale,
                 rhs=slot_words[a][:, cols].bitcast(FP8X4),
-                rhs_scale=shifted[:, cols] if a == SHIFTED else slot_planes[a // 4][PLANE_ROW[a] : P, cols],
+                rhs_scale=shifted[a][:, cols] if a in shifted else slot_planes[PLANE_ROW[a] : P, cols],
                 start=(a == 0),
                 stop=(a == PASSES - 1),
             )
 
-        def activate(acc, e, h):
-            nc.scalar.activation(y[h][:, e * C : (e + 1) * C], acc[:, 0:C], SILU, bias=bias[:, h, e : e + 1])
-
-        interleave_scalar(0, 0, 128)
-        interleave_vector(0, 128, 256)
-        interleave_vector(0, 256, T)
-        for a in range(1, PASSES):
-            interleave_scalar(a, 0, T)
-        shifted = keep.tile([P, S], U8, name="shifted", tag=f"raw{PASSES - 1}", align_bytes=64)
-        quantise(0)
-        for a in range(EARLY):
-            step = 512 if a == 0 else S // 2
-            for j in range(0, S, step):
-                gather_words(a, j, j + step, False)
-            quantise(a + 1)
-
         def bank(i):
             return psum.tile([P, T], F32, name=f"bank{i}")
 
+        def activate(acc, e, h):
+            nc.scalar.activation(y[h][:, e * C : (e + 1) * C], acc[:, 0:C], SILU, bias=bias[:, h, e : e + 1])
+
+        interleave_vector(ORDER[0], 0, 256)
+        interleave_scalar(ORDER[0], 256, T)
+        for a in ORDER[1:]:
+            interleave_scalar(a, 0, T)
+        turned_gate = bank(0)
+        for c in range(CHUNKS):
+            nc.tensor.transpose(turned_gate[:, c * P : (c + 1) * P], gate_rows[:, c * P : (c + 1) * P], ident[:])
+        nc.scalar.copy(gate_cols[:], turned_gate[:].rearrange("p (c r) -> p c r", c=CHUNKS)[:, :, 0:TOP])
+        for r in range(TOP):
+            spread = bank(1 + r)
+            for c in range(CHUNKS):
+                nc.tensor.transpose(spread[:, c * P : (c + 1) * P], gate_cols[:, c, r : r + 1].to_broadcast([P, P]), ident[:])
+            nc.scalar.copy(gates[:, r, :], spread[:])
+        shifted = {a: keep.tile([P, S], U8, name=f"shifted{a}", tag=f"raw{a}", align_bytes=64) for a in (3, 4)}
+        first, second = ORDER[:2]
+        quantise(first)
+        nc.gpsimd.dma_start(out=packed[16:P, 0:T].bitcast(I32), in_=planes[0:112, T : 2 * T].bitcast(I32))
+        for j in range(0, S, 512):
+            gather_words(first, j, j + 512, WORD_COLUMNS)
+        quantise(second)
+        for j in range(0, S, S // 2):
+            gather_words(second, j, j + S // 2, WORD_COLUMN[second] + WIDE)
+        quantise(1)
+        quantise(2)
+        gather_words(1, 0, 512, NARROW)
+        quantise(3)
+        for q in range(0, P, 32):
+            nc.vector.tensor_copy(out=packed[q : q + 16, 0:T].bitcast(I32), in_=planes[q : q + 16, 0:T].bitcast(I32))
+        for j in range(0, S, 512):
+            gather_planes(j, j + 512)
+        shift_plane(3)
+        shift_plane(4)
+
         turn = 0
         for e0, e1 in BATCHES:
-            j0, j1 = e0 * C, e1 * C
-            if e0 == 0:
-                quantise(3)
-                for j in range(0, S, 512):
-                    gather_planes(0, j, j + 512)
-                shift_planes(0, S)
-                gather_words(2, j0, j1, False)
-                gather_words(3, j0, j1, False)
-                quantise(4)
-                gather_planes(1, j0, j1)
-            else:
-                gather_words(2, j0, j1, True)
-                gather_words(3, j0, j1, True)
-                if e0 <= BATCHES[2][0]:
-                    gather_planes(1, j0, j0 + 512)
-            gather_words(4, j0, j1, True)
+            for a in (1, 2, 3):
+                if (a, e0) != (1, 0):
+                    gather_words(a, e0 * C, e1 * C, 4 * T)
             for h in range(HALVES):
                 experts = range(e0, e1 if h == 0 else min(e1, LATE))
                 accs = {e: bank((turn + e - e0) % BANKS) for e in experts}

@@ -28,11 +28,12 @@ ADD = mybir.AluOpType.add
 W8_ROW = 4
 PLANE_ROW = (4, 12, 0, 8, 16)
 ORDER = (4, 0, 1, 2, 3)
-BATCHES = ((0, 4), (4, 8), (8, 10), (10, 12))
+BATCHES = ((0, 4), (4, 6), (6, 8), (8, 10), (10, 12))
 NARROW = 704
 WIDE = 1024
 WORD_COLUMN = (3 * T, 0, T, 2 * T, 4 * T)
 WORD_COLUMNS = 4 * T + NARROW
+FIRST = 4
 LATE = 8
 BANKS = 8
 CHUNKS = T // P
@@ -51,8 +52,10 @@ def tile_moe_tk_lin_silu_kernel(tc, xT, w8_words, w8_scales, w4_words, w4_scales
         words = keep.tile([P, WORD_COLUMNS], I32, name="words", align_bytes=64)
         planes = keep.tile([P, 2 * T], U8, name="planes", align_bytes=64)
         packed = keep.tile([P, NARROW], U8, name="packed", align_bytes=64)
-        w8 = keep.tile([P, E * PASSES8, 4 * N], U8, name="w8", align_bytes=64)
-        w4 = keep.tile([P, E * PASSES4, 2 * N], U8, name="w4", align_bytes=64)
+        w8 = keep.tile([P, LATE * PASSES8, 4 * N], U8, name="w8", align_bytes=64)
+        w4 = keep.tile([P, LATE * PASSES4, 2 * N], U8, name="w4", align_bytes=64)
+        w8_late = [keep.tile([P, (E - LATE) * PASSES8, 4 * P], U8, name=f"w8_late{h}", align_bytes=64) for h in range(HALVES)]
+        w4_late = [keep.tile([P, (E - LATE) * PASSES4, 2 * P], U8, name=f"w4_late{h}", align_bytes=64) for h in range(HALVES)]
         ws = keep.tile([P, E * PASSES4, N], U8, name="ws", align_bytes=64)
         bias = keep.tile([P, HALVES, E], F32, name="bias")
         gates = keep.tile([P, TOP, T], F32, name="gates")
@@ -64,17 +67,16 @@ def tile_moe_tk_lin_silu_kernel(tc, xT, w8_words, w8_scales, w4_words, w4_scales
         gate_rows = keep.tile([P, T], F32, name="gate_rows")
         gate_cols = keep.tile([P, CHUNKS, TOP], F32, name="gate_cols")
         ident = keep.tile([P, P], F32, name="ident")
-        dummy = keep.tile([P, 1], F32, name="dummy")
+        zero = keep.tile([P, 1], F32, name="zero")
 
         x_rows = xT.rearrange("(a p j) t -> a p j t", p=P, j=4)
         nc.sync.dma_start(out=raw[ORDER[0]][:], in_=x_rows[ORDER[0]])
         nc.sync.dma_start(offs_sb[:], offs)
 
-        nc.vector.memset(dummy[:], 0.0)
-        nc.scalar.activation(dummy[:], dummy[:], SILU)
+        nc.vector.memset(zero[:], 0.0)
+        nc.scalar.activation(gate_rows[:], zero[:].to_broadcast([P, T]), SILU)
         nc.vector.memset(ws[:].rearrange("p e n -> p (e n)").bitcast(I32), 0)
         nc.vector.memset(planes[:].bitcast(I32), 0)
-        nc.vector.memset(gate_rows[:], 0.0)
         nc.vector.memset(packed[:].bitcast(I32), 0)
         nc.vector.memset(words[:, PASSES * T :], 0)
 
@@ -83,49 +85,39 @@ def tile_moe_tk_lin_silu_kernel(tc, xT, w8_words, w8_scales, w4_words, w4_scales
         w8s_rows = w8_scales.rearrange("e a q n -> q (e a) n").bitcast(I32)
         w4s_rows = w4_scales.rearrange("e a q n -> q (e a) n").bitcast(I32)
 
-        def load_w8(e0, e1, h0=0, h1=HALVES):
-            rows, cols = slice(e0 * PASSES8, e1 * PASSES8), slice(h0 * P, h1 * P)
-            nc.sync.dma_start(out=w8[:].bitcast(I32)[:, rows, cols], in_=w8_rows[:, rows, cols])
+        def load_w8(e0, e1):
+            rows = slice(e0 * PASSES8, e1 * PASSES8)
+            nc.sync.dma_start(out=w8[:, rows].bitcast(I32), in_=w8_rows[:, rows])
 
-        def load_w4(e0, e1, h0=0, h1=HALVES):
-            rows, cols = slice(e0 * PASSES4, e1 * PASSES4), slice(h0 * P // 2, h1 * P // 2)
-            nc.sync.dma_start(out=w4[:].bitcast(I32)[:, rows, cols], in_=w4_rows[:, rows, cols])
+        def load_w4(e0, e1):
+            rows = slice(e0 * PASSES4, e1 * PASSES4)
+            nc.sync.dma_start(out=w4[:, rows].bitcast(I32), in_=w4_rows[:, rows])
+
+        def load_w8_half(h):
+            nc.sync.dma_start(out=w8_late[h][:].bitcast(I32), in_=w8_rows[:, LATE * PASSES8 :, h * P : (h + 1) * P])
+
+        def load_w4_half(e0, e1, h):
+            nc.sync.dma_start(
+                out=w4_late[h][:, (e0 - LATE) * PASSES4 : (e1 - LATE) * PASSES4].bitcast(I32),
+                in_=w4_rows[:, e0 * PASSES4 : e1 * PASSES4, h * P // 2 : (h + 1) * P // 2],
+            )
 
         def load_x(a):
             nc.sync.dma_start(out=raw[a][:], in_=x_rows[a])
 
-        def load_scales8(e0, e1):
+        def load_scales8(queue, e0, e1):
             for r in range(4):
-                nc.sync.dma_start(out=ws[W8_ROW + r : P : 32, e0 * PASSES4 : e0 * PASSES4 + (e1 - e0) * PASSES8].bitcast(I32), in_=w8s_rows[r:16:4, e0 * PASSES8 : e1 * PASSES8])
+                queue.dma_start(out=ws[W8_ROW + r : P : 32, e0 * PASSES4 : e0 * PASSES4 + (e1 - e0) * PASSES8].bitcast(I32), in_=w8s_rows[r:16:4, e0 * PASSES8 : e1 * PASSES8])
 
-        def load_scales4(e0, e1):
+        def load_scales4(queue, e0, e1):
             for r in range(4):
-                nc.sync.dma_start(out=ws[r:P:32, e0 * PASSES4 : e1 * PASSES4].bitcast(I32), in_=w4s_rows[r:16:4, e0 * PASSES4 : e1 * PASSES4])
+                queue.dma_start(out=ws[r:P:32, e0 * PASSES4 : e1 * PASSES4].bitcast(I32), in_=w4s_rows[r:16:4, e0 * PASSES4 : e1 * PASSES4])
 
         make_identity(nc, ident[:])
-        for a in ORDER[1:-1]:
-            load_x(a)
-        nc.sync.dma_start(out=gate_rows[0:TOP, :], in_=gate[:, 0, :])
-        load_x(ORDER[-1])
-        load_scales8(0, E)
-        load_scales4(0, E)
-        for e0 in (0, 2):
-            load_w8(e0, e0 + 2)
-        for e0 in (0, 2):
-            load_w4(e0, e0 + 2)
-        for e0 in range(BATCHES[1][0], LATE):
-            load_w8(e0, e0 + 1)
-            load_w4(e0, e0 + 1)
-            if e0 == BATCHES[1][0]:
-                nc.sync.dma_start(out=bias[:], in_=b.rearrange("(h p) e -> p h e", p=P))
-                for r, pos in enumerate((pos1, pos2, pos3, pos4)):
-                    nc.sync.dma_start(pos_sb[r][:], pos)
-        for e0, e1 in BATCHES[2:]:
-            load_w8(e0, e1, 0, 1)
-            load_w4(e0, e1, 0, 1)
-        for e0, e1 in BATCHES[2:]:
-            load_w8(e0, e1, 1, 2)
-            load_w4(e0, e1, 1, 2)
+        load_scales8(nc.gpsimd, FIRST, E)
+        load_scales4(nc.gpsimd, FIRST, E)
+        load_x(ORDER[1])
+        load_x(ORDER[2])
 
         def interleave_scalar(a, t0, t1):
             nc.scalar.activation(grouped[a][:, t0:t1, :], raw[a][:, :, t0:t1].rearrange("p j t -> p t j"), COPY)
@@ -151,19 +143,20 @@ def tile_moe_tk_lin_silu_kernel(tc, xT, w8_words, w8_scales, w4_words, w4_scales
         def gather_planes(j0, j1):
             nc.vector.tensor_copy(out=slot_planes[:, j0:j1], in_=packed[:].indirect(offs_sb[:, j0 // 16 : j1 // 16]))
 
-        def shift_plane(a):
-            k = PLANE_ROW[a]
-            nc.gpsimd.dma_start(out=shifted[a][0:112, :].bitcast(I32), in_=slot_planes[k : k + 112, :].bitcast(I32))
+        def shift_planes(j0, j1):
+            for a in shifted:
+                k = PLANE_ROW[a]
+                nc.sync.dma_start(out=shifted[a][0:112, j0:j1].bitcast(I32), in_=slot_planes[k : k + 112, j0:j1].bitcast(I32))
 
-        def multiply(acc, a, e, h):
+        def multiply(acc, a, e, h, order):
             cols = slice(e * C, (e + 1) * C)
             if a < PASSES8:
                 i = e * PASSES8 + a
-                lhsT = w8[:, i, 4 * P * h : 4 * P * (h + 1)].bitcast(FP8X4)
-                lhsT_scale = ws[W8_ROW:P, i, P * h : P * (h + 1)]
+                lhsT = (w8[:, i, 4 * P * h : 4 * P * (h + 1)] if e < LATE else w8_late[h][:, i - LATE * PASSES8]).bitcast(FP8X4)
+                lhsT_scale = ws[W8_ROW:P, i if e < FIRST else i + FIRST, P * h : P * (h + 1)]
             else:
                 i = e * PASSES4 + a - PASSES8
-                lhsT = w4[:, i, 2 * P * h : 2 * P * (h + 1)].bitcast(FP4X4)
+                lhsT = (w4[:, i, 2 * P * h : 2 * P * (h + 1)] if e < LATE else w4_late[h][:, i - LATE * PASSES4]).bitcast(FP4X4)
                 lhsT_scale = ws[:, i, P * h : P * (h + 1)]
             nc.tensor.matmul_mx(
                 out=acc[:, 0:C],
@@ -171,8 +164,8 @@ def tile_moe_tk_lin_silu_kernel(tc, xT, w8_words, w8_scales, w4_words, w4_scales
                 lhsT_scale=lhsT_scale,
                 rhs=slot_words[a][:, cols].bitcast(FP8X4),
                 rhs_scale=shifted[a][:, cols] if a in shifted else slot_planes[PLANE_ROW[a] : P, cols],
-                start=(a == 0),
-                stop=(a == PASSES - 1),
+                start=(a == order[0]),
+                stop=(a == order[-1]),
             )
 
         def bank(i):
@@ -183,6 +176,17 @@ def tile_moe_tk_lin_silu_kernel(tc, xT, w8_words, w8_scales, w4_words, w4_scales
 
         interleave_vector(ORDER[0], 0, 256)
         interleave_scalar(ORDER[0], 256, T)
+        quantise(ORDER[0])
+        nc.sync.dma_start(out=packed[16:P, 0:T].bitcast(I32), in_=planes[0:112, T : 2 * T].bitcast(I32))
+        load_x(ORDER[3])
+        nc.sync.dma_start(out=gate_rows[0:TOP, :], in_=gate[:, 0, :])
+        load_x(ORDER[4])
+        load_scales8(nc.sync, 0, FIRST)
+        load_w8(0, 2)
+        load_scales4(nc.sync, 0, FIRST)
+        load_w8(2, FIRST)
+        for e in (0, 2):
+            load_w4(e, e + 2)
         for a in ORDER[1:]:
             interleave_scalar(a, 0, T)
         turned_gate = bank(0)
@@ -196,8 +200,6 @@ def tile_moe_tk_lin_silu_kernel(tc, xT, w8_words, w8_scales, w4_words, w4_scales
             nc.scalar.copy(gates[:, r, :], spread[:])
         shifted = {a: keep.tile([P, S], U8, name=f"shifted{a}", tag=f"raw{a}", align_bytes=64) for a in (3, 4)}
         first, second = ORDER[:2]
-        quantise(first)
-        nc.gpsimd.dma_start(out=packed[16:P, 0:T].bitcast(I32), in_=planes[0:112, T : 2 * T].bitcast(I32))
         for j in range(0, S, 512):
             gather_words(first, j, j + 512, WORD_COLUMNS)
         quantise(second)
@@ -205,33 +207,54 @@ def tile_moe_tk_lin_silu_kernel(tc, xT, w8_words, w8_scales, w4_words, w4_scales
             gather_words(second, j, j + S // 2, WORD_COLUMN[second] + WIDE)
         quantise(1)
         quantise(2)
-        gather_words(1, 0, 512, NARROW)
         quantise(3)
         for q in range(0, P, 32):
             nc.vector.tensor_copy(out=packed[q : q + 16, 0:T].bitcast(I32), in_=planes[q : q + 16, 0:T].bitcast(I32))
-        for j in range(0, S, 512):
-            gather_planes(j, j + 512)
-        shift_plane(3)
-        shift_plane(4)
+        gather_planes(0, 512)
+        gather_planes(512, 1024)
+        shift_planes(0, 1024)
+        nc.sync.dma_start(out=bias[:], in_=b.rearrange("(h p) e -> p h e", p=P))
+        load_w8(4, 6)
+        load_w4(4, 6)
+        load_w8(6, 8)
+        load_w4(6, 8)
 
         turn = 0
         for e0, e1 in BATCHES:
             for a in (1, 2, 3):
-                if (a, e0) != (1, 0):
+                if (a, e1) == (3, E):
+                    for e in range(e0, e1):
+                        gather_words(a, e * C, (e + 1) * C, 4 * T)
+                else:
                     gather_words(a, e0 * C, e1 * C, 4 * T)
-            for h in range(HALVES):
-                experts = range(e0, e1 if h == 0 else min(e1, LATE))
-                accs = {e: bank((turn + e - e0) % BANKS) for e in experts}
-                turn += len(experts)
-                for a in range(PASSES):
-                    for e in experts:
-                        multiply(accs[e], a, e, h)
-                        if a == PASSES - 1:
-                            activate(accs[e], e, h)
+            if e0 == 0:
+                gather_planes(1024, S)
+                shift_planes(1024, S)
+                for h in range(HALVES):
+                    load_w8_half(h)
+                    for f0, f1 in ((LATE, E - 2), (E - 2, E - 1), (E - 1, E)):
+                        load_w4_half(f0, f1, h)
+                    if h == 0:
+                        for r, pos in enumerate((pos1, pos2, pos3, pos4)):
+                            nc.sync.dma_start(pos_sb[r][:], pos)
+            groups = [(e, h) for h in range(HALVES) for e in range(e0, e1) if h == 0 or e < LATE]
+            accs = {g: bank((turn + i) % BANKS) for i, g in enumerate(groups)}
+            turn += len(groups)
+            order = (0, 4, 1, 2, 3) if e1 == E else (0, 1, 2, 3, 4)
+            if e1 == E:
+                steps = [(a, e, h) for a in order for e, h in groups]
+            elif e0 == 0:
+                steps = [(a, e, h) for a in range(3) for e, h in groups] + [(a, e, h) for e, h in groups for a in (3, 4)]
+            else:
+                steps = [(a, e, h) for e, h in groups for a in range(PASSES)]
+            for a, e, h in steps:
+                multiply(accs[e, h], a, e, h, order)
+                if a == order[-1]:
+                    activate(accs[e, h], e, h)
         for e in range(LATE, E):
             acc = bank((turn - 3 + (e - LATE) % 3) % BANKS)
             for a in range(PASSES):
-                multiply(acc, a, e, 1)
+                multiply(acc, a, e, 1, range(PASSES))
             activate(acc, e, 1)
 
         part = [[keep.tile([P, T], F32, name=f"part{h}_{r}") for r in range(TOP)] for h in range(HALVES)]

@@ -9,6 +9,8 @@ P = 128
 PASSES, PASSES8 = 5, 2
 PASSES4 = PASSES - PASSES8
 HALVES = N // P
+CHUNKS = T // P
+BANKS = 8
 FLOPS = 2 * S * K * N
 BYTES = 4 * K * T + E * N * (PASSES8 * (512 + 16) + PASSES4 * (256 + 16)) + 4 * N * E + 4 * TOP * T + 2 * P * (S + TOP * T) // 16 + 4 * N * T
 
@@ -25,18 +27,23 @@ SILU = mybir.ActivationFunctionType.Silu
 MULT = mybir.AluOpType.mult
 ADD = mybir.AluOpType.add
 
+ALIGN = 256
+QUADRANT = 32
 W8_ROW = 4
 PLANE_ROW = (4, 12, 0, 8, 16)
+SHIFTED = (3, 4)
+QUANTISED_ROWS = 16
+MOVED = P - QUANTISED_ROWS
 ORDER = (4, 0, 1, 2, 3)
-BATCHES = ((0, 4), (4, 6), (6, 8), (8, 10), (10, 12))
-NARROW = 704
-WIDE = 1024
+SPLIT = 256
+FEW, NARROW = 512, 704
+MANY, WIDE = 768, 1024
 WORD_COLUMN = (3 * T, 0, T, 2 * T, 4 * T)
 WORD_COLUMNS = 4 * T + NARROW
-FIRST = 4
+LATE_END = 4 * T
+BATCHES = ((0, 4), (4, 6), (6, 8), (8, 10), (10, 12))
 LATE = 8
-BANKS = 8
-CHUNKS = T // P
+LATE_BANKS = 3
 
 
 def tile_moe_tk_lin_silu_kernel(tc, xT, w8_words, w8_scales, w4_words, w4_scales, b, gate, offs, pos1, pos2, pos3, pos4, out):
@@ -49,20 +56,20 @@ def tile_moe_tk_lin_silu_kernel(tc, xT, w8_words, w8_scales, w4_words, w4_scales
         offs_sb = lists.tile([P, S // 16], U16, name="offs_sb")
         pos_sb = [lists.tile([P, T // 16], U16, name=f"pos_sb{r}") for r in range(TOP)]
 
-        words = keep.tile([P, WORD_COLUMNS], I32, name="words", align_bytes=64)
-        planes = keep.tile([P, 2 * T], U8, name="planes", align_bytes=64)
-        packed = keep.tile([P, NARROW], U8, name="packed", align_bytes=64)
-        w8 = keep.tile([P, LATE * PASSES8, 4 * N], U8, name="w8", align_bytes=64)
-        w4 = keep.tile([P, LATE * PASSES4, 2 * N], U8, name="w4", align_bytes=64)
-        w8_late = [keep.tile([P, (E - LATE) * PASSES8, 4 * P], U8, name=f"w8_late{h}", align_bytes=64) for h in range(HALVES)]
-        w4_late = [keep.tile([P, (E - LATE) * PASSES4, 2 * P], U8, name=f"w4_late{h}", align_bytes=64) for h in range(HALVES)]
-        ws = keep.tile([P, E * PASSES4, N], U8, name="ws", align_bytes=64)
+        words = keep.tile([P, WORD_COLUMNS], I32, name="words", align_bytes=ALIGN)
+        planes = keep.tile([P, 2 * T], U8, name="planes", align_bytes=ALIGN)
+        packed = keep.tile([P, NARROW], U8, name="packed", align_bytes=ALIGN)
+        w8 = keep.tile([P, LATE * PASSES8, 4 * N], U8, name="w8", align_bytes=ALIGN)
+        w4 = keep.tile([P, LATE * PASSES4, 2 * N], U8, name="w4", align_bytes=ALIGN)
+        w8_late = [keep.tile([P, (E - LATE) * PASSES8, 4 * P], U8, name=f"w8_late{h}", align_bytes=ALIGN) for h in range(HALVES)]
+        w4_late = [keep.tile([P, (E - LATE) * PASSES4, 2 * P], U8, name=f"w4_late{h}", align_bytes=ALIGN) for h in range(HALVES)]
+        w_planes = keep.tile([P, E * PASSES4, N], U8, name="w_planes", align_bytes=ALIGN)
         bias = keep.tile([P, HALVES, E], F32, name="bias")
         gates = keep.tile([P, TOP, T], F32, name="gates")
-        raw = [keep.tile([P, 4, T], F32, name=f"raw{a}", align_bytes=64) for a in range(PASSES)]
-        grouped = [keep.tile([P, T, 4], BF16, name=f"grouped{a}", align_bytes=64) for a in range(PASSES)]
-        slot_words = [keep.tile([P, S], U32, name=f"slot_words{a}", align_bytes=64) for a in range(PASSES)]
-        slot_planes = keep.tile([P, S], U8, name="slot_planes", align_bytes=64)
+        raw = [keep.tile([P, 4, T], F32, name=f"raw{a}", align_bytes=ALIGN) for a in range(PASSES)]
+        grouped = [keep.tile([P, T, 4], BF16, name=f"grouped{a}", align_bytes=ALIGN) for a in range(PASSES)]
+        slot_words = [keep.tile([P, S], U32, name=f"slot_words{a}", align_bytes=ALIGN) for a in range(PASSES)]
+        slot_planes = keep.tile([P, S], U8, name="slot_planes", align_bytes=ALIGN)
         y = [keep.tile([P, S], F32, name=f"y{h}") for h in range(HALVES)]
         gate_rows = keep.tile([P, T], F32, name="gate_rows")
         gate_cols = keep.tile([P, CHUNKS, TOP], F32, name="gate_cols")
@@ -70,20 +77,13 @@ def tile_moe_tk_lin_silu_kernel(tc, xT, w8_words, w8_scales, w4_words, w4_scales
         zero = keep.tile([P, 1], F32, name="zero")
 
         x_rows = xT.rearrange("(a p j) t -> a p j t", p=P, j=4)
-        nc.sync.dma_start(out=raw[ORDER[0]][:], in_=x_rows[ORDER[0]])
-        nc.sync.dma_start(offs_sb[:], offs)
-
-        nc.vector.memset(zero[:], 0.0)
-        nc.scalar.activation(gate_rows[:], zero[:].to_broadcast([P, T]), SILU)
-        nc.vector.memset(ws[:].rearrange("p e n -> p (e n)").bitcast(I32), 0)
-        nc.vector.memset(planes[:].bitcast(I32), 0)
-        nc.vector.memset(packed[:].bitcast(I32), 0)
-        nc.vector.memset(words[:, PASSES * T :], 0)
-
         w8_rows = w8_words.rearrange("e a p n r -> p (e a) (n r)").bitcast(I32)
         w4_rows = w4_words.rearrange("e a p n -> p (e a) n").bitcast(I32)
-        w8s_rows = w8_scales.rearrange("e a q n -> q (e a) n").bitcast(I32)
-        w4s_rows = w4_scales.rearrange("e a q n -> q (e a) n").bitcast(I32)
+        w8_scale_rows = w8_scales.rearrange("e a q n -> q (e a) n").bitcast(I32)
+        w4_scale_rows = w4_scales.rearrange("e a q n -> q (e a) n").bitcast(I32)
+
+        def load_x(a):
+            nc.sync.dma_start(out=raw[a][:], in_=x_rows[a])
 
         def load_w8(e0, e1):
             rows = slice(e0 * PASSES8, e1 * PASSES8)
@@ -93,102 +93,97 @@ def tile_moe_tk_lin_silu_kernel(tc, xT, w8_words, w8_scales, w4_words, w4_scales
             rows = slice(e0 * PASSES4, e1 * PASSES4)
             nc.sync.dma_start(out=w4[:, rows].bitcast(I32), in_=w4_rows[:, rows])
 
-        def load_w8_half(h):
-            nc.sync.dma_start(out=w8_late[h][:].bitcast(I32), in_=w8_rows[:, LATE * PASSES8 :, h * P : (h + 1) * P])
-
-        def load_w4_half(e0, e1, h):
+        def load_half(e, h):
             nc.sync.dma_start(
-                out=w4_late[h][:, (e0 - LATE) * PASSES4 : (e1 - LATE) * PASSES4].bitcast(I32),
-                in_=w4_rows[:, e0 * PASSES4 : e1 * PASSES4, h * P // 2 : (h + 1) * P // 2],
+                out=w8_late[h][:, (e - LATE) * PASSES8 : (e - LATE + 1) * PASSES8].bitcast(I32),
+                in_=w8_rows[:, e * PASSES8 : (e + 1) * PASSES8, h * P : (h + 1) * P],
+            )
+            nc.sync.dma_start(
+                out=w4_late[h][:, (e - LATE) * PASSES4 : (e - LATE + 1) * PASSES4].bitcast(I32),
+                in_=w4_rows[:, e * PASSES4 : (e + 1) * PASSES4, h * P // 2 : (h + 1) * P // 2],
             )
 
-        def load_x(a):
-            nc.sync.dma_start(out=raw[a][:], in_=x_rows[a])
-
-        def load_scales8(queue, e0, e1):
-            for r in range(4):
-                queue.dma_start(out=ws[W8_ROW + r : P : 32, e0 * PASSES4 : e0 * PASSES4 + (e1 - e0) * PASSES8].bitcast(I32), in_=w8s_rows[r:16:4, e0 * PASSES8 : e1 * PASSES8])
-
-        def load_scales4(queue, e0, e1):
-            for r in range(4):
-                queue.dma_start(out=ws[r:P:32, e0 * PASSES4 : e1 * PASSES4].bitcast(I32), in_=w4s_rows[r:16:4, e0 * PASSES4 : e1 * PASSES4])
-
-        make_identity(nc, ident[:])
-        load_scales8(nc.gpsimd, FIRST, E)
-        load_scales4(nc.gpsimd, FIRST, E)
-        load_x(ORDER[1])
-        load_x(ORDER[2])
-
-        def interleave_scalar(a, t0, t1):
-            nc.scalar.activation(grouped[a][:, t0:t1, :], raw[a][:, :, t0:t1].rearrange("p j t -> p t j"), COPY)
-
-        def interleave_vector(a, t0, t1):
-            nc.vector.tensor_copy(out=grouped[a][:, t0:t1, :], in_=raw[a][:, :, t0:t1].rearrange("p j t -> p t j"))
+        def bank(i):
+            return psum.tile([P, T], F32, name=f"bank{i % BANKS}")
 
         def quantise(a):
-            for t0, t1 in ((0, 256), (256, T)):
-                w0, s0, k = WORD_COLUMN[a], T if a == ORDER[0] else 0, 0 if a == ORDER[0] else PLANE_ROW[a]
+            column, row = (T, 0) if a == ORDER[0] else (0, PLANE_ROW[a])
+            for t0, t1 in ((0, SPLIT), (SPLIT, T)):
                 nc.vector.quantize_mx(
-                    out=words[:, w0 + t0 : w0 + t1].bitcast(FP8X4),
-                    scales=planes[k:P, s0 + t0 : s0 + t1],
+                    out=words[:, WORD_COLUMN[a] + t0 : WORD_COLUMN[a] + t1].bitcast(FP8X4),
+                    scales=planes[row:P, column + t0 : column + t1],
                     in_=grouped[a][:, t0:t1, :].rearrange("p t j -> p (t j)"),
                 )
 
-        def gather_words(a, j0, j1, w1):
+        def interleaved(a, t0, t1):
+            return raw[a][:, :, t0:t1].rearrange("p j t -> p t j")
+
+        def gather_words(a, j0, j1, end):
             nc.vector.tensor_copy(
                 out=slot_words[a][:, j0:j1],
-                in_=words[:, WORD_COLUMN[a] : w1].bitcast(U32).indirect(offs_sb[:, j0 // 16 : j1 // 16]),
+                in_=words[:, WORD_COLUMN[a] : end].bitcast(U32).indirect(offs_sb[:, j0 // 16 : j1 // 16]),
             )
 
         def gather_planes(j0, j1):
             nc.vector.tensor_copy(out=slot_planes[:, j0:j1], in_=packed[:].indirect(offs_sb[:, j0 // 16 : j1 // 16]))
 
         def shift_planes(j0, j1):
-            for a in shifted:
-                k = PLANE_ROW[a]
-                nc.sync.dma_start(out=shifted[a][0:112, j0:j1].bitcast(I32), in_=slot_planes[k : k + 112, j0:j1].bitcast(I32))
+            for a in SHIFTED:
+                row = PLANE_ROW[a]
+                nc.sync.dma_start(out=shifted[a][0:MOVED, j0:j1].bitcast(I32), in_=slot_planes[row : row + MOVED, j0:j1].bitcast(I32))
 
         def multiply(acc, a, e, h, order):
             cols = slice(e * C, (e + 1) * C)
             if a < PASSES8:
                 i = e * PASSES8 + a
                 lhsT = (w8[:, i, 4 * P * h : 4 * P * (h + 1)] if e < LATE else w8_late[h][:, i - LATE * PASSES8]).bitcast(FP8X4)
-                lhsT_scale = ws[W8_ROW:P, i if e < FIRST else i + FIRST, P * h : P * (h + 1)]
+                lhsT_scale = w_planes[W8_ROW:P, i, P * h : P * (h + 1)]
             else:
                 i = e * PASSES4 + a - PASSES8
                 lhsT = (w4[:, i, 2 * P * h : 2 * P * (h + 1)] if e < LATE else w4_late[h][:, i - LATE * PASSES4]).bitcast(FP4X4)
-                lhsT_scale = ws[:, i, P * h : P * (h + 1)]
+                lhsT_scale = w_planes[:, i, P * h : P * (h + 1)]
             nc.tensor.matmul_mx(
                 out=acc[:, 0:C],
                 lhsT=lhsT,
                 lhsT_scale=lhsT_scale,
                 rhs=slot_words[a][:, cols].bitcast(FP8X4),
-                rhs_scale=shifted[a][:, cols] if a in shifted else slot_planes[PLANE_ROW[a] : P, cols],
+                rhs_scale=shifted[a][:, cols] if a in SHIFTED else slot_planes[PLANE_ROW[a] : P, cols],
                 start=(a == order[0]),
                 stop=(a == order[-1]),
             )
+            if a == order[-1]:
+                nc.scalar.activation(y[h][:, cols], acc[:, 0:C], SILU, bias=bias[:, h, e : e + 1])
 
-        def bank(i):
-            return psum.tile([P, T], F32, name=f"bank{i}")
+        load_x(ORDER[0])
+        nc.sync.dma_start(offs_sb[:], offs)
 
-        def activate(acc, e, h):
-            nc.scalar.activation(y[h][:, e * C : (e + 1) * C], acc[:, 0:C], SILU, bias=bias[:, h, e : e + 1])
-
-        interleave_vector(ORDER[0], 0, 256)
-        interleave_scalar(ORDER[0], 256, T)
-        quantise(ORDER[0])
-        nc.sync.dma_start(out=packed[16:P, 0:T].bitcast(I32), in_=planes[0:112, T : 2 * T].bitcast(I32))
-        load_x(ORDER[3])
-        nc.sync.dma_start(out=gate_rows[0:TOP, :], in_=gate[:, 0, :])
-        load_x(ORDER[4])
-        load_scales8(nc.sync, 0, FIRST)
-        load_w8(0, 2)
-        load_scales4(nc.sync, 0, FIRST)
-        load_w8(2, FIRST)
-        for e in (0, 2):
-            load_w4(e, e + 2)
+        nc.vector.memset(zero[:], 0.0)
+        nc.scalar.activation(gate_rows[:], zero[:].to_broadcast([P, T]), SILU)
+        nc.vector.memset(w_planes[:].rearrange("p e n -> p (e n)").bitcast(I32), 0)
+        nc.vector.memset(planes[:].bitcast(I32), 0)
+        nc.vector.memset(packed[:].bitcast(I32), 0)
+        nc.vector.memset(words[:, PASSES * T :], 0)
+        make_identity(nc, ident[:])
         for a in ORDER[1:]:
-            interleave_scalar(a, 0, T)
+            load_x(a)
+
+        first, second = ORDER[:2]
+        nc.vector.tensor_copy(out=grouped[first][:, 0:SPLIT, :], in_=interleaved(first, 0, SPLIT))
+        nc.scalar.activation(grouped[first][:, SPLIT:T, :], interleaved(first, SPLIT, T), COPY)
+        quantise(first)
+        nc.sync.dma_start(out=packed[PLANE_ROW[first] : P, 0:T].bitcast(I32), in_=planes[0:MOVED, T : 2 * T].bitcast(I32))
+
+        nc.sync.dma_start(out=gate_rows[0:TOP, :], in_=gate[:, 0, :])
+        for r in range(4):
+            nc.sync.dma_start(out=w_planes[W8_ROW + r : P : QUADRANT, 0 : E * PASSES8].bitcast(I32), in_=w8_scale_rows[r:16:4])
+        for r in range(4):
+            nc.sync.dma_start(out=w_planes[r:P:QUADRANT].bitcast(I32), in_=w4_scale_rows[r:16:4])
+        for load in (load_w8, load_w4):
+            for e in range(*BATCHES[0], 2):
+                load(e, e + 2)
+        for a in ORDER[1:]:
+            nc.scalar.activation(grouped[a][:], interleaved(a, 0, T), COPY)
+
         turned_gate = bank(0)
         for c in range(CHUNKS):
             nc.tensor.transpose(turned_gate[:, c * P : (c + 1) * P], gate_rows[:, c * P : (c + 1) * P], ident[:])
@@ -198,96 +193,100 @@ def tile_moe_tk_lin_silu_kernel(tc, xT, w8_words, w8_scales, w4_words, w4_scales
             for c in range(CHUNKS):
                 nc.tensor.transpose(spread[:, c * P : (c + 1) * P], gate_cols[:, c, r : r + 1].to_broadcast([P, P]), ident[:])
             nc.scalar.copy(gates[:, r, :], spread[:])
-        shifted = {a: keep.tile([P, S], U8, name=f"shifted{a}", tag=f"raw{a}", align_bytes=64) for a in (3, 4)}
-        first, second = ORDER[:2]
-        for j in range(0, S, 512):
-            gather_words(first, j, j + 512, WORD_COLUMNS)
-        quantise(second)
-        for j in range(0, S, S // 2):
-            gather_words(second, j, j + S // 2, WORD_COLUMN[second] + WIDE)
-        quantise(1)
-        quantise(2)
-        quantise(3)
-        for q in range(0, P, 32):
-            nc.vector.tensor_copy(out=packed[q : q + 16, 0:T].bitcast(I32), in_=planes[q : q + 16, 0:T].bitcast(I32))
-        gather_planes(0, 512)
-        gather_planes(512, 1024)
-        shift_planes(0, 1024)
-        nc.sync.dma_start(out=bias[:], in_=b.rearrange("(h p) e -> p h e", p=P))
-        load_w8(4, 6)
-        load_w4(4, 6)
-        load_w8(6, 8)
-        load_w4(6, 8)
 
-        turn = 0
+        shifted = {a: keep.tile([P, S], U8, name=f"shifted{a}", tag=f"raw{a}", align_bytes=ALIGN) for a in SHIFTED}
+
+        for j in range(0, S, FEW):
+            gather_words(first, j, j + FEW, WORD_COLUMNS)
+        quantise(second)
+        for j in range(0, S, MANY):
+            gather_words(second, j, j + MANY, WORD_COLUMN[second] + WIDE)
+        for a in ORDER[2:]:
+            quantise(a)
+
+        for q in range(0, P, QUADRANT):
+            rows = slice(q, q + QUANTISED_ROWS)
+            nc.vector.tensor_copy(out=packed[rows, 0:T].bitcast(I32), in_=planes[rows, 0:T].bitcast(I32))
+        for j in range(0, LATE * C, FEW):
+            gather_planes(j, j + FEW)
+        nc.sync.dma_start(out=bias[:], in_=b.rearrange("(h p) e -> p h e", p=P))
+        load_w8(*BATCHES[1])
+        shift_planes(0, LATE * C)
+        load_w4(*BATCHES[1])
+        load_w8(*BATCHES[2])
+        for r, pos in enumerate((pos1, pos2, pos3, pos4)):
+            nc.sync.dma_start(pos_sb[r][:], pos)
+        load_w4(*BATCHES[2])
+        gather_planes(LATE * C, S)
+        shift_planes(LATE * C, S)
+        for h in range(HALVES):
+            for e in range(LATE, E):
+                load_half(e, h)
+
+        opened = 0
         for e0, e1 in BATCHES:
-            for a in (1, 2, 3):
-                if (a, e1) == (3, E):
-                    for e in range(e0, e1):
-                        gather_words(a, e * C, (e + 1) * C, 4 * T)
-                else:
-                    gather_words(a, e0 * C, e1 * C, 4 * T)
-            if e0 == 0:
-                gather_planes(1024, S)
-                shift_planes(1024, S)
-                for h in range(HALVES):
-                    load_w8_half(h)
-                    for f0, f1 in ((LATE, E - 2), (E - 2, E - 1), (E - 1, E)):
-                        load_w4_half(f0, f1, h)
-                    if h == 0:
-                        for r, pos in enumerate((pos1, pos2, pos3, pos4)):
-                            nc.sync.dma_start(pos_sb[r][:], pos)
+            last = e1 == E
+            for a in ORDER[2:]:
+                step = 1 if last and a == ORDER[-1] else e1 - e0
+                for e in range(e0, e1, step):
+                    gather_words(a, e * C, (e + step) * C, LATE_END)
             groups = [(e, h) for h in range(HALVES) for e in range(e0, e1) if h == 0 or e < LATE]
-            accs = {g: bank((turn + i) % BANKS) for i, g in enumerate(groups)}
-            turn += len(groups)
-            order = (0, 4, 1, 2, 3) if e1 == E else (0, 1, 2, 3, 4)
-            if e1 == E:
-                steps = [(a, e, h) for a in order for e, h in groups]
+            accs = {group: bank(opened + i) for i, group in enumerate(groups)}
+            opened += len(groups)
+            if last:
+                order = (second, first) + ORDER[2:]
+                steps = [(a, group) for a in order for group in groups]
             elif e0 == 0:
-                steps = [(a, e, h) for a in range(3) for e, h in groups] + [(a, e, h) for e, h in groups for a in (3, 4)]
+                order = range(PASSES)
+                steps = [(a, group) for a in order if a not in SHIFTED for group in groups]
+                steps += [(a, group) for group in groups for a in SHIFTED]
             else:
-                steps = [(a, e, h) for e, h in groups for a in range(PASSES)]
-            for a, e, h in steps:
+                order = range(PASSES)
+                steps = [(a, group) for group in groups for a in order]
+            for a, (e, h) in steps:
                 multiply(accs[e, h], a, e, h, order)
-                if a == order[-1]:
-                    activate(accs[e, h], e, h)
+        late_bank = opened - LATE_BANKS
         for e in range(LATE, E):
-            acc = bank((turn - 3 + (e - LATE) % 3) % BANKS)
+            acc = bank(late_bank + (e - LATE) % LATE_BANKS)
             for a in range(PASSES):
                 multiply(acc, a, e, 1, range(PASSES))
-            activate(acc, e, 1)
 
         part = [[keep.tile([P, T], F32, name=f"part{h}_{r}") for r in range(TOP)] for h in range(HALVES)]
         turned = [keep.tile([P, T], F32, name=f"turned{h}") for h in range(HALVES)]
         three = keep.tile([P, T], F32, name="three")
-        total = [keep.tile([P, T], F32, name=f"total{h}") for h in range(HALVES)]
+        total = [keep.tile([P, T], F32, name=f"total{h}", align_bytes=ALIGN) for h in range(HALVES)]
 
-        def pick(h, r):
-            nc.vector.tensor_tensor(part[h][r][:], y[h][:].indirect(pos_sb[r][:]), gates[:, r, :], MULT)
+        def add_turned(acc, h, r, c, count):
+            nc.tensor.matmul(acc, part[h][r][:, c * P : (c + 1) * P], ident[:], start=(r == 0), stop=(r == count - 1), is_transpose=True)
 
-        def sum_on_tensor(h, count):
-            banks = [bank((turn - 3 + 3 * h + c) % BANKS) for c in range(CHUNKS)]
-            for r in range(count):
-                for c in range(CHUNKS):
-                    nc.tensor.matmul(banks[c][:, 0:P], part[h][r][:, c * P : (c + 1) * P], ident[:], start=(r == 0), stop=(r == count - 1), is_transpose=True)
-            back = bank((turn + 3 + h) % BANKS)
-            for c in range(CHUNKS):
-                nc.scalar.copy(turned[h][:, c * P : (c + 1) * P], banks[c][:, 0:P])
-                nc.tensor.transpose(back[:, c * P : (c + 1) * P], turned[h][:, c * P : (c + 1) * P], ident[:])
-            return back
-
-        def store(h, t0, t1):
-            nc.sync.dma_start(out=out[h * P : (h + 1) * P, t0:t1], in_=total[h][:, t0:t1])
+        def turn_back(back, h, c):
+            nc.tensor.transpose(back[:, c * P : (c + 1) * P], turned[h][:, c * P : (c + 1) * P], ident[:])
 
         for h in range(HALVES):
             for r in range(TOP):
-                pick(h, r)
-        back = sum_on_tensor(0, TOP)
+                nc.vector.tensor_tensor(part[h][r][:], y[h][:].indirect(pos_sb[r][:]), gates[:, r, :], MULT)
+        last_bank = late_bank + (E - 1 - LATE) % LATE_BANKS
+        four = bank(last_bank)
+        for c in range(CHUNKS):
+            for r in range(TOP):
+                add_turned(four[:, c * P : (c + 1) * P], 0, r, c, TOP)
+        nc.scalar.copy(turned[0][:], four[:])
+        back = bank(last_bank + 1)
+        for c in range(CHUNKS):
+            turn_back(back, 0, c)
         nc.scalar.copy(total[0][:], back[:])
-        store(0, 0, T)
-        back = sum_on_tensor(1, 2)
-        for t0 in (0, T // 2):
-            nc.vector.tensor_tensor(three[:, t0 : t0 + T // 2], part[1][2][:, t0 : t0 + T // 2], back[:, t0 : t0 + T // 2], ADD)
-        for t0 in (0, T // 2):
-            nc.vector.tensor_tensor(total[1][:, t0 : t0 + T // 2], three[:, t0 : t0 + T // 2], part[1][3][:, t0 : t0 + T // 2], ADD)
-            store(1, t0, t0 + T // 2)
+        nc.sync.dma_start(out=out[0:P, :], in_=total[0][:])
+        sums = [bank(last_bank + 2 + c) for c in range(CHUNKS)]
+        for r in range(2):
+            for c in range(CHUNKS):
+                add_turned(sums[c][:, 0:P], 1, r, c, 2)
+        two = bank(last_bank + 2 + CHUNKS)
+        for c in range(CHUNKS):
+            nc.scalar.copy(turned[1][:, c * P : (c + 1) * P], sums[c][:, 0:P])
+            turn_back(two, 1, c)
+        runs = [slice(t0, t0 + T // 2) for t0 in (0, T // 2)]
+        for run in runs:
+            nc.vector.tensor_tensor(three[:, run], part[1][2][:, run], two[:, run], ADD)
+        for run in runs:
+            nc.vector.tensor_tensor(total[1][:, run], three[:, run], part[1][3][:, run], ADD)
+            nc.sync.dma_start(out=out[P:N, run], in_=total[1][:, run])

@@ -30,17 +30,17 @@ ADD = mybir.AluOpType.add
 ALIGN = 256
 QUADRANT = 32
 W8_ROW = 4
-PLANE_ROW = (4, 12, 0, 8, 16)
+PLANE_ROW = (4, 12, 0, 8)
 SHIFTED = (3, 4)
-QUANTISED_ROWS = 16
-MOVED = P - QUANTISED_ROWS
+FIFTH = P - 16
 ORDER = (4, 0, 1, 2, 3)
 SPLIT = 256
+PIECE = 128
 FEW, NARROW = 512, 704
 MANY, WIDE = 768, 1024
-WORD_COLUMN = (3 * T, 0, T, 2 * T, 4 * T)
-WORD_COLUMNS = 4 * T + NARROW
-LATE_END = 4 * T
+GAP = 128
+WORD_COLUMN = (4 * T + GAP, 0, T, 2 * T, 3 * T)
+WORD_COLUMNS = WORD_COLUMN[0] + WIDE
 BATCHES = ((0, 4), (4, 6), (6, 8), (8, 10), (10, 12))
 LATE = 8
 LATE_BANKS = 3
@@ -68,13 +68,14 @@ def tile_moe_tk_lin_silu_kernel(tc, xT, w8_words, w8_scales, w4_words, w4_scales
         gates = keep.tile([P, TOP, T], F32, name="gates")
         raw = [keep.tile([P, 4, T], F32, name=f"raw{a}", align_bytes=ALIGN) for a in range(PASSES)]
         grouped = [keep.tile([P, T, 4], BF16, name=f"grouped{a}", align_bytes=ALIGN) for a in range(PASSES)]
-        slot_words = [keep.tile([P, S], U32, name=f"slot_words{a}", align_bytes=ALIGN) for a in range(PASSES)]
+        slot_words = [keep.tile([P, FEW if a in ORDER[2:] else S], U32, name=f"slot_words{a}", align_bytes=ALIGN) for a in range(PASSES)]
         slot_planes = keep.tile([P, S], U8, name="slot_planes", align_bytes=ALIGN)
         y = [keep.tile([P, S], F32, name=f"y{h}") for h in range(HALVES)]
         gate_rows = keep.tile([P, T], F32, name="gate_rows")
         gate_cols = keep.tile([P, CHUNKS, TOP], F32, name="gate_cols")
         ident = keep.tile([P, P], F32, name="ident")
         zero = keep.tile([P, 1], F32, name="zero")
+        late_words = []
 
         x_rows = xT.rearrange("(a p j) t -> a p j t", p=P, j=4)
         w8_rows = w8_words.rearrange("e a p n r -> p (e a) (n r)").bitcast(I32)
@@ -106,9 +107,9 @@ def tile_moe_tk_lin_silu_kernel(tc, xT, w8_words, w8_scales, w4_words, w4_scales
         def bank(i):
             return psum.tile([P, T], F32, name=f"bank{i % BANKS}")
 
-        def quantise(a):
+        def quantise(a, cuts=((0, SPLIT), (SPLIT, T))):
             column, row = (T, 0) if a == ORDER[0] else (0, PLANE_ROW[a])
-            for t0, t1 in ((0, SPLIT), (SPLIT, T)):
+            for t0, t1 in cuts:
                 nc.vector.quantize_mx(
                     out=words[:, WORD_COLUMN[a] + t0 : WORD_COLUMN[a] + t1].bitcast(FP8X4),
                     scales=planes[row:P, column + t0 : column + t1],
@@ -118,9 +119,15 @@ def tile_moe_tk_lin_silu_kernel(tc, xT, w8_words, w8_scales, w4_words, w4_scales
         def interleaved(a, t0, t1):
             return raw[a][:, :, t0:t1].rearrange("p j t -> p t j")
 
+        def slots(a, j0, j1):
+            if a in ORDER[2:] and j0 >= FEW:
+                column = (a - 1) * (S - FEW) - FEW
+                return late_words[0][:, column + j0 : column + j1]
+            return slot_words[a][:, j0:j1]
+
         def gather_words(a, j0, j1, end):
             nc.vector.tensor_copy(
-                out=slot_words[a][:, j0:j1],
+                out=slots(a, j0, j1),
                 in_=words[:, WORD_COLUMN[a] : end].bitcast(U32).indirect(offs_sb[:, j0 // 16 : j1 // 16]),
             )
 
@@ -128,9 +135,13 @@ def tile_moe_tk_lin_silu_kernel(tc, xT, w8_words, w8_scales, w4_words, w4_scales
             nc.vector.tensor_copy(out=slot_planes[:, j0:j1], in_=packed[:].indirect(offs_sb[:, j0 // 16 : j1 // 16]))
 
         def shift_planes(j0, j1):
-            for a in SHIFTED:
-                row = PLANE_ROW[a]
-                nc.sync.dma_start(out=shifted[a][0:MOVED, j0:j1].bitcast(I32), in_=slot_planes[row : row + MOVED, j0:j1].bitcast(I32))
+            row = PLANE_ROW[3]
+            nc.sync.dma_start(out=shifted[3][0:FIFTH, j0:j1].bitcast(I32), in_=slot_planes[row : row + FIFTH, j0:j1].bitcast(I32))
+            for q in range(4):
+                nc.sync.dma_start(
+                    out=shifted[4][QUADRANT * q : QUADRANT * q + 4, j0:j1].bitcast(I32),
+                    in_=slot_planes[FIFTH + 4 * q : FIFTH + 4 * q + 4, j0:j1].bitcast(I32),
+                )
 
         def multiply(acc, a, e, h, order):
             cols = slice(e * C, (e + 1) * C)
@@ -146,7 +157,7 @@ def tile_moe_tk_lin_silu_kernel(tc, xT, w8_words, w8_scales, w4_words, w4_scales
                 out=acc[:, 0:C],
                 lhsT=lhsT,
                 lhsT_scale=lhsT_scale,
-                rhs=slot_words[a][:, cols].bitcast(FP8X4),
+                rhs=slots(a, e * C, (e + 1) * C).bitcast(FP8X4),
                 rhs_scale=shifted[a][:, cols] if a in SHIFTED else slot_planes[PLANE_ROW[a] : P, cols],
                 start=(a == order[0]),
                 stop=(a == order[-1]),
@@ -162,25 +173,31 @@ def tile_moe_tk_lin_silu_kernel(tc, xT, w8_words, w8_scales, w4_words, w4_scales
         nc.vector.memset(w_planes[:].rearrange("p e n -> p (e n)").bitcast(I32), 0)
         nc.vector.memset(planes[:].bitcast(I32), 0)
         nc.vector.memset(packed[:].bitcast(I32), 0)
-        nc.vector.memset(words[:, PASSES * T :], 0)
+        nc.vector.memset(words[:, 4 * T : 4 * T + GAP], 0)
+        nc.vector.memset(words[:, WORD_COLUMN[0] + T :], 0)
         make_identity(nc, ident[:])
         for a in ORDER[1:]:
             load_x(a)
 
         first, second = ORDER[:2]
-        nc.vector.tensor_copy(out=grouped[first][:, 0:SPLIT, :], in_=interleaved(first, 0, SPLIT))
+        for t in range(0, SPLIT, PIECE):
+            nc.vector.tensor_copy(out=grouped[first][:, t : t + PIECE, :], in_=interleaved(first, t, t + PIECE))
         nc.scalar.activation(grouped[first][:, SPLIT:T, :], interleaved(first, SPLIT, T), COPY)
-        quantise(first)
-        nc.sync.dma_start(out=packed[PLANE_ROW[first] : P, 0:T].bitcast(I32), in_=planes[0:MOVED, T : 2 * T].bitcast(I32))
+        quantise(first, [(t, t + PIECE) for t in range(0, T, PIECE)])
+        for q in range(4):
+            nc.sync.dma_start(
+                out=packed[FIFTH + 4 * q : FIFTH + 4 * q + 4, 0:T].bitcast(I32),
+                in_=planes[QUADRANT * q : QUADRANT * q + 4, T : 2 * T].bitcast(I32),
+            )
 
         nc.sync.dma_start(out=gate_rows[0:TOP, :], in_=gate[:, 0, :])
         for r in range(4):
             nc.sync.dma_start(out=w_planes[W8_ROW + r : P : QUADRANT, 0 : E * PASSES8].bitcast(I32), in_=w8_scale_rows[r:16:4])
         for r in range(4):
             nc.sync.dma_start(out=w_planes[r:P:QUADRANT].bitcast(I32), in_=w4_scale_rows[r:16:4])
-        for load in (load_w8, load_w4):
-            for e in range(*BATCHES[0], 2):
-                load(e, e + 2)
+        for r, pos in enumerate((pos1, pos2, pos3, pos4)):
+            (load_w8, load_w4)[r // 2](2 * (r % 2), 2 * (r % 2) + 2)
+            nc.sync.dma_start(pos_sb[r][:], pos)
         for a in ORDER[1:]:
             nc.scalar.activation(grouped[a][:], interleaved(a, 0, T), COPY)
 
@@ -196,17 +213,18 @@ def tile_moe_tk_lin_silu_kernel(tc, xT, w8_words, w8_scales, w4_words, w4_scales
 
         shifted = {a: keep.tile([P, S], U8, name=f"shifted{a}", tag=f"raw{a}", align_bytes=ALIGN) for a in SHIFTED}
 
-        for j in range(0, S, FEW):
-            gather_words(first, j, j + FEW, WORD_COLUMNS)
+        for j in range(0, S - T, T):
+            gather_words(first, j, j + T, WORD_COLUMN[second])
         quantise(second)
+        gather_words(first, S - T, S, WORD_COLUMN[second] + SPLIT)
         for j in range(0, S, MANY):
-            gather_words(second, j, j + MANY, WORD_COLUMN[second] + WIDE)
-        for a in ORDER[2:]:
-            quantise(a)
-
-        for q in range(0, P, QUADRANT):
-            rows = slice(q, q + QUANTISED_ROWS)
-            nc.vector.tensor_copy(out=packed[rows, 0:T].bitcast(I32), in_=planes[rows, 0:T].bitcast(I32))
+            gather_words(second, j, j + MANY, WORD_COLUMNS)
+        quantise(1)
+        quantise(2)
+        quantise(3)
+        gather_words(1, 0, C, WORD_COLUMN[3] + SPLIT)
+        nc.vector.tensor_copy(out=packed[0:FIFTH, 0:T].bitcast(I32), in_=planes[0:FIFTH, 0:T].bitcast(I32))
+        gather_words(1, C, 2 * C, WORD_COLUMN[3] + SPLIT)
         for j in range(0, LATE * C, FEW):
             gather_planes(j, j + FEW)
         nc.sync.dma_start(out=bias[:], in_=b.rearrange("(h p) e -> p h e", p=P))
@@ -214,22 +232,25 @@ def tile_moe_tk_lin_silu_kernel(tc, xT, w8_words, w8_scales, w4_words, w4_scales
         shift_planes(0, LATE * C)
         load_w4(*BATCHES[1])
         load_w8(*BATCHES[2])
-        for r, pos in enumerate((pos1, pos2, pos3, pos4)):
-            nc.sync.dma_start(pos_sb[r][:], pos)
         load_w4(*BATCHES[2])
+        load_half(LATE, 0)
         gather_planes(LATE * C, S)
+        gather_words(1, 2 * C, FEW, WORD_COLUMN[3] + T)
+        gather_words(2, 0, FEW, WORD_COLUMN[3] + T)
+        gather_words(3, 0, FEW, WORD_COLUMN[3] + NARROW)
+        late_words.append(keep.tile([P, PASSES4 * (S - FEW)], U32, name="late_words", tag="packed", align_bytes=ALIGN))
         shift_planes(LATE * C, S)
         for h in range(HALVES):
-            for e in range(LATE, E):
+            for e in range(LATE + 1 - h, E):
                 load_half(e, h)
 
         opened = 0
         for e0, e1 in BATCHES:
             last = e1 == E
-            for a in ORDER[2:]:
+            for a in ORDER[2:] if e0 > 0 else ():
                 step = 1 if last and a == ORDER[-1] else e1 - e0
                 for e in range(e0, e1, step):
-                    gather_words(a, e * C, (e + step) * C, LATE_END)
+                    gather_words(a, e * C, (e + step) * C, WORD_COLUMN[3] + (NARROW if a == 3 else T))
             groups = [(e, h) for h in range(HALVES) for e in range(e0, e1) if h == 0 or e < LATE]
             accs = {group: bank(opened + i) for i, group in enumerate(groups)}
             opened += len(groups)

@@ -38,7 +38,7 @@ SPLIT = 256
 PIECE = 128
 FEW, NARROW = 512, 704
 MANY, WIDE = 768, 1024
-GAP = 128
+GAP = NARROW - T
 WORD_COLUMN = (4 * T + GAP, 0, T, 2 * T, 3 * T)
 WORD_COLUMNS = WORD_COLUMN[0] + WIDE
 BATCHES = ((0, 4), (4, 6), (6, 8), (8, 10), (10, 12))
@@ -63,10 +63,12 @@ def tile_moe_tk_lin_silu_kernel(tc, xT, w8_words, w8_scales, w4_words, w4_scales
         w4 = keep.tile([P, LATE * PASSES4, 2 * N], U8, name="w4", align_bytes=ALIGN)
         w8_late = [keep.tile([P, (E - LATE) * PASSES8, 4 * P], U8, name=f"w8_late{h}", align_bytes=ALIGN) for h in range(HALVES)]
         w4_late = [keep.tile([P, (E - LATE) * PASSES4, 2 * P], U8, name=f"w4_late{h}", align_bytes=ALIGN) for h in range(HALVES)]
-        w_planes = keep.tile([P, E * PASSES4, N], U8, name="w_planes", align_bytes=ALIGN)
         bias = keep.tile([P, HALVES, E], F32, name="bias")
         gates = keep.tile([P, TOP, T], F32, name="gates")
-        raw = [keep.tile([P, 4, T], F32, name=f"raw{a}", align_bytes=ALIGN) for a in range(PASSES)]
+        early = keep.tile([P, 2, 4, T], F32, name="early", align_bytes=ALIGN)
+        raw = {a: early[:, i] for i, a in enumerate(ORDER[:2])}
+        for a in ORDER[2:]:
+            raw[a] = keep.tile([P, 4, T], F32, name=f"raw{a}", align_bytes=ALIGN)[:]
         grouped = [keep.tile([P, T, 4], BF16, name=f"grouped{a}", align_bytes=ALIGN) for a in range(PASSES)]
         slot_words = [keep.tile([P, FEW if a in ORDER[2:] else S], U32, name=f"slot_words{a}", align_bytes=ALIGN) for a in range(PASSES)]
         slot_planes = keep.tile([P, S], U8, name="slot_planes", align_bytes=ALIGN)
@@ -84,7 +86,7 @@ def tile_moe_tk_lin_silu_kernel(tc, xT, w8_words, w8_scales, w4_words, w4_scales
         w4_scale_rows = w4_scales.rearrange("e a q n -> q (e a) n").bitcast(I32)
 
         def load_x(a):
-            nc.sync.dma_start(out=raw[a][:], in_=x_rows[a])
+            nc.sync.dma_start(out=raw[a], in_=x_rows[a])
 
         def load_w8(e0, e1):
             rows = slice(e0 * PASSES8, e1 * PASSES8)
@@ -117,7 +119,10 @@ def tile_moe_tk_lin_silu_kernel(tc, xT, w8_words, w8_scales, w4_words, w4_scales
                 )
 
         def interleaved(a, t0, t1):
-            return raw[a][:, :, t0:t1].rearrange("p j t -> p t j")
+            return (
+                grouped[a][:, t0:t1, :].rearrange("p (c i) j -> p c j i", i=4),
+                raw[a][:, :, t0:t1].rearrange("p j (c i) -> p c j i", i=4),
+            )
 
         def slots(a, j0, j1):
             if a in ORDER[2:] and j0 >= FEW:
@@ -170,9 +175,8 @@ def tile_moe_tk_lin_silu_kernel(tc, xT, w8_words, w8_scales, w4_words, w4_scales
 
         nc.vector.memset(zero[:], 0.0)
         nc.scalar.activation(gate_rows[:], zero[:].to_broadcast([P, T]), SILU)
-        nc.vector.memset(w_planes[:].rearrange("p e n -> p (e n)").bitcast(I32), 0)
         nc.vector.memset(planes[:].bitcast(I32), 0)
-        nc.vector.memset(packed[:].bitcast(I32), 0)
+        nc.vector.memset(packed[:, T:].bitcast(I32), 0)
         nc.vector.memset(words[:, 4 * T : 4 * T + GAP], 0)
         nc.vector.memset(words[:, WORD_COLUMN[0] + T :], 0)
         make_identity(nc, ident[:])
@@ -181,14 +185,18 @@ def tile_moe_tk_lin_silu_kernel(tc, xT, w8_words, w8_scales, w4_words, w4_scales
 
         first, second = ORDER[:2]
         for t in range(0, SPLIT, PIECE):
-            nc.vector.tensor_copy(out=grouped[first][:, t : t + PIECE, :], in_=interleaved(first, t, t + PIECE))
-        nc.scalar.activation(grouped[first][:, SPLIT:T, :], interleaved(first, SPLIT, T), COPY)
+            nc.vector.tensor_copy(*interleaved(first, t, t + PIECE))
+        nc.scalar.activation(*interleaved(first, SPLIT, T), COPY)
         quantise(first, [(t, t + PIECE) for t in range(0, T, PIECE)])
         for q in range(4):
             nc.sync.dma_start(
                 out=packed[FIFTH + 4 * q : FIFTH + 4 * q + 4, 0:T].bitcast(I32),
                 in_=planes[QUADRANT * q : QUADRANT * q + 4, T : 2 * T].bitcast(I32),
             )
+
+        for a in ORDER[1:]:
+            nc.scalar.activation(*interleaved(a, 0, T), COPY)
+        w_planes = keep.tile([P, E * PASSES4, N], U8, name="w_planes", tag="early", align_bytes=ALIGN)
 
         nc.sync.dma_start(out=gate_rows[0:TOP, :], in_=gate[:, 0, :])
         for r in range(4):
@@ -198,8 +206,6 @@ def tile_moe_tk_lin_silu_kernel(tc, xT, w8_words, w8_scales, w4_words, w4_scales
         for r, pos in enumerate((pos1, pos2, pos3, pos4)):
             (load_w8, load_w4)[r // 2](2 * (r % 2), 2 * (r % 2) + 2)
             nc.sync.dma_start(pos_sb[r][:], pos)
-        for a in ORDER[1:]:
-            nc.scalar.activation(grouped[a][:], interleaved(a, 0, T), COPY)
 
         turned_gate = bank(0)
         for c in range(CHUNKS):
@@ -211,12 +217,12 @@ def tile_moe_tk_lin_silu_kernel(tc, xT, w8_words, w8_scales, w4_words, w4_scales
                 nc.tensor.transpose(spread[:, c * P : (c + 1) * P], gate_cols[:, c, r : r + 1].to_broadcast([P, P]), ident[:])
             nc.scalar.copy(gates[:, r, :], spread[:])
 
-        shifted = {a: keep.tile([P, S], U8, name=f"shifted{a}", tag=f"raw{a}", align_bytes=ALIGN) for a in SHIFTED}
+        shifted = {a: keep.tile([P, S], U8, name=f"shifted{a}", tag=f"raw{a - 1}", align_bytes=ALIGN) for a in SHIFTED}
 
-        for j in range(0, S - T, T):
-            gather_words(first, j, j + T, WORD_COLUMN[second])
+        for j in range(0, S - C, FEW):
+            gather_words(first, j, min(j + FEW, S - C), WORD_COLUMN[second])
         quantise(second)
-        gather_words(first, S - T, S, WORD_COLUMN[second] + SPLIT)
+        gather_words(first, S - C, S, WORD_COLUMN[second] + SPLIT)
         for j in range(0, S, MANY):
             gather_words(second, j, j + MANY, WORD_COLUMNS)
         quantise(1)

@@ -42,7 +42,7 @@ GAP = NARROW - T
 WORD_COLUMN = (4 * T + GAP, 0, T, 2 * T, 3 * T)
 WORD_COLUMNS = WORD_COLUMN[0] + WIDE
 BATCHES = ((0, 4), (4, 6), (6, 8), (8, 10), (10, 12))
-LATE = 8
+LATE = 4
 LATE_BANKS = 3
 
 
@@ -60,9 +60,8 @@ def tile_moe_tk_lin_silu_kernel(tc, xT, w8_words, w8_scales, w4_words, w4_scales
         planes = keep.tile([P, 2 * T], U8, name="planes", align_bytes=ALIGN)
         packed = keep.tile([P, NARROW], U8, name="packed", align_bytes=ALIGN)
         w8 = keep.tile([P, LATE * PASSES8, 4 * N], U8, name="w8", align_bytes=ALIGN)
-        w4 = keep.tile([P, LATE * PASSES4, 2 * N], U8, name="w4", align_bytes=ALIGN)
+        w4 = keep.tile([P, E * PASSES4, 2 * N], U8, name="w4", align_bytes=ALIGN)
         w8_late = [keep.tile([P, (E - LATE) * PASSES8, 4 * P], U8, name=f"w8_late{h}", align_bytes=ALIGN) for h in range(HALVES)]
-        w4_late = [keep.tile([P, (E - LATE) * PASSES4, 2 * P], U8, name=f"w4_late{h}", align_bytes=ALIGN) for h in range(HALVES)]
         bias = keep.tile([P, HALVES, E], F32, name="bias")
         gates = keep.tile([P, TOP, T], F32, name="gates")
         early = keep.tile([P, 2, 4, T], F32, name="early", align_bytes=ALIGN)
@@ -96,14 +95,10 @@ def tile_moe_tk_lin_silu_kernel(tc, xT, w8_words, w8_scales, w4_words, w4_scales
             rows = slice(e0 * PASSES4, e1 * PASSES4)
             nc.sync.dma_start(out=w4[:, rows].bitcast(I32), in_=w4_rows[:, rows])
 
-        def load_half(e, h):
+        def load_w8_half(e0, e1, h):
             nc.sync.dma_start(
-                out=w8_late[h][:, (e - LATE) * PASSES8 : (e - LATE + 1) * PASSES8].bitcast(I32),
-                in_=w8_rows[:, e * PASSES8 : (e + 1) * PASSES8, h * P : (h + 1) * P],
-            )
-            nc.sync.dma_start(
-                out=w4_late[h][:, (e - LATE) * PASSES4 : (e - LATE + 1) * PASSES4].bitcast(I32),
-                in_=w4_rows[:, e * PASSES4 : (e + 1) * PASSES4, h * P // 2 : (h + 1) * P // 2],
+                out=w8_late[h][:, (e0 - LATE) * PASSES8 : (e1 - LATE) * PASSES8].bitcast(I32),
+                in_=w8_rows[:, e0 * PASSES8 : e1 * PASSES8, h * P : (h + 1) * P],
             )
 
         def bank(i):
@@ -156,7 +151,7 @@ def tile_moe_tk_lin_silu_kernel(tc, xT, w8_words, w8_scales, w4_words, w4_scales
                 lhsT_scale = w_planes[W8_ROW:P, i, P * h : P * (h + 1)]
             else:
                 i = e * PASSES4 + a - PASSES8
-                lhsT = (w4[:, i, 2 * P * h : 2 * P * (h + 1)] if e < LATE else w4_late[h][:, i - LATE * PASSES4]).bitcast(FP4X4)
+                lhsT = w4[:, i, 2 * P * h : 2 * P * (h + 1)].bitcast(FP4X4)
                 lhsT_scale = w_planes[:, i, P * h : P * (h + 1)]
             nc.tensor.matmul_mx(
                 out=acc[:, 0:C],
@@ -203,9 +198,14 @@ def tile_moe_tk_lin_silu_kernel(tc, xT, w8_words, w8_scales, w4_words, w4_scales
             nc.sync.dma_start(out=w_planes[W8_ROW + r : P : QUADRANT, 0 : E * PASSES8].bitcast(I32), in_=w8_scale_rows[r:16:4])
         for r in range(4):
             nc.sync.dma_start(out=w_planes[r:P:QUADRANT].bitcast(I32), in_=w4_scale_rows[r:16:4])
-        for r, pos in enumerate((pos1, pos2, pos3, pos4)):
-            (load_w8, load_w4)[r // 2](2 * (r % 2), 2 * (r % 2) + 2)
-            nc.sync.dma_start(pos_sb[r][:], pos)
+        inverse = (pos1, pos2, pos3, pos4)
+        for e in range(*BATCHES[0], 2):
+            load_w8(e, e + 2)
+            for r in (e, e + 1):
+                nc.sync.dma_start(pos_sb[r][:], inverse[r])
+        load_w4(0, 2)
+        nc.sync.dma_start(out=bias[:], in_=b.rearrange("(h p) e -> p h e", p=P))
+        load_w4(2, 4)
 
         turned_gate = bank(0)
         for c in range(CHUNKS):
@@ -231,24 +231,26 @@ def tile_moe_tk_lin_silu_kernel(tc, xT, w8_words, w8_scales, w4_words, w4_scales
         gather_words(1, 0, C, WORD_COLUMN[3] + SPLIT)
         nc.vector.tensor_copy(out=packed[0:FIFTH, 0:T].bitcast(I32), in_=planes[0:FIFTH, 0:T].bitcast(I32))
         gather_words(1, C, 2 * C, WORD_COLUMN[3] + SPLIT)
-        for j in range(0, LATE * C, FEW):
-            gather_planes(j, j + FEW)
-        nc.sync.dma_start(out=bias[:], in_=b.rearrange("(h p) e -> p h e", p=P))
-        load_w8(*BATCHES[1])
-        shift_planes(0, LATE * C)
+        gather_planes(0, FEW)
+        shift_planes(0, FEW)
+        load_w8_half(*BATCHES[1], 0)
         load_w4(*BATCHES[1])
-        load_w8(*BATCHES[2])
+        load_w8_half(*BATCHES[2], 0)
+        for j in range(FEW, S, FEW):
+            gather_planes(j, j + FEW)
+        shift_planes(FEW, S)
         load_w4(*BATCHES[2])
-        load_half(LATE, 0)
-        gather_planes(LATE * C, S)
+        for e0, e1 in BATCHES[3:]:
+            load_w8_half(e0, e1, 0)
+            step = 1 if e1 == E else e1 - e0
+            for e in range(e0, e1, step):
+                load_w4(e, e + step)
+        for e0, e1 in BATCHES[1:]:
+            load_w8_half(e0, e1, 1)
         gather_words(1, 2 * C, FEW, WORD_COLUMN[3] + T)
         gather_words(2, 0, FEW, WORD_COLUMN[3] + T)
         gather_words(3, 0, FEW, WORD_COLUMN[3] + NARROW)
         late_words.append(keep.tile([P, PASSES4 * (S - FEW)], U32, name="late_words", tag="packed", align_bytes=ALIGN))
-        shift_planes(LATE * C, S)
-        for h in range(HALVES):
-            for e in range(LATE + 1 - h, E):
-                load_half(e, h)
 
         opened = 0
         for e0, e1 in BATCHES:
@@ -261,8 +263,9 @@ def tile_moe_tk_lin_silu_kernel(tc, xT, w8_words, w8_scales, w4_words, w4_scales
             accs = {group: bank(opened + i) for i, group in enumerate(groups)}
             opened += len(groups)
             if last:
-                order = (second, first) + ORDER[2:]
-                steps = [(a, group) for a in order for group in groups]
+                order = (0, 1, 4, 2, 3)
+                steps = [(a, group) for a in order[:PASSES8] for group in groups]
+                steps += [(a, group) for group in groups for a in order[PASSES8:]]
             elif e0 == 0:
                 order = range(PASSES)
                 steps = [(a, group) for a in order if a not in SHIFTED for group in groups]
@@ -275,8 +278,9 @@ def tile_moe_tk_lin_silu_kernel(tc, xT, w8_words, w8_scales, w4_words, w4_scales
         late_bank = opened - LATE_BANKS
         for e in range(LATE, E):
             acc = bank(late_bank + (e - LATE) % LATE_BANKS)
-            for a in range(PASSES):
-                multiply(acc, a, e, 1, range(PASSES))
+            order = ORDER[3:] + ORDER[:3]
+            for a in order:
+                multiply(acc, a, e, 1, order)
 
         part = [[keep.tile([P, T], F32, name=f"part{h}_{r}") for r in range(TOP)] for h in range(HALVES)]
         turned = [keep.tile([P, T], F32, name=f"turned{h}") for h in range(HALVES)]

@@ -43,7 +43,9 @@ WORD_COLUMN = (4 * T + GAP, 0, T, 2 * T, 3 * T)
 WORD_COLUMNS = WORD_COLUMN[0] + WIDE
 BATCHES = ((0, 4), (4, 6), (6, 8), (8, 10), (10, 12))
 LATE = 4
-LATE_BANKS = 3
+HALF1_BANK = (2, 3, 4, 5, 6, 7, 4, 5)
+HALF1_BATCHES = ((6, 8), (8, 10), (4, 6), (10, 12))
+LATE_ORDER = (2, 3, 4, 0, 1)
 
 
 def tile_moe_tk_lin_silu_kernel(tc, xT, w8_words, w8_scales, w4_words, w4_scales, b, gate, offs, pos1, pos2, pos3, pos4, out):
@@ -165,7 +167,8 @@ def tile_moe_tk_lin_silu_kernel(tc, xT, w8_words, w8_scales, w4_words, w4_scales
             if a == order[-1]:
                 nc.scalar.activation(y[h][:, cols], acc[:, 0:C], SILU, bias=bias[:, h, e : e + 1])
 
-        load_x(ORDER[0])
+        for t0, t1 in ((0, SPLIT), (SPLIT, T)):
+            nc.sync.dma_start(out=raw[ORDER[0]][:, :, t0:t1], in_=x_rows[ORDER[0]][:, :, t0:t1])
         nc.sync.dma_start(offs_sb[:], offs)
 
         nc.vector.memset(zero[:], 0.0)
@@ -179,9 +182,9 @@ def tile_moe_tk_lin_silu_kernel(tc, xT, w8_words, w8_scales, w4_words, w4_scales
             load_x(a)
 
         first, second = ORDER[:2]
-        for t in range(0, SPLIT, PIECE):
-            nc.vector.tensor_copy(*interleaved(first, t, t + PIECE))
-        nc.scalar.activation(*interleaved(first, SPLIT, T), COPY)
+        nc.vector.tensor_copy(*interleaved(first, 0, PIECE))
+        nc.scalar.activation(*interleaved(first, PIECE, SPLIT), COPY)
+        nc.vector.tensor_copy(*interleaved(first, SPLIT, T))
         quantise(first, [(t, t + PIECE) for t in range(0, T, PIECE)])
         for q in range(4):
             nc.sync.dma_start(
@@ -221,14 +224,13 @@ def tile_moe_tk_lin_silu_kernel(tc, xT, w8_words, w8_scales, w4_words, w4_scales
 
         for j in range(0, S - C, FEW):
             gather_words(first, j, min(j + FEW, S - C), WORD_COLUMN[second])
-        quantise(second)
-        gather_words(first, S - C, S, WORD_COLUMN[second] + SPLIT)
+        quantise(second, [(t, t + PIECE) for t in range(0, T, PIECE)])
+        gather_words(first, S - C, S, WORD_COLUMN[second] + PIECE)
         for j in range(0, S, MANY):
             gather_words(second, j, j + MANY, WORD_COLUMNS)
-        quantise(1)
-        quantise(2)
-        quantise(3)
-        gather_words(1, 0, C, WORD_COLUMN[3] + SPLIT)
+        for a in ORDER[2:]:
+            quantise(a, [(t, t + PIECE) for t in range(0, T, PIECE)])
+        gather_words(1, 0, C, WORD_COLUMN[3] + PIECE)
         nc.vector.tensor_copy(out=packed[0:FIFTH, 0:T].bitcast(I32), in_=planes[0:FIFTH, 0:T].bitcast(I32))
         gather_words(1, C, 2 * C, WORD_COLUMN[3] + SPLIT)
         gather_planes(0, FEW)
@@ -245,12 +247,19 @@ def tile_moe_tk_lin_silu_kernel(tc, xT, w8_words, w8_scales, w4_words, w4_scales
             step = 1 if e1 == E else e1 - e0
             for e in range(e0, e1, step):
                 load_w4(e, e + step)
-        for e0, e1 in BATCHES[1:]:
+        for e0, e1 in HALF1_BATCHES:
             load_w8_half(e0, e1, 1)
         gather_words(1, 2 * C, FEW, WORD_COLUMN[3] + T)
         gather_words(2, 0, FEW, WORD_COLUMN[3] + T)
         gather_words(3, 0, FEW, WORD_COLUMN[3] + NARROW)
         late_words.append(keep.tile([P, PASSES4 * (S - FEW)], U32, name="late_words", tag="packed", align_bytes=ALIGN))
+
+        waiting = {}
+
+        def open_late(e, i):
+            waiting[e] = bank(i)
+            for a in LATE_ORDER[:PASSES4]:
+                multiply(waiting[e], a, e, 1, LATE_ORDER)
 
         opened = 0
         for e0, e1 in BATCHES:
@@ -260,7 +269,7 @@ def tile_moe_tk_lin_silu_kernel(tc, xT, w8_words, w8_scales, w4_words, w4_scales
                 for e in range(e0, e1, step):
                     gather_words(a, e * C, (e + step) * C, WORD_COLUMN[3] + (NARROW if a == 3 else T))
             groups = [(e, h) for h in range(HALVES) for e in range(e0, e1) if h == 0 or e < LATE]
-            accs = {group: bank(opened + i) for i, group in enumerate(groups)}
+            accs = {group: bank(opened % 4 + i) for i, group in enumerate(groups)}
             opened += len(groups)
             if last:
                 order = (0, 1, 4, 2, 3)
@@ -275,12 +284,15 @@ def tile_moe_tk_lin_silu_kernel(tc, xT, w8_words, w8_scales, w4_words, w4_scales
                 steps = [(a, group) for group in groups for a in order]
             for a, (e, h) in steps:
                 multiply(accs[e, h], a, e, h, order)
-        late_bank = opened - LATE_BANKS
-        for e in range(LATE, E):
-            acc = bank(late_bank + (e - LATE) % LATE_BANKS)
-            order = ORDER[3:] + ORDER[:3]
-            for a in order:
-                multiply(acc, a, e, 1, order)
+            if e0 in (6, 8):
+                for e in range(e0, e1):
+                    open_late(e, HALF1_BANK[e - LATE])
+        for e0, e1 in HALF1_BATCHES:
+            for e in range(e0, e1):
+                if e not in waiting:
+                    open_late(e, HALF1_BANK[e - LATE])
+                for a in LATE_ORDER[PASSES4:]:
+                    multiply(waiting[e], a, e, 1, LATE_ORDER)
 
         part = [[keep.tile([P, T], F32, name=f"part{h}_{r}") for r in range(TOP)] for h in range(HALVES)]
         turned = [keep.tile([P, T], F32, name=f"turned{h}") for h in range(HALVES)]
@@ -296,7 +308,7 @@ def tile_moe_tk_lin_silu_kernel(tc, xT, w8_words, w8_scales, w4_words, w4_scales
         for h in range(HALVES):
             for r in range(TOP):
                 nc.vector.tensor_tensor(part[h][r][:], y[h][:].indirect(pos_sb[r][:]), gates[:, r, :], MULT)
-        last_bank = late_bank + (E - 1 - LATE) % LATE_BANKS
+        last_bank = HALF1_BANK[-1]
         four = bank(last_bank)
         for c in range(CHUNKS):
             for r in range(TOP):

@@ -198,17 +198,15 @@ def tile_moe_tk_lin_silu_kernel(tc, xT, w8_words, w8_scales, w4_words, w4_scales
 
         nc.sync.dma_start(out=gate_rows[0:TOP, :], in_=gate[:, 0, :])
         for r in range(4):
-            nc.sync.dma_start(out=w_planes[W8_ROW + r : P : QUADRANT, 0 : E * PASSES8].bitcast(I32), in_=w8_scale_rows[r:16:4])
-        for r in range(4):
             nc.sync.dma_start(out=w_planes[r:P:QUADRANT].bitcast(I32), in_=w4_scale_rows[r:16:4])
-        inverse = (pos1, pos2, pos3, pos4)
-        for e in range(*BATCHES[0], 2):
-            load_w8(e, e + 2)
-            for r in (e, e + 1):
-                nc.sync.dma_start(pos_sb[r][:], inverse[r])
-        load_w4(0, 2)
+        for r in range(4):
+            nc.sync.dma_start(out=w_planes[W8_ROW + r : P : QUADRANT, 0 : E * PASSES8].bitcast(I32), in_=w8_scale_rows[r:16:4])
+        load_w8(0, 2)
         nc.sync.dma_start(out=bias[:], in_=b.rearrange("(h p) e -> p h e", p=P))
+        load_w8(2, 4)
+        load_w4(0, 2)
         load_w4(2, 4)
+        load_w8_half(*BATCHES[1], 0)
 
         turned_gate = bank(0)
         for c in range(CHUNKS):
@@ -235,19 +233,21 @@ def tile_moe_tk_lin_silu_kernel(tc, xT, w8_words, w8_scales, w4_words, w4_scales
         gather_words(1, C, 2 * C, WORD_COLUMN[3] + SPLIT)
         gather_planes(0, FEW)
         shift_planes(0, FEW)
-        load_w8_half(*BATCHES[1], 0)
         load_w4(*BATCHES[1])
         load_w8_half(*BATCHES[2], 0)
+        load_w4(*BATCHES[2])
         for j in range(FEW, S, FEW):
             gather_planes(j, j + FEW)
         shift_planes(FEW, S)
-        load_w4(*BATCHES[2])
         for e0, e1 in BATCHES[3:]:
             load_w8_half(e0, e1, 0)
             step = 1 if e1 == E else e1 - e0
             for e in range(e0, e1, step):
                 load_w4(e, e + step)
-        for e0, e1 in HALF1_BATCHES:
+        inverse = (pos1, pos2, pos3, pos4)
+        for i, (e0, e1) in enumerate(HALF1_BATCHES):
+            for r in range(2 * i, min(2 * i + 2, TOP)):
+                nc.sync.dma_start(pos_sb[r][:], inverse[r])
             load_w8_half(e0, e1, 1)
         gather_words(1, 2 * C, FEW, WORD_COLUMN[3] + T)
         gather_words(2, 0, FEW, WORD_COLUMN[3] + T)
@@ -310,9 +310,10 @@ def tile_moe_tk_lin_silu_kernel(tc, xT, w8_words, w8_scales, w4_words, w4_scales
                 nc.vector.tensor_tensor(part[h][r][:], y[h][:].indirect(pos_sb[r][:]), gates[:, r, :], MULT)
         last_bank = HALF1_BANK[-1]
         four = bank(last_bank)
-        for c in range(CHUNKS):
-            for r in range(TOP):
-                add_turned(four[:, c * P : (c + 1) * P], 0, r, c, TOP)
+        for r in range(TOP):
+            for c in range(CHUNKS):
+                cols = slice(c * P, (c + 1) * P)
+                nc.tensor.matmul(four[:, cols], part[0][r][:, cols], ident[:], start=(r == 0 and c == 0), stop=(r == TOP - 1 and c == CHUNKS - 1), is_transpose=True)
         nc.scalar.copy(turned[0][:], four[:])
         back = bank(last_bank + 1)
         for c in range(CHUNKS):

@@ -34,8 +34,8 @@ PLANE_ROW = (4, 12, 0, 8)
 SHIFTED = (3, 4)
 FIFTH = P - 16
 ORDER = (4, 0, 1, 2, 3)
-SPLIT = 256
 PIECE = 128
+PIECES = [(t, t + PIECE) for t in range(0, T, PIECE)]
 FEW, NARROW = 512, 704
 MANY, WIDE = 768, 1024
 GAP = NARROW - T
@@ -43,9 +43,11 @@ WORD_COLUMN = (4 * T + GAP, 0, T, 2 * T, 3 * T)
 WORD_COLUMNS = WORD_COLUMN[0] + WIDE
 BATCHES = ((0, 4), (4, 6), (6, 8), (8, 10), (10, 12))
 LATE = 4
-HALF1_BANK = (2, 3, 4, 5, 6, 7, 4, 5)
-HALF1_BATCHES = ((6, 8), (8, 10), (4, 6), (10, 12))
-LATE_ORDER = (2, 3, 4, 0, 1)
+HALF0_BANKS = 4
+HALF1_ORDER = (2, 3, 4, 0, 1)
+AHEAD = BATCHES[2:4]
+HALF1_BATCHES = AHEAD + (BATCHES[1], BATCHES[4])
+HALF1_BANK = {4: 2, 5: 3, 6: 4, 7: 5, 8: 6, 9: 7, 10: 4, 11: 5}
 
 
 def tile_moe_tk_lin_silu_kernel(tc, xT, w8_words, w8_scales, w4_words, w4_scales, b, gate, offs, pos1, pos2, pos3, pos4, out):
@@ -78,7 +80,6 @@ def tile_moe_tk_lin_silu_kernel(tc, xT, w8_words, w8_scales, w4_words, w4_scales
         gate_cols = keep.tile([P, CHUNKS, TOP], F32, name="gate_cols")
         ident = keep.tile([P, P], F32, name="ident")
         zero = keep.tile([P, 1], F32, name="zero")
-        late_words = []
 
         x_rows = xT.rearrange("(a p j) t -> a p j t", p=P, j=4)
         w8_rows = w8_words.rearrange("e a p n r -> p (e a) (n r)").bitcast(I32)
@@ -106,9 +107,9 @@ def tile_moe_tk_lin_silu_kernel(tc, xT, w8_words, w8_scales, w4_words, w4_scales
         def bank(i):
             return psum.tile([P, T], F32, name=f"bank{i % BANKS}")
 
-        def quantise(a, cuts=((0, SPLIT), (SPLIT, T))):
+        def quantise(a):
             column, row = (T, 0) if a == ORDER[0] else (0, PLANE_ROW[a])
-            for t0, t1 in cuts:
+            for t0, t1 in PIECES:
                 nc.vector.quantize_mx(
                     out=words[:, WORD_COLUMN[a] + t0 : WORD_COLUMN[a] + t1].bitcast(FP8X4),
                     scales=planes[row:P, column + t0 : column + t1],
@@ -124,7 +125,7 @@ def tile_moe_tk_lin_silu_kernel(tc, xT, w8_words, w8_scales, w4_words, w4_scales
         def slots(a, j0, j1):
             if a in ORDER[2:] and j0 >= FEW:
                 column = (a - 1) * (S - FEW) - FEW
-                return late_words[0][:, column + j0 : column + j1]
+                return late_words[:, column + j0 : column + j1]
             return slot_words[a][:, j0:j1]
 
         def gather_words(a, j0, j1, end):
@@ -167,8 +168,9 @@ def tile_moe_tk_lin_silu_kernel(tc, xT, w8_words, w8_scales, w4_words, w4_scales
             if a == order[-1]:
                 nc.scalar.activation(y[h][:, cols], acc[:, 0:C], SILU, bias=bias[:, h, e : e + 1])
 
-        for t0, t1 in ((0, SPLIT), (SPLIT, T)):
-            nc.sync.dma_start(out=raw[ORDER[0]][:, :, t0:t1], in_=x_rows[ORDER[0]][:, :, t0:t1])
+        first, second = ORDER[:2]
+        for t0, t1 in ((0, 2 * PIECE), (2 * PIECE, T)):
+            nc.sync.dma_start(out=raw[first][:, :, t0:t1], in_=x_rows[first][:, :, t0:t1])
         nc.sync.dma_start(offs_sb[:], offs)
 
         nc.vector.memset(zero[:], 0.0)
@@ -181,11 +183,10 @@ def tile_moe_tk_lin_silu_kernel(tc, xT, w8_words, w8_scales, w4_words, w4_scales
         for a in ORDER[1:]:
             load_x(a)
 
-        first, second = ORDER[:2]
-        nc.vector.tensor_copy(*interleaved(first, 0, PIECE))
-        nc.scalar.activation(*interleaved(first, PIECE, SPLIT), COPY)
-        nc.vector.tensor_copy(*interleaved(first, SPLIT, T))
-        quantise(first, [(t, t + PIECE) for t in range(0, T, PIECE)])
+        nc.vector.tensor_copy(*interleaved(first, *PIECES[0]))
+        nc.scalar.activation(*interleaved(first, *PIECES[1]), COPY)
+        nc.vector.tensor_copy(*interleaved(first, *PIECES[2]))
+        quantise(first)
         for q in range(4):
             nc.sync.dma_start(
                 out=packed[FIFTH + 4 * q : FIFTH + 4 * q + 4, 0:T].bitcast(I32),
@@ -222,15 +223,18 @@ def tile_moe_tk_lin_silu_kernel(tc, xT, w8_words, w8_scales, w4_words, w4_scales
 
         for j in range(0, S - C, FEW):
             gather_words(first, j, min(j + FEW, S - C), WORD_COLUMN[second])
-        quantise(second, [(t, t + PIECE) for t in range(0, T, PIECE)])
+        quantise(second)
         gather_words(first, S - C, S, WORD_COLUMN[second] + PIECE)
         for j in range(0, S, MANY):
             gather_words(second, j, j + MANY, WORD_COLUMNS)
-        for a in ORDER[2:]:
-            quantise(a, [(t, t + PIECE) for t in range(0, T, PIECE)])
+        quantise(1)
+        quantise(2)
+        gather_words(1, 2 * C, FEW, WORD_COLUMN[2] + PIECE)
+        quantise(3)
+
         gather_words(1, 0, C, WORD_COLUMN[3] + PIECE)
         nc.vector.tensor_copy(out=packed[0:FIFTH, 0:T].bitcast(I32), in_=planes[0:FIFTH, 0:T].bitcast(I32))
-        gather_words(1, C, 2 * C, WORD_COLUMN[3] + SPLIT)
+        gather_words(1, C, 2 * C, WORD_COLUMN[3] + 2 * PIECE)
         gather_planes(0, FEW)
         shift_planes(0, FEW)
         load_w4(*BATCHES[1])
@@ -249,27 +253,27 @@ def tile_moe_tk_lin_silu_kernel(tc, xT, w8_words, w8_scales, w4_words, w4_scales
             for r in range(2 * i, min(2 * i + 2, TOP)):
                 nc.sync.dma_start(pos_sb[r][:], inverse[r])
             load_w8_half(e0, e1, 1)
-        gather_words(1, 2 * C, FEW, WORD_COLUMN[3] + T)
         gather_words(2, 0, FEW, WORD_COLUMN[3] + T)
         gather_words(3, 0, FEW, WORD_COLUMN[3] + NARROW)
-        late_words.append(keep.tile([P, PASSES4 * (S - FEW)], U32, name="late_words", tag="packed", align_bytes=ALIGN))
+        late_words = keep.tile([P, len(ORDER[2:]) * (S - FEW)], U32, name="late_words", tag="packed", align_bytes=ALIGN)
 
         waiting = {}
 
-        def open_late(e, i):
-            waiting[e] = bank(i)
-            for a in LATE_ORDER[:PASSES4]:
-                multiply(waiting[e], a, e, 1, LATE_ORDER)
+        def open_half1(e):
+            waiting[e] = bank(HALF1_BANK[e])
+            for a in HALF1_ORDER[:PASSES4]:
+                multiply(waiting[e], a, e, 1, HALF1_ORDER)
 
         opened = 0
         for e0, e1 in BATCHES:
             last = e1 == E
-            for a in ORDER[2:] if e0 > 0 else ():
-                step = 1 if last and a == ORDER[-1] else e1 - e0
-                for e in range(e0, e1, step):
-                    gather_words(a, e * C, (e + step) * C, WORD_COLUMN[3] + (NARROW if a == 3 else T))
+            if e0 > 0:
+                for a in ORDER[2:]:
+                    step = 1 if last and a == ORDER[-1] else e1 - e0
+                    for e in range(e0, e1, step):
+                        gather_words(a, e * C, (e + step) * C, WORD_COLUMN[3] + (NARROW if a == 3 else T))
             groups = [(e, h) for h in range(HALVES) for e in range(e0, e1) if h == 0 or e < LATE]
-            accs = {group: bank(opened % 4 + i) for i, group in enumerate(groups)}
+            accs = {group: bank(opened % HALF0_BANKS + i) for i, group in enumerate(groups)}
             opened += len(groups)
             if last:
                 order = (0, 1, 4, 2, 3)
@@ -284,23 +288,23 @@ def tile_moe_tk_lin_silu_kernel(tc, xT, w8_words, w8_scales, w4_words, w4_scales
                 steps = [(a, group) for group in groups for a in order]
             for a, (e, h) in steps:
                 multiply(accs[e, h], a, e, h, order)
-            if e0 in (6, 8):
+            if (e0, e1) in AHEAD:
                 for e in range(e0, e1):
-                    open_late(e, HALF1_BANK[e - LATE])
+                    open_half1(e)
         for e0, e1 in HALF1_BATCHES:
             for e in range(e0, e1):
                 if e not in waiting:
-                    open_late(e, HALF1_BANK[e - LATE])
-                for a in LATE_ORDER[PASSES4:]:
-                    multiply(waiting[e], a, e, 1, LATE_ORDER)
+                    open_half1(e)
+                for a in HALF1_ORDER[PASSES4:]:
+                    multiply(waiting[e], a, e, 1, HALF1_ORDER)
 
         part = [[keep.tile([P, T], F32, name=f"part{h}_{r}") for r in range(TOP)] for h in range(HALVES)]
         turned = [keep.tile([P, T], F32, name=f"turned{h}") for h in range(HALVES)]
         three = keep.tile([P, T], F32, name="three")
         total = [keep.tile([P, T], F32, name=f"total{h}", align_bytes=ALIGN) for h in range(HALVES)]
 
-        def add_turned(acc, h, r, c, count):
-            nc.tensor.matmul(acc, part[h][r][:, c * P : (c + 1) * P], ident[:], start=(r == 0), stop=(r == count - 1), is_transpose=True)
+        def add_turned(acc, h, r, c, start, stop):
+            nc.tensor.matmul(acc, part[h][r][:, c * P : (c + 1) * P], ident[:], start=start, stop=stop, is_transpose=True)
 
         def turn_back(back, h, c):
             nc.tensor.transpose(back[:, c * P : (c + 1) * P], turned[h][:, c * P : (c + 1) * P], ident[:])
@@ -308,12 +312,11 @@ def tile_moe_tk_lin_silu_kernel(tc, xT, w8_words, w8_scales, w4_words, w4_scales
         for h in range(HALVES):
             for r in range(TOP):
                 nc.vector.tensor_tensor(part[h][r][:], y[h][:].indirect(pos_sb[r][:]), gates[:, r, :], MULT)
-        last_bank = HALF1_BANK[-1]
+        last_bank = HALF1_BANK[E - 1]
         four = bank(last_bank)
         for r in range(TOP):
             for c in range(CHUNKS):
-                cols = slice(c * P, (c + 1) * P)
-                nc.tensor.matmul(four[:, cols], part[0][r][:, cols], ident[:], start=(r == 0 and c == 0), stop=(r == TOP - 1 and c == CHUNKS - 1), is_transpose=True)
+                add_turned(four[:, c * P : (c + 1) * P], 0, r, c, r == 0 and c == 0, r == TOP - 1 and c == CHUNKS - 1)
         nc.scalar.copy(turned[0][:], four[:])
         back = bank(last_bank + 1)
         for c in range(CHUNKS):
@@ -323,7 +326,7 @@ def tile_moe_tk_lin_silu_kernel(tc, xT, w8_words, w8_scales, w4_words, w4_scales
         sums = [bank(last_bank + 2 + c) for c in range(CHUNKS)]
         for r in range(2):
             for c in range(CHUNKS):
-                add_turned(sums[c][:, 0:P], 1, r, c, 2)
+                add_turned(sums[c][:, 0:P], 1, r, c, r == 0, r == 1)
         two = bank(last_bank + 2 + CHUNKS)
         for c in range(CHUNKS):
             nc.scalar.copy(turned[1][:, c * P : (c + 1) * P], sums[c][:, 0:P])

@@ -48,6 +48,7 @@ HALF1_ORDER = (2, 3, 4, 0, 1)
 AHEAD = BATCHES[2:4]
 HALF1_BATCHES = AHEAD + (BATCHES[1], BATCHES[4])
 HALF1_BANK = {4: 2, 5: 3, 6: 4, 7: 5, 8: 6, 9: 7, 10: 4, 11: 5}
+ON_SCALAR = ((0, 3), (1, 2), (1, 3))
 
 
 def tile_moe_tk_lin_silu_kernel(tc, xT, w8_words, w8_scales, w4_words, w4_scales, b, gate, offs, pos1, pos2, pos3, pos4, out):
@@ -309,9 +310,17 @@ def tile_moe_tk_lin_silu_kernel(tc, xT, w8_words, w8_scales, w4_words, w4_scales
         def turn_back(back, h, c):
             nc.tensor.transpose(back[:, c * P : (c + 1) * P], turned[h][:, c * P : (c + 1) * P], ident[:])
 
+        plain = {(h, r): keep.tile([P, T], F32, name=f"plain{h}_{r}") for h, r in ON_SCALAR}
+        runs = [slice(t0, t0 + T // 2) for t0 in (0, T // 2)]
+        for h, r in ON_SCALAR:
+            nc.scalar.activation(plain[h, r][:], y[h][:].indirect(pos_sb[r][:]), COPY)
         for h in range(HALVES):
             for r in range(TOP):
-                nc.vector.tensor_tensor(part[h][r][:], y[h][:].indirect(pos_sb[r][:]), gates[:, r, :], MULT)
+                if (h, r) in ON_SCALAR:
+                    for run in runs if (h, r) == ON_SCALAR[-1] else [slice(0, T)]:
+                        nc.vector.tensor_tensor(part[h][r][:, run], plain[h, r][:, run], gates[:, r, run], MULT)
+                else:
+                    nc.vector.tensor_tensor(part[h][r][:], y[h][:].indirect(pos_sb[r][:]), gates[:, r, :], MULT)
         last_bank = HALF1_BANK[E - 1]
         four = bank(last_bank)
         for r in range(TOP):
@@ -331,9 +340,8 @@ def tile_moe_tk_lin_silu_kernel(tc, xT, w8_words, w8_scales, w4_words, w4_scales
         for c in range(CHUNKS):
             nc.scalar.copy(turned[1][:, c * P : (c + 1) * P], sums[c][:, 0:P])
             turn_back(two, 1, c)
-        runs = [slice(t0, t0 + T // 2) for t0 in (0, T // 2)]
         for run in runs:
-            nc.vector.tensor_tensor(three[:, run], part[1][2][:, run], two[:, run], ADD)
+            nc.vector.tensor_tensor(three[:, run], part[1][2][:, run], part[1][3][:, run], ADD)
         for run in runs:
-            nc.vector.tensor_tensor(total[1][:, run], three[:, run], part[1][3][:, run], ADD)
+            nc.vector.tensor_tensor(total[1][:, run], three[:, run], two[:, run], ADD)
             nc.sync.dma_start(out=out[P:N, run], in_=total[1][:, run])

@@ -152,7 +152,7 @@ def tile_moe_tk_lin_silu_kernel(tc, xT, w8_words, w8_scales, w4_words, w4_scales
             if a < PASSES8:
                 i = e * PASSES8 + a
                 lhsT = (w8[:, i, 4 * P * h : 4 * P * (h + 1)] if e < LATE else w8_late[h][:, i - LATE * PASSES8]).bitcast(FP8X4)
-                lhsT_scale = w_planes[W8_ROW:P, i, P * h : P * (h + 1)]
+                lhsT_scale = w8_planes[W8_ROW:P, i, P * h : P * (h + 1)]
             else:
                 i = e * PASSES4 + a - PASSES8
                 lhsT = w4[:, i, 2 * P * h : 2 * P * (h + 1)].bitcast(FP4X4)
@@ -181,7 +181,7 @@ def tile_moe_tk_lin_silu_kernel(tc, xT, w8_words, w8_scales, w4_words, w4_scales
         nc.vector.memset(words[:, 4 * T : 4 * T + GAP], 0)
         nc.vector.memset(words[:, WORD_COLUMN[0] + T :], 0)
         make_identity(nc, ident[:])
-        for a in ORDER[1:]:
+        for a in ORDER[1:-1]:
             load_x(a)
 
         nc.vector.tensor_copy(*interleaved(first, *PIECES[0]))
@@ -193,6 +193,7 @@ def tile_moe_tk_lin_silu_kernel(tc, xT, w8_words, w8_scales, w4_words, w4_scales
                 out=packed[FIFTH + 4 * q : FIFTH + 4 * q + 4, 0:T].bitcast(I32),
                 in_=planes[QUADRANT * q : QUADRANT * q + 4, T : 2 * T].bitcast(I32),
             )
+        load_x(ORDER[-1])
 
         for a in ORDER[1:]:
             nc.scalar.activation(*interleaved(a, 0, T), COPY)
@@ -201,8 +202,9 @@ def tile_moe_tk_lin_silu_kernel(tc, xT, w8_words, w8_scales, w4_words, w4_scales
         nc.sync.dma_start(out=gate_rows[0:TOP, :], in_=gate[:, 0, :])
         for r in range(4):
             nc.sync.dma_start(out=w_planes[r:P:QUADRANT].bitcast(I32), in_=w4_scale_rows[r:16:4])
+        w8_planes = keep.tile([P, E * PASSES8, N], U8, name="w8_planes", tag="raw1", align_bytes=ALIGN)
         for r in range(4):
-            nc.sync.dma_start(out=w_planes[W8_ROW + r : P : QUADRANT, 0 : E * PASSES8].bitcast(I32), in_=w8_scale_rows[r:16:4])
+            nc.scalar.dma_start(out=w8_planes[W8_ROW + r : P : QUADRANT].bitcast(I32), in_=w8_scale_rows[r:16:4])
         load_w8(0, 2)
         nc.sync.dma_start(out=bias[:], in_=b.rearrange("(h p) e -> p h e", p=P))
         load_w8(2, 4)

@@ -36,11 +36,12 @@ FIFTH = P - 16
 ORDER = (4, 0, 1, 2, 3)
 PIECE = 128
 PIECES = [(t, t + PIECE) for t in range(0, T, PIECE)]
+TWO_PIECES = [(0, PIECE), (PIECE, T)]
 FEW, NARROW = 512, 704
-MANY, WIDE = 768, 1024
-GAP = NARROW - T
-WORD_COLUMN = (4 * T + GAP, 0, T, 2 * T, 3 * T)
-WORD_COLUMNS = WORD_COLUMN[0] + WIDE
+PACKED = 1376
+MANY, WIDE = 10 * C, 1712
+WORD_COLUMN = (WIDE, WIDE + NARROW, WIDE + NARROW + T, WIDE + NARROW + 2 * T, 0)
+WORD_COLUMNS = WORD_COLUMN[3] + NARROW
 BATCHES = ((0, 4), (4, 6), (6, 8), (8, 10), (10, 12))
 LATE = 4
 HALF0_BANKS = 4
@@ -63,7 +64,7 @@ def tile_moe_tk_lin_silu_kernel(tc, xT, w8_words, w8_scales, w4_words, w4_scales
 
         words = keep.tile([P, WORD_COLUMNS], I32, name="words", align_bytes=ALIGN)
         planes = keep.tile([P, 2 * T], U8, name="planes", align_bytes=ALIGN)
-        packed = keep.tile([P, NARROW], U8, name="packed", align_bytes=ALIGN)
+        packed = keep.tile([P, PACKED], U8, name="packed", align_bytes=ALIGN)
         w8 = keep.tile([P, LATE * PASSES8, 4 * N], U8, name="w8", align_bytes=ALIGN)
         w4 = keep.tile([P, E * PASSES4, 2 * N], U8, name="w4", align_bytes=ALIGN)
         w8_late = [keep.tile([P, (E - LATE) * PASSES8, 4 * P], U8, name=f"w8_late{h}", align_bytes=ALIGN) for h in range(HALVES)]
@@ -110,7 +111,7 @@ def tile_moe_tk_lin_silu_kernel(tc, xT, w8_words, w8_scales, w4_words, w4_scales
 
         def quantise(a):
             column, row = (T, 0) if a == ORDER[0] else (0, PLANE_ROW[a])
-            for t0, t1 in PIECES:
+            for t0, t1 in PIECES if a == ORDER[0] else TWO_PIECES:
                 nc.vector.quantize_mx(
                     out=words[:, WORD_COLUMN[a] + t0 : WORD_COLUMN[a] + t1].bitcast(FP8X4),
                     scales=planes[row:P, column + t0 : column + t1],
@@ -135,8 +136,8 @@ def tile_moe_tk_lin_silu_kernel(tc, xT, w8_words, w8_scales, w4_words, w4_scales
                 in_=words[:, WORD_COLUMN[a] : end].bitcast(U32).indirect(offs_sb[:, j0 // 16 : j1 // 16]),
             )
 
-        def gather_planes(j0, j1):
-            nc.vector.tensor_copy(out=slot_planes[:, j0:j1], in_=packed[:].indirect(offs_sb[:, j0 // 16 : j1 // 16]))
+        def gather_planes(j0, j1, end):
+            nc.vector.tensor_copy(out=slot_planes[:, j0:j1], in_=packed[:, 0:end].indirect(offs_sb[:, j0 // 16 : j1 // 16]))
 
         def shift_planes(j0, j1):
             row = PLANE_ROW[3]
@@ -178,8 +179,8 @@ def tile_moe_tk_lin_silu_kernel(tc, xT, w8_words, w8_scales, w4_words, w4_scales
         nc.scalar.activation(gate_rows[:], zero[:].to_broadcast([P, T]), SILU)
         nc.vector.memset(planes[:].bitcast(I32), 0)
         nc.vector.memset(packed[:, T:].bitcast(I32), 0)
-        nc.vector.memset(words[:, 4 * T : 4 * T + GAP], 0)
-        nc.vector.memset(words[:, WORD_COLUMN[0] + T :], 0)
+        for a, end in ((4, WORD_COLUMN[0]), (0, WORD_COLUMN[1]), (3, WORD_COLUMNS)):
+            nc.vector.memset(words[:, WORD_COLUMN[a] + T : end], 0)
         make_identity(nc, ident[:])
         for a in ORDER[1:-1]:
             load_x(a)
@@ -224,27 +225,25 @@ def tile_moe_tk_lin_silu_kernel(tc, xT, w8_words, w8_scales, w4_words, w4_scales
 
         shifted = {a: keep.tile([P, S], U8, name=f"shifted{a}", tag=f"raw{a - 1}", align_bytes=ALIGN) for a in SHIFTED}
 
-        for j in range(0, S - C, FEW):
-            gather_words(first, j, min(j + FEW, S - C), WORD_COLUMN[second])
+        gather_words(first, 0, MANY, WORD_COLUMN[second])
         quantise(second)
-        gather_words(first, S - C, S, WORD_COLUMN[second] + PIECE)
-        for j in range(0, S, MANY):
-            gather_words(second, j, j + MANY, WORD_COLUMNS)
+        gather_words(first, MANY, S, WORD_COLUMN[second] + PIECE)
+        gather_words(second, 0, FEW, WORD_COLUMN[1])
         quantise(1)
+        gather_words(second, FEW, 2 * FEW, WORD_COLUMN[1] + PIECE)
         quantise(2)
-        gather_words(1, 2 * C, FEW, WORD_COLUMN[2] + PIECE)
+        gather_words(second, 2 * FEW, S, WORD_COLUMN[2] + PIECE)
         quantise(3)
 
-        gather_words(1, 0, C, WORD_COLUMN[3] + PIECE)
+        gather_words(1, 0, FEW // 2, WORD_COLUMN[3] + PIECE)
         nc.vector.tensor_copy(out=packed[0:FIFTH, 0:T].bitcast(I32), in_=planes[0:FIFTH, 0:T].bitcast(I32))
-        gather_words(1, C, 2 * C, WORD_COLUMN[3] + 2 * PIECE)
-        gather_planes(0, FEW)
+        gather_words(1, FEW // 2, FEW, WORD_COLUMN[3] + T)
+        gather_planes(0, FEW, NARROW)
         shift_planes(0, FEW)
         load_w4(*BATCHES[1])
         load_w8_half(*BATCHES[2], 0)
         load_w4(*BATCHES[2])
-        for j in range(FEW, S, FEW):
-            gather_planes(j, j + FEW)
+        gather_planes(FEW, S, PACKED)
         shift_planes(FEW, S)
         for e0, e1 in BATCHES[3:]:
             load_w8_half(e0, e1, 0)
@@ -257,7 +256,7 @@ def tile_moe_tk_lin_silu_kernel(tc, xT, w8_words, w8_scales, w4_words, w4_scales
                 nc.sync.dma_start(pos_sb[r][:], inverse[r])
             load_w8_half(e0, e1, 1)
         gather_words(2, 0, FEW, WORD_COLUMN[3] + T)
-        gather_words(3, 0, FEW, WORD_COLUMN[3] + NARROW)
+        gather_words(3, 0, FEW, WORD_COLUMNS)
         late_words = keep.tile([P, len(ORDER[2:]) * (S - FEW)], U32, name="late_words", tag="packed", align_bytes=ALIGN)
 
         waiting = {}
@@ -274,7 +273,7 @@ def tile_moe_tk_lin_silu_kernel(tc, xT, w8_words, w8_scales, w4_words, w4_scales
                 for a in ORDER[2:]:
                     step = 1 if last and a == ORDER[-1] else e1 - e0
                     for e in range(e0, e1, step):
-                        gather_words(a, e * C, (e + step) * C, WORD_COLUMN[3] + (NARROW if a == 3 else T))
+                        gather_words(a, e * C, (e + step) * C, WORD_COLUMN[a] + NARROW)
             groups = [(e, h) for h in range(HALVES) for e in range(e0, e1) if h == 0 or e < LATE]
             accs = {group: bank(opened % HALF0_BANKS + i) for i, group in enumerate(groups)}
             opened += len(groups)

@@ -43,13 +43,13 @@ MANY, WIDE = 10 * C, 1712
 WORD_COLUMN = (WIDE, WIDE + NARROW, WIDE + NARROW + T, WIDE + NARROW + 2 * T, 0)
 WORD_COLUMNS = WORD_COLUMN[3] + NARROW
 BATCHES = ((0, 4), (4, 6), (6, 8), (8, 10), (10, 12))
-LATE = 4
-HALF0_BANKS = 4
-HALF1_ORDER = (2, 3, 4, 0, 1)
-AHEAD = BATCHES[2:4]
-HALF1_BATCHES = AHEAD + (BATCHES[1], BATCHES[4])
-HALF1_BANK = {4: 2, 5: 3, 6: 4, 7: 5, 8: 6, 9: 7, 10: 4, 11: 5}
-ON_SCALAR = ((0, 3), (1, 2), (1, 3))
+LATE = 8
+FIRST_BANK = (0, 0, 4, 0, 4)
+HALF1_ORDER = (3, 2, 4, 0, 1)
+AHEAD = BATCHES[3:4]
+HALF1_BATCHES = BATCHES[3:]
+HALF1_BANK = {8: 2, 9: 3, 10: 6, 11: 7}
+ON_SCALAR = ((0, 2), (0, 3), (1, 2), (1, 3))
 
 
 def tile_moe_tk_lin_silu_kernel(tc, xT, w8_words, w8_scales, w4_words, w4_scales, b, gate, offs, pos1, pos2, pos3, pos4, out):
@@ -67,7 +67,11 @@ def tile_moe_tk_lin_silu_kernel(tc, xT, w8_words, w8_scales, w4_words, w4_scales
         packed = keep.tile([P, PACKED], U8, name="packed", align_bytes=ALIGN)
         w8 = keep.tile([P, LATE * PASSES8, 4 * N], U8, name="w8", align_bytes=ALIGN)
         w4 = keep.tile([P, E * PASSES4, 2 * N], U8, name="w4", align_bytes=ALIGN)
-        w8_late = [keep.tile([P, (E - LATE) * PASSES8, 4 * P], U8, name=f"w8_late{h}", align_bytes=ALIGN) for h in range(HALVES)]
+        w8_late = {
+            (e0, h): keep.tile([P, (e1 - e0) * PASSES8, 4 * P], U8, name=f"w8_late{e0}_{h}", align_bytes=ALIGN)
+            for e0, e1 in HALF1_BATCHES
+            for h in range(HALVES)
+        }
         bias = keep.tile([P, HALVES, E], F32, name="bias")
         gates = keep.tile([P, TOP, T], F32, name="gates")
         early = keep.tile([P, 2, 4, T], F32, name="early", align_bytes=ALIGN)
@@ -102,7 +106,7 @@ def tile_moe_tk_lin_silu_kernel(tc, xT, w8_words, w8_scales, w4_words, w4_scales
 
         def load_w8_half(e0, e1, h):
             nc.sync.dma_start(
-                out=w8_late[h][:, (e0 - LATE) * PASSES8 : (e1 - LATE) * PASSES8].bitcast(I32),
+                out=w8_late[e0 - e0 % 2, h][:, e0 % 2 * PASSES8 : (e0 % 2 + e1 - e0) * PASSES8].bitcast(I32),
                 in_=w8_rows[:, e0 * PASSES8 : e1 * PASSES8, h * P : (h + 1) * P],
             )
 
@@ -148,27 +152,28 @@ def tile_moe_tk_lin_silu_kernel(tc, xT, w8_words, w8_scales, w4_words, w4_scales
                     in_=slot_planes[FIFTH + 4 * q : FIFTH + 4 * q + 4, j0:j1].bitcast(I32),
                 )
 
-        def multiply(acc, a, e, h, order):
+        def multiply(acc, a, e, h, start, stop):
             cols = slice(e * C, (e + 1) * C)
             if a < PASSES8:
                 i = e * PASSES8 + a
-                lhsT = (w8[:, i, 4 * P * h : 4 * P * (h + 1)] if e < LATE else w8_late[h][:, i - LATE * PASSES8]).bitcast(FP8X4)
+                lhsT = (w8[:, i, 4 * P * h : 4 * P * (h + 1)] if e < LATE else w8_late[e - e % 2, h][:, e % 2 * PASSES8 + a]).bitcast(FP8X4)
                 lhsT_scale = w8_planes[W8_ROW:P, i, P * h : P * (h + 1)]
             else:
                 i = e * PASSES4 + a - PASSES8
                 lhsT = w4[:, i, 2 * P * h : 2 * P * (h + 1)].bitcast(FP4X4)
                 lhsT_scale = w_planes[:, i, P * h : P * (h + 1)]
             nc.tensor.matmul_mx(
-                out=acc[:, 0:C],
+                out=acc,
                 lhsT=lhsT,
                 lhsT_scale=lhsT_scale,
                 rhs=slots(a, e * C, (e + 1) * C).bitcast(FP8X4),
                 rhs_scale=shifted[a][:, cols] if a in SHIFTED else slot_planes[PLANE_ROW[a] : P, cols],
-                start=(a == order[0]),
-                stop=(a == order[-1]),
+                start=start,
+                stop=stop,
             )
-            if a == order[-1]:
-                nc.scalar.activation(y[h][:, cols], acc[:, 0:C], SILU, bias=bias[:, h, e : e + 1])
+
+        def silu(acc, e, h):
+            nc.scalar.activation(y[h][:, e * C : (e + 1) * C], acc, SILU, bias=bias[:, h, e : e + 1])
 
         first, second = ORDER[:2]
         for t0, t1 in ((0, 2 * PIECE), (2 * PIECE, T)):
@@ -187,7 +192,8 @@ def tile_moe_tk_lin_silu_kernel(tc, xT, w8_words, w8_scales, w4_words, w4_scales
 
         nc.vector.tensor_copy(*interleaved(first, *PIECES[0]))
         nc.scalar.activation(*interleaved(first, *PIECES[1]), COPY)
-        nc.vector.tensor_copy(*interleaved(first, *PIECES[2]))
+        nc.vector.tensor_copy(*interleaved(first, 2 * PIECE, T - PIECE // 2))
+        nc.scalar.activation(*interleaved(first, T - PIECE // 2, T), COPY)
         quantise(first)
         for q in range(4):
             nc.sync.dma_start(
@@ -211,7 +217,7 @@ def tile_moe_tk_lin_silu_kernel(tc, xT, w8_words, w8_scales, w4_words, w4_scales
         load_w8(2, 4)
         load_w4(0, 2)
         load_w4(2, 4)
-        load_w8_half(*BATCHES[1], 0)
+        load_w8(*BATCHES[1])
 
         turned_gate = bank(0)
         for c in range(CHUNKS):
@@ -241,7 +247,7 @@ def tile_moe_tk_lin_silu_kernel(tc, xT, w8_words, w8_scales, w4_words, w4_scales
         gather_planes(0, FEW, NARROW)
         shift_planes(0, FEW)
         load_w4(*BATCHES[1])
-        load_w8_half(*BATCHES[2], 0)
+        load_w8(*BATCHES[2])
         load_w4(*BATCHES[2])
         gather_planes(FEW, S, PACKED)
         shift_planes(FEW, S)
@@ -254,7 +260,9 @@ def tile_moe_tk_lin_silu_kernel(tc, xT, w8_words, w8_scales, w4_words, w4_scales
         for i, (e0, e1) in enumerate(HALF1_BATCHES):
             for r in range(2 * i, min(2 * i + 2, TOP)):
                 nc.sync.dma_start(pos_sb[r][:], inverse[r])
-            load_w8_half(e0, e1, 1)
+            step = 1 if e1 == E else e1 - e0
+            for e in range(e0, e1, step):
+                load_w8_half(e, e + step, 1)
         gather_words(2, 0, FEW, WORD_COLUMN[3] + T)
         gather_words(3, 0, FEW, WORD_COLUMNS)
         late_words = keep.tile([P, len(ORDER[2:]) * (S - FEW)], U32, name="late_words", tag="packed", align_bytes=ALIGN)
@@ -262,12 +270,11 @@ def tile_moe_tk_lin_silu_kernel(tc, xT, w8_words, w8_scales, w4_words, w4_scales
         waiting = {}
 
         def open_half1(e):
-            waiting[e] = bank(HALF1_BANK[e])
+            waiting[e] = bank(HALF1_BANK[e])[:, 0:C]
             for a in HALF1_ORDER[:PASSES4]:
-                multiply(waiting[e], a, e, 1, HALF1_ORDER)
+                multiply(waiting[e], a, e, 1, a == HALF1_ORDER[0], False)
 
-        opened = 0
-        for e0, e1 in BATCHES:
+        for (e0, e1), first_bank in zip(BATCHES, FIRST_BANK):
             last = e1 == E
             if e0 > 0:
                 for a in ORDER[2:]:
@@ -275,8 +282,7 @@ def tile_moe_tk_lin_silu_kernel(tc, xT, w8_words, w8_scales, w4_words, w4_scales
                     for e in range(e0, e1, step):
                         gather_words(a, e * C, (e + step) * C, WORD_COLUMN[a] + NARROW)
             groups = [(e, h) for h in range(HALVES) for e in range(e0, e1) if h == 0 or e < LATE]
-            accs = {group: bank(opened % HALF0_BANKS + i) for i, group in enumerate(groups)}
-            opened += len(groups)
+            accs = {group: bank(first_bank + i)[:, 0:C] for i, group in enumerate(groups)}
             if last:
                 order = (0, 1, 4, 2, 3)
                 steps = [(a, group) for a in order[:PASSES8] for group in groups]
@@ -289,16 +295,24 @@ def tile_moe_tk_lin_silu_kernel(tc, xT, w8_words, w8_scales, w4_words, w4_scales
                 order = range(PASSES)
                 steps = [(a, group) for group in groups for a in order]
             for a, (e, h) in steps:
-                multiply(accs[e, h], a, e, h, order)
+                multiply(accs[e, h], a, e, h, a == order[0], a == order[-1])
+                if a == order[-1]:
+                    silu(accs[e, h], e, h)
             if (e0, e1) in AHEAD:
                 for e in range(e0, e1):
                     open_half1(e)
-        for e0, e1 in HALF1_BATCHES:
-            for e in range(e0, e1):
-                if e not in waiting:
-                    open_half1(e)
-                for a in HALF1_ORDER[PASSES4:]:
-                    multiply(waiting[e], a, e, 1, HALF1_ORDER)
+        shared = bank(HALF1_BANK[E - 1])
+        for i, e in enumerate((E - 1, E - 2)):
+            waiting[e] = shared[:, i * C : (i + 1) * C]
+            for a in HALF1_ORDER[:PASSES4]:
+                multiply(waiting[e], a, e, 1, i == 0 and a == HALF1_ORDER[0], False)
+        for e in range(LATE, E):
+            for a in HALF1_ORDER[PASSES4:]:
+                multiply(waiting[e], a, e, 1, False, a == HALF1_ORDER[-1] and e != E - 2)
+            if e < E - 2:
+                silu(waiting[e], e, 1)
+        for e in (E - 2, E - 1):
+            silu(waiting[e], e, 1)
 
         part = [[keep.tile([P, T], F32, name=f"part{h}_{r}") for r in range(TOP)] for h in range(HALVES)]
         turned = [keep.tile([P, T], F32, name=f"turned{h}") for h in range(HALVES)]
@@ -311,38 +325,35 @@ def tile_moe_tk_lin_silu_kernel(tc, xT, w8_words, w8_scales, w4_words, w4_scales
         def turn_back(back, h, c):
             nc.tensor.transpose(back[:, c * P : (c + 1) * P], turned[h][:, c * P : (c + 1) * P], ident[:])
 
-        plain = {(h, r): keep.tile([P, T], F32, name=f"plain{h}_{r}") for h, r in ON_SCALAR}
+        tags = [f"w8_late{e0}_1" for e0, e1 in HALF1_BATCHES] + ["plain2", "plain3"]
+        plain = {key: keep.tile([P, T], F32, name=f"plain{i}", tag=tags[i], align_bytes=ALIGN) for i, key in enumerate(ON_SCALAR)}
         runs = [slice(t0, t0 + T // 2) for t0 in (0, T // 2)]
         for h, r in ON_SCALAR:
             nc.scalar.activation(plain[h, r][:], y[h][:].indirect(pos_sb[r][:]), COPY)
-        for h in range(HALVES):
-            for r in range(TOP):
-                if (h, r) in ON_SCALAR:
-                    for run in runs if (h, r) == ON_SCALAR[-1] else [slice(0, T)]:
-                        nc.vector.tensor_tensor(part[h][r][:, run], plain[h, r][:, run], gates[:, r, run], MULT)
-                else:
-                    nc.vector.tensor_tensor(part[h][r][:], y[h][:].indirect(pos_sb[r][:]), gates[:, r, :], MULT)
+        for h, r in ((0, 0), (0, 1), (0, 2), (1, 0), (0, 3), (1, 2), (1, 1), (1, 3)):
+            if (h, r) in ON_SCALAR:
+                for run in runs if (h, r) == ON_SCALAR[-1] else [slice(0, T)]:
+                    nc.vector.tensor_tensor(part[h][r][:, run], plain[h, r][:, run], gates[:, r, run], MULT)
+            else:
+                nc.vector.tensor_tensor(part[h][r][:], y[h][:].indirect(pos_sb[r][:]), gates[:, r, :], MULT)
         last_bank = HALF1_BANK[E - 1]
-        four = bank(last_bank)
-        for r in range(TOP):
+        sums = [bank(last_bank), bank(last_bank + 1)]
+        summed = ((0, 1, 2, 3), (0, 2))
+        for h, r in ((0, 0), (0, 1), (0, 2), (1, 0), (0, 3), (1, 2)):
             for c in range(CHUNKS):
-                add_turned(four[:, c * P : (c + 1) * P], 0, r, c, r == 0 and c == 0, r == TOP - 1 and c == CHUNKS - 1)
-        nc.scalar.copy(turned[0][:], four[:])
-        back = bank(last_bank + 1)
-        for c in range(CHUNKS):
-            turn_back(back, 0, c)
-        nc.scalar.copy(total[0][:], back[:])
+                start = r == summed[h][0] and c == 0
+                stop = r == summed[h][-1] and c == CHUNKS - 1
+                add_turned(sums[h][:, c * P : (c + 1) * P], h, r, c, start, stop)
+        back = [bank(last_bank + 2), bank(last_bank + 3)]
+        for h in range(HALVES):
+            nc.scalar.copy(turned[h][:], sums[h][:])
+            for c in range(CHUNKS):
+                turn_back(back[h], h, c)
+        nc.scalar.copy(total[0][:], back[0][:])
         nc.sync.dma_start(out=out[0:P, :], in_=total[0][:])
-        sums = [bank(last_bank + 2 + c) for c in range(CHUNKS)]
-        for r in range(2):
-            for c in range(CHUNKS):
-                add_turned(sums[c][:, 0:P], 1, r, c, r == 0, r == 1)
-        two = bank(last_bank + 2 + CHUNKS)
-        for c in range(CHUNKS):
-            nc.scalar.copy(turned[1][:, c * P : (c + 1) * P], sums[c][:, 0:P])
-            turn_back(two, 1, c)
+        two = back[1]
         for run in runs:
-            nc.vector.tensor_tensor(three[:, run], part[1][2][:, run], part[1][3][:, run], ADD)
+            nc.vector.tensor_tensor(three[:, run], part[1][1][:, run], part[1][3][:, run], ADD)
         for run in runs:
             nc.vector.tensor_tensor(total[1][:, run], three[:, run], two[:, run], ADD)
             nc.sync.dma_start(out=out[P:N, run], in_=total[1][:, run])

@@ -209,7 +209,7 @@ def tile_moe_tk_lin_silu_kernel(tc, xT, w8_words, w8_scales, w4_words, w4_scales
         nc.sync.dma_start(out=gate_rows[0:TOP, :], in_=gate[:, 0, :])
         for r in range(4):
             nc.sync.dma_start(out=w_planes[r:P:QUADRANT].bitcast(I32), in_=w4_scale_rows[r:16:4])
-        w8_planes = keep.tile([P, E * PASSES8, N], U8, name="w8_planes", tag="raw1", align_bytes=ALIGN)
+        w8_planes = keep.tile([P, E * PASSES8, N], U8, name="w8_planes", tag="raw2", align_bytes=ALIGN)
         for r in range(4):
             nc.scalar.dma_start(out=w8_planes[W8_ROW + r : P : QUADRANT].bitcast(I32), in_=w8_scale_rows[r:16:4])
         load_w8(0, 2)
@@ -229,7 +229,7 @@ def tile_moe_tk_lin_silu_kernel(tc, xT, w8_words, w8_scales, w4_words, w4_scales
                 nc.tensor.transpose(spread[:, c * P : (c + 1) * P], gate_cols[:, c, r : r + 1].to_broadcast([P, P]), ident[:])
             nc.scalar.copy(gates[:, r, :], spread[:])
 
-        shifted = {a: keep.tile([P, S], U8, name=f"shifted{a}", tag=f"raw{a - 1}", align_bytes=ALIGN) for a in SHIFTED}
+        shifted = {a: keep.tile([P, S], U8, name=f"shifted{a}", tag=f"raw{2 * a - 5}", align_bytes=ALIGN) for a in SHIFTED}
 
         gather_words(first, 0, MANY, WORD_COLUMN[second])
         quantise(second)

@@ -330,12 +330,15 @@ def tile_moe_tk_lin_silu_kernel(tc, xT, w8_words, w8_scales, w4_words, w4_scales
         runs = [slice(t0, t0 + T // 2) for t0 in (0, T // 2)]
         for h, r in ON_SCALAR:
             nc.scalar.activation(plain[h, r][:], y[h][:].indirect(pos_sb[r][:]), COPY)
-        for h, r in ((0, 0), (0, 1), (0, 2), (1, 0), (0, 3), (1, 2), (1, 1), (1, 3)):
+        for h, r in ((0, 0), (0, 1), (0, 2), (1, 0), (0, 3), (1, 2), (1, 3)):
             if (h, r) in ON_SCALAR:
-                for run in runs if (h, r) == ON_SCALAR[-1] else [slice(0, T)]:
-                    nc.vector.tensor_tensor(part[h][r][:, run], plain[h, r][:, run], gates[:, r, run], MULT)
+                nc.vector.tensor_tensor(part[h][r][:], plain[h, r][:], gates[:, r, :], MULT)
             else:
                 nc.vector.tensor_tensor(part[h][r][:], y[h][:].indirect(pos_sb[r][:]), gates[:, r, :], MULT)
+        part[1][1] = keep.tile([P, T], F32, name="last_part", tag=tags[1], align_bytes=ALIGN)
+        for run in runs:
+            offsets = pos_sb[1][:, run.start // 16 : run.stop // 16]
+            nc.vector.tensor_tensor(part[1][1][:, run], y[1][:].indirect(offsets), gates[:, 1, run], MULT)
         last_bank = HALF1_BANK[E - 1]
         sums = [bank(last_bank), bank(last_bank + 1)]
         summed = ((0, 1, 2, 3), (0, 2))

@@ -79,7 +79,7 @@ def tile_moe_tk_lin_silu_kernel(tc, xT, w8_words, w8_scales, w4_words, w4_scales
         for a in ORDER[2:]:
             raw[a] = keep.tile([P, 4, T], F32, name=f"raw{a}", align_bytes=ALIGN)[:]
         grouped = [keep.tile([P, T, 4], BF16, name=f"grouped{a}", align_bytes=ALIGN) for a in range(PASSES)]
-        slot_words = [keep.tile([P, FEW if a in ORDER[2:] else S], U32, name=f"slot_words{a}", align_bytes=ALIGN) for a in range(PASSES)]
+        slot_words = [keep.tile([P, FEW if a in ORDER[2:] else S], U32, name=f"slot_words{a}", align_bytes=ALIGN) if a != 3 else None for a in range(PASSES)]
         slot_planes = keep.tile([P, S], U8, name="slot_planes", align_bytes=ALIGN)
         y = [keep.tile([P, S], F32, name=f"y{h}") for h in range(HALVES)]
         gate_rows = keep.tile([P, T], F32, name="gate_rows")
@@ -239,11 +239,12 @@ def tile_moe_tk_lin_silu_kernel(tc, xT, w8_words, w8_scales, w4_words, w4_scales
         gather_words(second, FEW, 2 * FEW, WORD_COLUMN[1] + PIECE)
         quantise(2)
         gather_words(second, 2 * FEW, S, WORD_COLUMN[2] + PIECE)
+        gather_words(1, 0, FEW, WORD_COLUMN[3])
         quantise(3)
 
-        gather_words(1, 0, FEW // 2, WORD_COLUMN[3] + PIECE)
+        gather_words(2, 0, FEW // 2, WORD_COLUMN[3] + PIECE)
         nc.vector.tensor_copy(out=packed[0:FIFTH, 0:T].bitcast(I32), in_=planes[0:FIFTH, 0:T].bitcast(I32))
-        gather_words(1, FEW // 2, FEW, WORD_COLUMN[3] + T)
+        gather_words(2, FEW // 2, FEW, WORD_COLUMN[3] + T)
         gather_planes(0, FEW, NARROW)
         shift_planes(0, FEW)
         load_w4(*BATCHES[1])
@@ -263,7 +264,7 @@ def tile_moe_tk_lin_silu_kernel(tc, xT, w8_words, w8_scales, w4_words, w4_scales
             step = 1 if e1 == E else e1 - e0
             for e in range(e0, e1, step):
                 load_w8_half(e, e + step, 1)
-        gather_words(2, 0, FEW, WORD_COLUMN[3] + T)
+        slot_words[3] = keep.tile([P, FEW], U32, name="slot_words3", tag="planes", align_bytes=ALIGN)
         gather_words(3, 0, FEW, WORD_COLUMNS)
         late_words = keep.tile([P, len(ORDER[2:]) * (S - FEW)], U32, name="late_words", tag="packed", align_bytes=ALIGN)
 

@@ -35,13 +35,14 @@ SHIFTED = (3, 4)
 FIFTH = P - 16
 ORDER = (4, 0, 1, 2, 3)
 PIECE = 128
-PIECES = [(t, t + PIECE) for t in range(0, T, PIECE)]
-TWO_PIECES = [(0, PIECE), (PIECE, T)]
+QUANTISE_PIECES = (((0, PIECE), (PIECE, T)),) * 2 + (((0, T),), ((0, PIECE), (PIECE, T)), ((0, 2 * PIECE), (2 * PIECE, T)))
+VECTOR_SHARE = (160, 80)
 FEW, NARROW = 512, 704
 PACKED = 1376
 MANY, WIDE = 10 * C, 1712
-WORD_COLUMN = (WIDE, WIDE + NARROW, WIDE + NARROW + T, WIDE + NARROW + 2 * T, 0)
-WORD_COLUMNS = WORD_COLUMN[3] + NARROW
+WORD_COLUMN = (WIDE, WIDE + NARROW + T, WIDE + NARROW + 2 * T, WIDE + NARROW, 0)
+WORD_COLUMNS = WORD_COLUMN[2] + NARROW
+RAW = 4 * 4 * T
 BATCHES = ((0, 4), (4, 6), (6, 8), (8, 10), (10, 12))
 LATE = 8
 FIRST_BANK = (0, 0, 4, 0, 4)
@@ -57,6 +58,7 @@ def tile_moe_tk_lin_silu_kernel(tc, xT, w8_words, w8_scales, w4_words, w4_scales
     with ExitStack() as ctx:
         lists = ctx.enter_context(tc.tile_pool(name="lists", bufs=1))
         keep = ctx.enter_context(tc.tile_pool(name="keep", bufs=1))
+        reused = ctx.enter_context(tc.tile_pool(name="reused", bufs=1))
         psum = ctx.enter_context(tc.psum_pool(name="psum", bufs=1))
 
         offs_sb = lists.tile([P, S // 16], U16, name="offs_sb")
@@ -74,12 +76,12 @@ def tile_moe_tk_lin_silu_kernel(tc, xT, w8_words, w8_scales, w4_words, w4_scales
         }
         bias = keep.tile([P, HALVES, E], F32, name="bias")
         gates = keep.tile([P, TOP, T], F32, name="gates")
-        early = keep.tile([P, 2, 4, T], F32, name="early", align_bytes=ALIGN)
-        raw = {a: early[:, i] for i, a in enumerate(ORDER[:2])}
-        for a in ORDER[2:]:
-            raw[a] = keep.tile([P, 4, T], F32, name=f"raw{a}", align_bytes=ALIGN)[:]
+        raw = {a: reused.tile([P, 4, T], F32, name=f"raw{a}", align_bytes=ALIGN, offset=i * RAW)[:] for i, a in enumerate(ORDER)}
         grouped = [keep.tile([P, T, 4], BF16, name=f"grouped{a}", align_bytes=ALIGN) for a in range(PASSES)]
-        slot_words = [keep.tile([P, FEW if a in ORDER[2:] else S], U32, name=f"slot_words{a}", align_bytes=ALIGN) if a != 3 else None for a in range(PASSES)]
+        held = {
+            (4, 0): keep.tile([P, MANY], U32, name="words4", align_bytes=ALIGN),
+            (0, 0): keep.tile([P, FEW], U32, name="words0", align_bytes=ALIGN),
+        }
         slot_planes = keep.tile([P, S], U8, name="slot_planes", align_bytes=ALIGN)
         y = [keep.tile([P, S], F32, name=f"y{h}") for h in range(HALVES)]
         gate_rows = keep.tile([P, T], F32, name="gate_rows")
@@ -115,7 +117,7 @@ def tile_moe_tk_lin_silu_kernel(tc, xT, w8_words, w8_scales, w4_words, w4_scales
 
         def quantise(a):
             column, row = (T, 0) if a == ORDER[0] else (0, PLANE_ROW[a])
-            for t0, t1 in PIECES if a == ORDER[0] else TWO_PIECES:
+            for t0, t1 in QUANTISE_PIECES[a]:
                 nc.vector.quantize_mx(
                     out=words[:, WORD_COLUMN[a] + t0 : WORD_COLUMN[a] + t1].bitcast(FP8X4),
                     scales=planes[row:P, column + t0 : column + t1],
@@ -129,15 +131,16 @@ def tile_moe_tk_lin_silu_kernel(tc, xT, w8_words, w8_scales, w4_words, w4_scales
             )
 
         def slots(a, j0, j1):
-            if a in ORDER[2:] and j0 >= FEW:
-                column = (a - 1) * (S - FEW) - FEW
-                return late_words[:, column + j0 : column + j1]
-            return slot_words[a][:, j0:j1]
+            begin = max(j for b, j in held if b == a and j <= j0)
+            return held[a, begin][:, j0 - begin : j1 - begin]
 
-        def gather_words(a, j0, j1, end):
+        def over_raw(shape, dtype, name, i, byte):
+            return reused.tile(shape, dtype, name=name, align_bytes=ALIGN, offset=i * RAW + byte)
+
+        def gather_words(a, j0, j1):
             nc.vector.tensor_copy(
                 out=slots(a, j0, j1),
-                in_=words[:, WORD_COLUMN[a] : end].bitcast(U32).indirect(offs_sb[:, j0 // 16 : j1 // 16]),
+                in_=words[:, WORD_COLUMN[a] : WORD_COLUMN[a] + (WIDE if j1 - j0 > FEW else NARROW)].bitcast(U32).indirect(offs_sb[:, j0 // 16 : j1 // 16]),
             )
 
         def gather_planes(j0, j1, end):
@@ -176,7 +179,7 @@ def tile_moe_tk_lin_silu_kernel(tc, xT, w8_words, w8_scales, w4_words, w4_scales
             nc.scalar.activation(y[h][:, e * C : (e + 1) * C], acc, SILU, bias=bias[:, h, e : e + 1])
 
         first, second = ORDER[:2]
-        for t0, t1 in ((0, 2 * PIECE), (2 * PIECE, T)):
+        for t0, t1 in QUANTISE_PIECES[first]:
             nc.sync.dma_start(out=raw[first][:, :, t0:t1], in_=x_rows[first][:, :, t0:t1])
         nc.sync.dma_start(offs_sb[:], offs)
 
@@ -184,16 +187,15 @@ def tile_moe_tk_lin_silu_kernel(tc, xT, w8_words, w8_scales, w4_words, w4_scales
         nc.scalar.activation(gate_rows[:], zero[:].to_broadcast([P, T]), SILU)
         nc.vector.memset(planes[:].bitcast(I32), 0)
         nc.vector.memset(packed[:, T:].bitcast(I32), 0)
-        for a, end in ((4, WORD_COLUMN[0]), (0, WORD_COLUMN[1]), (3, WORD_COLUMNS)):
+        for a, end in ((4, WORD_COLUMN[0]), (0, WORD_COLUMN[3]), (2, WORD_COLUMNS)):
             nc.vector.memset(words[:, WORD_COLUMN[a] + T : end], 0)
         make_identity(nc, ident[:])
         for a in ORDER[1:-1]:
             load_x(a)
 
-        nc.vector.tensor_copy(*interleaved(first, *PIECES[0]))
-        nc.scalar.activation(*interleaved(first, *PIECES[1]), COPY)
-        nc.vector.tensor_copy(*interleaved(first, 2 * PIECE, T - PIECE // 2))
-        nc.scalar.activation(*interleaved(first, T - PIECE // 2, T), COPY)
+        for t0, t1, t2 in ((0, VECTOR_SHARE[0], 2 * PIECE), (2 * PIECE, 2 * PIECE + VECTOR_SHARE[1], T)):
+            nc.vector.tensor_copy(*interleaved(first, t0, t1))
+            nc.scalar.activation(*interleaved(first, t1, t2), COPY)
         quantise(first)
         for q in range(4):
             nc.sync.dma_start(
@@ -204,12 +206,12 @@ def tile_moe_tk_lin_silu_kernel(tc, xT, w8_words, w8_scales, w4_words, w4_scales
 
         for a in ORDER[1:]:
             nc.scalar.activation(*interleaved(a, 0, T), COPY)
-        w_planes = keep.tile([P, E * PASSES4, N], U8, name="w_planes", tag="early", align_bytes=ALIGN)
+        w_planes = over_raw([P, E * PASSES4, N], U8, "w_planes", 0, 0)
 
         nc.sync.dma_start(out=gate_rows[0:TOP, :], in_=gate[:, 0, :])
         for r in range(4):
             nc.sync.dma_start(out=w_planes[r:P:QUADRANT].bitcast(I32), in_=w4_scale_rows[r:16:4])
-        w8_planes = keep.tile([P, E * PASSES8, N], U8, name="w8_planes", tag="raw2", align_bytes=ALIGN)
+        w8_planes = over_raw([P, E * PASSES8, N], U8, "w8_planes", 2, 4 * FEW)
         for r in range(4):
             nc.scalar.dma_start(out=w8_planes[W8_ROW + r : P : QUADRANT].bitcast(I32), in_=w8_scale_rows[r:16:4])
         load_w8(0, 2)
@@ -229,22 +231,28 @@ def tile_moe_tk_lin_silu_kernel(tc, xT, w8_words, w8_scales, w4_words, w4_scales
                 nc.tensor.transpose(spread[:, c * P : (c + 1) * P], gate_cols[:, c, r : r + 1].to_broadcast([P, P]), ident[:])
             nc.scalar.copy(gates[:, r, :], spread[:])
 
-        shifted = {a: keep.tile([P, S], U8, name=f"shifted{a}", tag=f"raw{2 * a - 5}", align_bytes=ALIGN) for a in SHIFTED}
+        shifted = {a: over_raw([P, S], U8, f"shifted{a}", 4, 2 * FEW + i * S) for i, a in enumerate(SHIFTED)}
 
-        gather_words(first, 0, MANY, WORD_COLUMN[second])
+        gather_words(first, 0, MANY)
         quantise(second)
-        gather_words(first, MANY, S, WORD_COLUMN[second] + PIECE)
-        gather_words(second, 0, FEW, WORD_COLUMN[1])
+        held[first, MANY] = over_raw([P, S - MANY], U32, "words4b", 1, RAW // 2)
+        gather_words(first, MANY, S)
+        gather_words(second, 0, FEW)
         quantise(1)
-        gather_words(second, FEW, 2 * FEW, WORD_COLUMN[1] + PIECE)
+        held[second, FEW] = over_raw([P, FEW], U32, "words0b", 2, 0)
+        gather_words(second, FEW, 2 * FEW)
         quantise(2)
-        gather_words(second, 2 * FEW, S, WORD_COLUMN[2] + PIECE)
-        gather_words(1, 0, FEW, WORD_COLUMN[3])
+        held[second, 2 * FEW] = over_raw([P, FEW], U32, "words0c", 3, 4 * FEW)
+        held[1, 0] = over_raw([P, FEW], U32, "words1", 3, 8 * FEW)
+        gather_words(second, 2 * FEW, S)
+        gather_words(1, 0, FEW)
         quantise(3)
 
-        gather_words(2, 0, FEW // 2, WORD_COLUMN[3] + PIECE)
+        held[2, 0] = over_raw([P, FEW // 2], U32, "words2", 4, 0)
+        gather_words(2, 0, FEW // 2)
         nc.vector.tensor_copy(out=packed[0:FIFTH, 0:T].bitcast(I32), in_=planes[0:FIFTH, 0:T].bitcast(I32))
-        gather_words(2, FEW // 2, FEW, WORD_COLUMN[3] + T)
+        held[2, FEW // 2] = keep.tile([P, FEW // 2], U32, name="words2b", tag="grouped3", align_bytes=ALIGN)
+        gather_words(2, FEW // 2, FEW)
         gather_planes(0, FEW, NARROW)
         shift_planes(0, FEW)
         load_w4(*BATCHES[1])
@@ -264,9 +272,11 @@ def tile_moe_tk_lin_silu_kernel(tc, xT, w8_words, w8_scales, w4_words, w4_scales
             step = 1 if e1 == E else e1 - e0
             for e in range(e0, e1, step):
                 load_w8_half(e, e + step, 1)
-        slot_words[3] = keep.tile([P, FEW], U32, name="slot_words3", tag="planes", align_bytes=ALIGN)
-        gather_words(3, 0, FEW, WORD_COLUMNS)
+        held[3, 0] = keep.tile([P, FEW], U32, name="words3", tag="planes", align_bytes=ALIGN)
+        gather_words(3, 0, FEW)
         late_words = keep.tile([P, len(ORDER[2:]) * (S - FEW)], U32, name="late_words", tag="packed", align_bytes=ALIGN)
+        for i, a in enumerate(ORDER[2:]):
+            held[a, FEW] = late_words[:, i * (S - FEW) : (i + 1) * (S - FEW)]
 
         waiting = {}
 
@@ -281,7 +291,7 @@ def tile_moe_tk_lin_silu_kernel(tc, xT, w8_words, w8_scales, w4_words, w4_scales
                 for a in ORDER[2:]:
                     step = 1 if last and a == ORDER[-1] else e1 - e0
                     for e in range(e0, e1, step):
-                        gather_words(a, e * C, (e + step) * C, WORD_COLUMN[a] + NARROW)
+                        gather_words(a, e * C, (e + step) * C)
             groups = [(e, h) for h in range(HALVES) for e in range(e0, e1) if h == 0 or e < LATE]
             accs = {group: bank(first_bank + i)[:, 0:C] for i, group in enumerate(groups)}
             if last:

@@ -40,8 +40,8 @@ VECTOR_SHARE = (160, 80)
 FEW, NARROW = 512, 704
 PACKED = 1376
 MANY, WIDE = 10 * C, 1712
-WORD_COLUMN = (WIDE, WIDE + NARROW + T, WIDE + NARROW + 2 * T, WIDE + NARROW, 0)
-WORD_COLUMNS = WORD_COLUMN[2] + NARROW
+WORD_COLUMN = tuple((PASSES - 1 - list(ORDER).index(a)) * T for a in range(PASSES))
+WORD_COLUMNS = WORD_COLUMN[ORDER[0]] + WIDE
 RAW = 4 * 4 * T
 BATCHES = ((0, 4), (4, 6), (6, 8), (8, 10), (10, 12))
 LATE = 8
@@ -51,6 +51,7 @@ AHEAD = BATCHES[3:4]
 HALF1_BATCHES = BATCHES[3:]
 HALF1_BANK = {8: 2, 9: 3, 10: 6, 11: 7}
 ON_SCALAR = ((0, 2), (0, 3), (1, 2), (1, 3))
+LAST_PART = (1, 1)
 
 
 def tile_moe_tk_lin_silu_kernel(tc, xT, w8_words, w8_scales, w4_words, w4_scales, b, gate, offs, pos1, pos2, pos3, pos4, out):
@@ -140,7 +141,7 @@ def tile_moe_tk_lin_silu_kernel(tc, xT, w8_words, w8_scales, w4_words, w4_scales
         def gather_words(a, j0, j1):
             nc.vector.tensor_copy(
                 out=slots(a, j0, j1),
-                in_=words[:, WORD_COLUMN[a] : WORD_COLUMN[a] + (WIDE if j1 - j0 > FEW else NARROW)].bitcast(U32).indirect(offs_sb[:, j0 // 16 : j1 // 16]),
+                in_=words[:, WORD_COLUMN[a] : WORD_COLUMN[a] + {MANY: WIDE, 2 * FEW: PACKED}.get(j1 - j0, NARROW)].bitcast(U32).indirect(offs_sb[:, j0 // 16 : j1 // 16]),
             )
 
         def gather_planes(j0, j1, end):
@@ -187,8 +188,7 @@ def tile_moe_tk_lin_silu_kernel(tc, xT, w8_words, w8_scales, w4_words, w4_scales
         nc.scalar.activation(gate_rows[:], zero[:].to_broadcast([P, T]), SILU)
         nc.vector.memset(planes[:].bitcast(I32), 0)
         nc.vector.memset(packed[:, T:].bitcast(I32), 0)
-        for a, end in ((4, WORD_COLUMN[0]), (0, WORD_COLUMN[3]), (2, WORD_COLUMNS)):
-            nc.vector.memset(words[:, WORD_COLUMN[a] + T : end], 0)
+        nc.vector.memset(words[:, PASSES * T :], 0)
         make_identity(nc, ident[:])
         for a in ORDER[1:-1]:
             load_x(a)
@@ -211,7 +211,7 @@ def tile_moe_tk_lin_silu_kernel(tc, xT, w8_words, w8_scales, w4_words, w4_scales
         nc.sync.dma_start(out=gate_rows[0:TOP, :], in_=gate[:, 0, :])
         for r in range(4):
             nc.sync.dma_start(out=w_planes[r:P:QUADRANT].bitcast(I32), in_=w4_scale_rows[r:16:4])
-        w8_planes = over_raw([P, E * PASSES8, N], U8, "w8_planes", 2, 4 * FEW)
+        w8_planes = over_raw([P, E * PASSES8, N], U8, "w8_planes", 2, 8 * FEW)
         for r in range(4):
             nc.scalar.dma_start(out=w8_planes[W8_ROW + r : P : QUADRANT].bitcast(I32), in_=w8_scale_rows[r:16:4])
         load_w8(0, 2)
@@ -239,12 +239,10 @@ def tile_moe_tk_lin_silu_kernel(tc, xT, w8_words, w8_scales, w4_words, w4_scales
         gather_words(first, MANY, S)
         gather_words(second, 0, FEW)
         quantise(1)
-        held[second, FEW] = over_raw([P, FEW], U32, "words0b", 2, 0)
-        gather_words(second, FEW, 2 * FEW)
+        held[second, FEW] = over_raw([P, S - FEW], U32, "words0b", 2, 0)
+        gather_words(second, FEW, S)
         quantise(2)
-        held[second, 2 * FEW] = over_raw([P, FEW], U32, "words0c", 3, 4 * FEW)
         held[1, 0] = over_raw([P, FEW], U32, "words1", 3, 8 * FEW)
-        gather_words(second, 2 * FEW, S)
         gather_words(1, 0, FEW)
         quantise(3)
 
@@ -325,13 +323,13 @@ def tile_moe_tk_lin_silu_kernel(tc, xT, w8_words, w8_scales, w4_words, w4_scales
         for e in (E - 2, E - 1):
             silu(waiting[e], e, 1)
 
-        part = [[keep.tile([P, T], F32, name=f"part{h}_{r}") for r in range(TOP)] for h in range(HALVES)]
+        part = {(h, r): keep.tile([P, T], F32, name=f"part{h}_{r}") for h in range(HALVES) for r in range(TOP) if (h, r) != LAST_PART}
         turned = [keep.tile([P, T], F32, name=f"turned{h}") for h in range(HALVES)]
         three = keep.tile([P, T], F32, name="three")
         total = [keep.tile([P, T], F32, name=f"total{h}", align_bytes=ALIGN) for h in range(HALVES)]
 
         def add_turned(acc, h, r, c, start, stop):
-            nc.tensor.matmul(acc, part[h][r][:, c * P : (c + 1) * P], ident[:], start=start, stop=stop, is_transpose=True)
+            nc.tensor.matmul(acc, part[h, r][:, c * P : (c + 1) * P], ident[:], start=start, stop=stop, is_transpose=True)
 
         def turn_back(back, h, c):
             nc.tensor.transpose(back[:, c * P : (c + 1) * P], turned[h][:, c * P : (c + 1) * P], ident[:])
@@ -341,15 +339,18 @@ def tile_moe_tk_lin_silu_kernel(tc, xT, w8_words, w8_scales, w4_words, w4_scales
         runs = [slice(t0, t0 + T // 2) for t0 in (0, T // 2)]
         for h, r in ON_SCALAR:
             nc.scalar.activation(plain[h, r][:], y[h][:].indirect(pos_sb[r][:]), COPY)
-        for h, r in ((0, 0), (0, 1), (0, 2), (1, 0), (0, 3), (1, 2), (1, 3)):
+        for h, r in ((0, 0), (0, 1), (0, 2), (1, 0), (0, 3), (1, 2)):
             if (h, r) in ON_SCALAR:
-                nc.vector.tensor_tensor(part[h][r][:], plain[h, r][:], gates[:, r, :], MULT)
+                nc.vector.tensor_tensor(part[h, r][:], plain[h, r][:], gates[:, r, :], MULT)
             else:
-                nc.vector.tensor_tensor(part[h][r][:], y[h][:].indirect(pos_sb[r][:]), gates[:, r, :], MULT)
-        part[1][1] = keep.tile([P, T], F32, name="last_part", tag=tags[1], align_bytes=ALIGN)
-        for run in runs:
+                nc.vector.tensor_tensor(part[h, r][:], y[h][:].indirect(pos_sb[r][:]), gates[:, r, :], MULT)
+        last_part = []
+        for i, run in enumerate(runs):
+            last_part.append(keep.tile([P, T // 2], F32, name=f"last_part{i}", tag=tags[1 + i], align_bytes=ALIGN))
             offsets = pos_sb[1][:, run.start // 16 : run.stop // 16]
-            nc.vector.tensor_tensor(part[1][1][:, run], y[1][:].indirect(offsets), gates[:, 1, run], MULT)
+            nc.vector.tensor_tensor(last_part[i][:], y[1][:].indirect(offsets), gates[:, 1, run], MULT)
+            if i == 0:
+                nc.vector.tensor_tensor(part[1, 3][:], plain[1, 3][:], gates[:, 3, :], MULT)
         last_bank = HALF1_BANK[E - 1]
         sums = [bank(last_bank), bank(last_bank + 1)]
         summed = ((0, 1, 2, 3), (0, 2))
@@ -366,8 +367,8 @@ def tile_moe_tk_lin_silu_kernel(tc, xT, w8_words, w8_scales, w4_words, w4_scales
         nc.scalar.copy(total[0][:], back[0][:])
         nc.sync.dma_start(out=out[0:P, :], in_=total[0][:])
         two = back[1]
-        for run in runs:
-            nc.vector.tensor_tensor(three[:, run], part[1][1][:, run], part[1][3][:, run], ADD)
+        for i, run in enumerate(runs):
+            nc.vector.tensor_tensor(three[:, run], last_part[i][:], part[1, 3][:, run], ADD)
         for run in runs:
             nc.vector.tensor_tensor(total[1][:, run], three[:, run], two[:, run], ADD)
             nc.sync.dma_start(out=out[P:N, run], in_=total[1][:, run])

@@ -332,11 +332,11 @@ def tile_moe_tk_lin_silu_kernel(tc, xT, w8_words, w8_scales, w4_words, w4_scales
             nc.tensor.matmul(acc, part[h, r][:, c * P : (c + 1) * P], ident[:], start=start, stop=stop, is_transpose=True)
 
         def turn_back(back, h, c):
-            nc.tensor.transpose(back[:, c * P : (c + 1) * P], turned[h][:, c * P : (c + 1) * P], ident[:])
+            nc.tensor.transpose(back, turned[h][:, c * P : (c + 1) * P], ident[:])
 
-        tags = [f"w8_late{e0}_1" for e0, e1 in HALF1_BATCHES] + ["plain2", "plain3"]
+        tags = ["plain0", f"w8_late{E - 2}_1", "plain2", "plain3"]
         plain = {key: keep.tile([P, T], F32, name=f"plain{i}", tag=tags[i], align_bytes=ALIGN) for i, key in enumerate(ON_SCALAR)}
-        runs = [slice(t0, t0 + T // 2) for t0 in (0, T // 2)]
+        runs = [slice(0, 2 * P), slice(2 * P, T)]
         for h, r in ON_SCALAR:
             nc.scalar.activation(plain[h, r][:], y[h][:].indirect(pos_sb[r][:]), COPY)
         for h, r in ((0, 0), (0, 1), (0, 2), (1, 0), (0, 3), (1, 2)):
@@ -346,29 +346,31 @@ def tile_moe_tk_lin_silu_kernel(tc, xT, w8_words, w8_scales, w4_words, w4_scales
                 nc.vector.tensor_tensor(part[h, r][:], y[h][:].indirect(pos_sb[r][:]), gates[:, r, :], MULT)
         last_part = []
         for i, run in enumerate(runs):
-            last_part.append(keep.tile([P, T // 2], F32, name=f"last_part{i}", tag=tags[1 + i], align_bytes=ALIGN))
+            last_part.append(keep.tile([P, run.stop - run.start], F32, name=f"last_part{i}", tag=tags[1 + i], align_bytes=ALIGN))
             offsets = pos_sb[1][:, run.start // 16 : run.stop // 16]
             nc.vector.tensor_tensor(last_part[i][:], y[1][:].indirect(offsets), gates[:, 1, run], MULT)
             if i == 0:
                 nc.vector.tensor_tensor(part[1, 3][:], plain[1, 3][:], gates[:, 3, :], MULT)
         last_bank = HALF1_BANK[E - 1]
-        sums = [bank(last_bank), bank(last_bank + 1)]
+        pieces = [(0, slice(0, T))] + [(1, run) for run in runs]
+        sums = [bank(last_bank + i) for i in range(len(pieces))]
         summed = ((0, 1, 2, 3), (0, 2))
         for h, r in ((0, 0), (0, 1), (0, 2), (1, 0), (0, 3), (1, 2)):
-            for c in range(CHUNKS):
-                start = r == summed[h][0] and c == 0
-                stop = r == summed[h][-1] and c == CHUNKS - 1
-                add_turned(sums[h][:, c * P : (c + 1) * P], h, r, c, start, stop)
-        back = [bank(last_bank + 2), bank(last_bank + 3)]
-        for h in range(HALVES):
-            nc.scalar.copy(turned[h][:], sums[h][:])
-            for c in range(CHUNKS):
-                turn_back(back[h], h, c)
+            for (half, run), acc in zip(pieces, sums):
+                chunks = range(run.start // P, run.stop // P) if half == h else ()
+                for c in chunks:
+                    start = r == summed[h][0] and c == chunks[0]
+                    stop = r == summed[h][-1] and c == chunks[-1]
+                    add_turned(acc[:, c * P - run.start : (c + 1) * P - run.start], h, r, c, start, stop)
+        back = [bank(last_bank + len(pieces) + i) for i in range(len(pieces))]
+        for (h, run), acc, turned_back in zip(pieces, sums, back):
+            nc.scalar.copy(turned[h][:, run], acc[:, 0 : run.stop - run.start])
+            for c in range(run.start // P, run.stop // P):
+                turn_back(turned_back[:, c * P - run.start : (c + 1) * P - run.start], h, c)
         nc.scalar.copy(total[0][:], back[0][:])
         nc.sync.dma_start(out=out[0:P, :], in_=total[0][:])
-        two = back[1]
         for i, run in enumerate(runs):
             nc.vector.tensor_tensor(three[:, run], last_part[i][:], part[1, 3][:, run], ADD)
-        for run in runs:
-            nc.vector.tensor_tensor(total[1][:, run], three[:, run], two[:, run], ADD)
+        for run, two in zip(runs, back[1:]):
+            nc.vector.tensor_tensor(total[1][:, run], three[:, run], two[:, 0 : run.stop - run.start], ADD)
             nc.sync.dma_start(out=out[P:N, run], in_=total[1][:, run])

from contextlib import ExitStack

import concourse.mybir as mybir
from concourse.masks import make_identity

K, T, E, C, N, TOP = 2560, 384, 12, 128, 256, 4
S = E * C
P = 128
PASSES, PASSES8 = 5, 2
PASSES4 = PASSES - PASSES8
HALVES = N // P
CHUNKS = T // P
BANKS = 8
FLOPS = 2 * S * K * N
BYTES = 4 * K * T + E * N * (PASSES8 * (512 + 16) + PASSES4 * (256 + 16)) + 4 * N * E + 4 * TOP * T + 2 * P * (S + TOP * T) // 16 + 4 * N * T

F32 = mybir.dt.float32
BF16 = mybir.dt.bfloat16
I32 = mybir.dt.int32
U32 = mybir.dt.uint32
U16 = mybir.dt.uint16
U8 = mybir.dt.uint8
FP8X4 = mybir.dt.float8_e4m3fn_x4
FP4X4 = mybir.dt.float4_e2m1fn_x4
COPY = mybir.ActivationFunctionType.Copy
SILU = mybir.ActivationFunctionType.Silu
MULT = mybir.AluOpType.mult
ADD = mybir.AluOpType.add

ALIGN = 256
QUADRANT = 32
W8_ROW = 4
PLANE_ROW = (4, 12, 0, 8)
SHIFTED = (3, 4)
FIFTH = P - 16
ORDER = (4, 0, 1, 2, 3)
PIECE = 128
QUANTISE_PIECES = (((0, PIECE), (PIECE, T)),) * 2 + (((0, T),), ((0, PIECE), (PIECE, T)), ((0, 2 * PIECE), (2 * PIECE, T)))
VECTOR_SHARE = (160, 80)
FEW, NARROW = 512, 704
PACKED = 1376
MANY, WIDE = 10 * C, 1712
WORD_COLUMN = tuple((PASSES - 1 - list(ORDER).index(a)) * T for a in range(PASSES))
WORD_COLUMNS = WORD_COLUMN[ORDER[0]] + WIDE
RAW = 4 * 4 * T
BATCHES = ((0, 4), (4, 6), (6, 8), (8, 10), (10, 12))
LATE = 8
FIRST_BANK = (0, 0, 4, 0, 4)
HALF1_ORDER = (3, 2, 4, 0, 1)
AHEAD = BATCHES[3:4]
HALF1_BATCHES = BATCHES[3:]
HALF1_BANK = {8: 2, 9: 3, 10: 6, 11: 7}
ON_SCALAR = ((0, 2), (0, 3), (1, 2), (1, 3))
LAST_PART = (1, 1)


def tile_moe_tk_lin_silu_kernel(tc, xT, w8_words, w8_scales, w4_words, w4_scales, b, gate, offs, pos1, pos2, pos3, pos4, out):
    nc = tc.nc
    with ExitStack() as ctx:
        lists = ctx.enter_context(tc.tile_pool(name="lists", bufs=1))
        keep = ctx.enter_context(tc.tile_pool(name="keep", bufs=1))
        reused = ctx.enter_context(tc.tile_pool(name="reused", bufs=1))
        psum = ctx.enter_context(tc.psum_pool(name="psum", bufs=1))

        offs_sb = lists.tile([P, S // 16], U16, name="offs_sb")
        pos_sb = [lists.tile([P, T // 16], U16, name=f"pos_sb{r}") for r in range(TOP)]

        words = keep.tile([P, WORD_COLUMNS], I32, name="words", align_bytes=ALIGN)
        planes = keep.tile([P, 2 * T], U8, name="planes", align_bytes=ALIGN)
        packed = keep.tile([P, PACKED], U8, name="packed", align_bytes=ALIGN)
        w8 = keep.tile([P, LATE * PASSES8, 4 * N], U8, name="w8", align_bytes=ALIGN)
        w4 = keep.tile([P, E * PASSES4, 2 * N], U8, name="w4", align_bytes=ALIGN)
        w8_late = {
            (e0, h): keep.tile([P, (e1 - e0) * PASSES8, 4 * P], U8, name=f"w8_late{e0}_{h}", align_bytes=ALIGN)
            for e0, e1 in HALF1_BATCHES
            for h in range(HALVES)
        }
        bias = keep.tile([P, HALVES, E], F32, name="bias")
        gates = keep.tile([P, TOP, T], F32, name="gates")
        raw = {a: reused.tile([P, 4, T], F32, name=f"raw{a}", align_bytes=ALIGN, offset=i * RAW)[:] for i, a in enumerate(ORDER)}
        grouped = [keep.tile([P, T, 4], BF16, name=f"grouped{a}", align_bytes=ALIGN) for a in range(PASSES)]
        held = {
            (4, 0): keep.tile([P, MANY], U32, name="words4", align_bytes=ALIGN),
            (0, 0): keep.tile([P, FEW], U32, name="words0", align_bytes=ALIGN),
        }
        slot_planes = keep.tile([P, S], U8, name="slot_planes", align_bytes=ALIGN)
        y = [keep.tile([P, S], F32, name=f"y{h}") for h in range(HALVES)]
        gate_rows = keep.tile([P, T], F32, name="gate_rows")
        gate_cols = keep.tile([P, CHUNKS, TOP], F32, name="gate_cols")
        ident = keep.tile([P, P], F32, name="ident")
        zero = keep.tile([P, 1], F32, name="zero")

        x_rows = xT.rearrange("(a p j) t -> a p j t", p=P, j=4)
        w8_rows = w8_words.rearrange("e a p n r -> p (e a) (n r)").bitcast(I32)
        w4_rows = w4_words.rearrange("e a p n -> p (e a) n").bitcast(I32)
        w8_scale_rows = w8_scales.rearrange("e a q n -> q (e a) n").bitcast(I32)
        w4_scale_rows = w4_scales.rearrange("e a q n -> q (e a) n").bitcast(I32)

        def load_x(a):
            nc.sync.dma_start(out=raw[a], in_=x_rows[a])

        def load_w8(e0, e1):
            rows = slice(e0 * PASSES8, e1 * PASSES8)
            nc.sync.dma_start(out=w8[:, rows].bitcast(I32), in_=w8_rows[:, rows])

        def load_w4(e0, e1):
            rows = slice(e0 * PASSES4, e1 * PASSES4)
            nc.sync.dma_start(out=w4[:, rows].bitcast(I32), in_=w4_rows[:, rows])

        def load_w8_half(e0, e1, h):
            nc.sync.dma_start(
                out=w8_late[e0 - e0 % 2, h][:, e0 % 2 * PASSES8 : (e0 % 2 + e1 - e0) * PASSES8].bitcast(I32),
                in_=w8_rows[:, e0 * PASSES8 : e1 * PASSES8, h * P : (h + 1) * P],
            )

        def bank(i):
            return psum.tile([P, T], F32, name=f"bank{i % BANKS}")

        def quantise(a):
            column, row = (T, 0) if a == ORDER[0] else (0, PLANE_ROW[a])
            for t0, t1 in QUANTISE_PIECES[a]:
                nc.vector.quantize_mx(
                    out=words[:, WORD_COLUMN[a] + t0 : WORD_COLUMN[a] + t1].bitcast(FP8X4),
                    scales=planes[row:P, column + t0 : column + t1],
                    in_=grouped[a][:, t0:t1, :].rearrange("p t j -> p (t j)"),
                )

        def interleaved(a, t0, t1):
            return (
                grouped[a][:, t0:t1, :].rearrange("p (c i) j -> p c j i", i=4),
                raw[a][:, :, t0:t1].rearrange("p j (c i) -> p c j i", i=4),
            )

        def slots(a, j0, j1):
            begin = max(j for b, j in held if b == a and j <= j0)
            return held[a, begin][:, j0 - begin : j1 - begin]

        def over_raw(shape, dtype, name, i, byte):
            return reused.tile(shape, dtype, name=name, align_bytes=ALIGN, offset=i * RAW + byte)

        def gather_words(a, j0, j1):
            nc.vector.tensor_copy(
                out=slots(a, j0, j1),
                in_=words[:, WORD_COLUMN[a] : WORD_COLUMN[a] + {MANY: WIDE, 2 * FEW: PACKED}.get(j1 - j0, NARROW)].bitcast(U32).indirect(offs_sb[:, j0 // 16 : j1 // 16]),
            )

        def gather_planes(j0, j1, end):
            nc.vector.tensor_copy(out=slot_planes[:, j0:j1], in_=packed[:, 0:end].indirect(offs_sb[:, j0 // 16 : j1 // 16]))

        def shift_planes(j0, j1):
            row = PLANE_ROW[3]
            nc.sync.dma_start(out=shifted[3][0:FIFTH, j0:j1].bitcast(I32), in_=slot_planes[row : row + FIFTH, j0:j1].bitcast(I32))
            for q in range(4):
                nc.sync.dma_start(
                    out=shifted[4][QUADRANT * q : QUADRANT * q + 4, j0:j1].bitcast(I32),
                    in_=slot_planes[FIFTH + 4 * q : FIFTH + 4 * q + 4, j0:j1].bitcast(I32),
                )

        def multiply(acc, a, e, h, start, stop):
            cols = slice(e * C, (e + 1) * C)
            if a < PASSES8:
                i = e * PASSES8 + a
                lhsT = (w8[:, i, 4 * P * h : 4 * P * (h + 1)] if e < LATE else w8_late[e - e % 2, h][:, e % 2 * PASSES8 + a]).bitcast(FP8X4)
                lhsT_scale = w8_planes[W8_ROW:P, i, P * h : P * (h + 1)]
            else:
                i = e * PASSES4 + a - PASSES8
                lhsT = w4[:, i, 2 * P * h : 2 * P * (h + 1)].bitcast(FP4X4)
                lhsT_scale = w_planes[:, i, P * h : P * (h + 1)]
            nc.tensor.matmul_mx(
                out=acc,
                lhsT=lhsT,
                lhsT_scale=lhsT_scale,
                rhs=slots(a, e * C, (e + 1) * C).bitcast(FP8X4),
                rhs_scale=shifted[a][:, cols] if a in SHIFTED else slot_planes[PLANE_ROW[a] : P, cols],
                start=start,
                stop=stop,
            )

        def silu(acc, e, h):
            nc.scalar.activation(y[h][:, e * C : (e + 1) * C], acc, SILU, bias=bias[:, h, e : e + 1])

        first, second = ORDER[:2]
        for t0, t1 in QUANTISE_PIECES[first]:
            nc.sync.dma_start(out=raw[first][:, :, t0:t1], in_=x_rows[first][:, :, t0:t1])
        nc.sync.dma_start(offs_sb[:], offs)

        nc.vector.memset(zero[:], 0.0)
        nc.scalar.activation(gate_rows[:], zero[:].to_broadcast([P, T]), SILU)
        nc.vector.memset(planes[:].bitcast(I32), 0)
        nc.vector.memset(packed[:, T:].bitcast(I32), 0)
        nc.vector.memset(words[:, PASSES * T :], 0)
        make_identity(nc, ident[:])
        for a in ORDER[1:-1]:
            load_x(a)

        for t0, t1, t2 in ((0, VECTOR_SHARE[0], 2 * PIECE), (2 * PIECE, 2 * PIECE + VECTOR_SHARE[1], T)):
            nc.vector.tensor_copy(*interleaved(first, t0, t1))
            nc.scalar.activation(*interleaved(first, t1, t2), COPY)
        quantise(first)
        for q in range(4):
            nc.sync.dma_start(
                out=packed[FIFTH + 4 * q : FIFTH + 4 * q + 4, 0:T].bitcast(I32),
                in_=planes[QUADRANT * q : QUADRANT * q + 4, T : 2 * T].bitcast(I32),
            )
        load_x(ORDER[-1])

        for a in ORDER[1:]:
            nc.scalar.activation(*interleaved(a, 0, T), COPY)
        w_planes = over_raw([P, E * PASSES4, N], U8, "w_planes", 0, 0)

        nc.sync.dma_start(out=gate_rows[0:TOP, :], in_=gate[:, 0, :])
        for r in range(4):
            nc.sync.dma_start(out=w_planes[r:P:QUADRANT].bitcast(I32), in_=w4_scale_rows[r:16:4])
        w8_planes = over_raw([P, E * PASSES8, N], U8, "w8_planes", 2, 8 * FEW)
        for r in range(4):
            nc.scalar.dma_start(out=w8_planes[W8_ROW + r : P : QUADRANT].bitcast(I32), in_=w8_scale_rows[r:16:4])
        load_w8(0, 2)
        nc.sync.dma_start(out=bias[:], in_=b.rearrange("(h p) e -> p h e", p=P))
        load_w8(2, 4)
        load_w4(0, 2)
        load_w4(2, 4)
        load_w8(*BATCHES[1])

        turned_gate = bank(0)
        for c in range(CHUNKS):
            nc.tensor.transpose(turned_gate[:, c * P : (c + 1) * P], gate_rows[:, c * P : (c + 1) * P], ident[:])
        nc.scalar.copy(gate_cols[:], turned_gate[:].rearrange("p (c r) -> p c r", c=CHUNKS)[:, :, 0:TOP])
        for r in range(TOP):
            spread = bank(1 + r)
            for c in range(CHUNKS):
                nc.tensor.transpose(spread[:, c * P : (c + 1) * P], gate_cols[:, c, r : r + 1].to_broadcast([P, P]), ident[:])
            nc.scalar.copy(gates[:, r, :], spread[:])

        shifted = {a: over_raw([P, S], U8, f"shifted{a}", 4, 2 * FEW + i * S) for i, a in enumerate(SHIFTED)}

        gather_words(first, 0, MANY)
        quantise(second)
        held[first, MANY] = over_raw([P, S - MANY], U32, "words4b", 1, RAW // 2)
        gather_words(first, MANY, S)
        gather_words(second, 0, FEW)
        quantise(1)
        held[second, FEW] = over_raw([P, S - FEW], U32, "words0b", 2, 0)
        gather_words(second, FEW, S)
        quantise(2)
        held[1, 0] = over_raw([P, FEW], U32, "words1", 3, 8 * FEW)
        gather_words(1, 0, FEW)
        quantise(3)

        held[2, 0] = over_raw([P, FEW // 2], U32, "words2", 4, 0)
        gather_words(2, 0, FEW // 2)
        nc.vector.tensor_copy(out=packed[0:FIFTH, 0:T].bitcast(I32), in_=planes[0:FIFTH, 0:T].bitcast(I32))
        held[2, FEW // 2] = keep.tile([P, FEW // 2], U32, name="words2b", tag="grouped3", align_bytes=ALIGN)
        gather_words(2, FEW // 2, FEW)
        gather_planes(0, FEW, NARROW)
        shift_planes(0, FEW)
        load_w4(*BATCHES[1])
        load_w8(*BATCHES[2])
        load_w4(*BATCHES[2])
        gather_planes(FEW, S, PACKED)
        shift_planes(FEW, S)
        for e0, e1 in BATCHES[3:]:
            load_w8_half(e0, e1, 0)
            step = 1 if e1 == E else e1 - e0
            for e in range(e0, e1, step):
                load_w4(e, e + step)
        inverse = (pos1, pos2, pos3, pos4)
        for i, (e0, e1) in enumerate(HALF1_BATCHES):
            for r in range(2 * i, min(2 * i + 2, TOP)):
                nc.sync.dma_start(pos_sb[r][:], inverse[r])
            step = 1 if e1 == E else e1 - e0
            for e in range(e0, e1, step):
                load_w8_half(e, e + step, 1)
        held[3, 0] = keep.tile([P, FEW], U32, name="words3", tag="planes", align_bytes=ALIGN)
        gather_words(3, 0, FEW)
        late_words = keep.tile([P, len(ORDER[2:]) * (S - FEW)], U32, name="late_words", tag="packed", align_bytes=ALIGN)
        for i, a in enumerate(ORDER[2:]):
            held[a, FEW] = late_words[:, i * (S - FEW) : (i + 1) * (S - FEW)]

        waiting = {}

        def open_half1(e):
            waiting[e] = bank(HALF1_BANK[e])[:, 0:C]
            for a in HALF1_ORDER[:PASSES4]:
                multiply(waiting[e], a, e, 1, a == HALF1_ORDER[0], False)

        for (e0, e1), first_bank in zip(BATCHES, FIRST_BANK):
            last = e1 == E
            if e0 > 0:
                for a in ORDER[2:]:
                    step = 1 if last and a == ORDER[-1] else e1 - e0
                    for e in range(e0, e1, step):
                        gather_words(a, e * C, (e + step) * C)
            groups = [(e, h) for h in range(HALVES) for e in range(e0, e1) if h == 0 or e < LATE]
            accs = {group: bank(first_bank + i)[:, 0:C] for i, group in enumerate(groups)}
            if last:
                order = (0, 1, 4, 2, 3)
                steps = [(a, group) for a in order[:PASSES8] for group in groups]
                steps += [(a, group) for group in groups for a in order[PASSES8:]]
            elif e0 == 0:
                order = range(PASSES)
                steps = [(a, group) for a in order if a not in SHIFTED for group in groups]
                steps += [(a, group) for group in groups for a in SHIFTED]
            else:
                order = range(PASSES)
                steps = [(a, group) for group in groups for a in order]
            for a, (e, h) in steps:
                multiply(accs[e, h], a, e, h, a == order[0], a == order[-1])
                if a == order[-1]:
                    silu(accs[e, h], e, h)
            if (e0, e1) in AHEAD:
                for e in range(e0, e1):
                    open_half1(e)
        shared = bank(HALF1_BANK[E - 1])
        for i, e in enumerate((E - 1, E - 2)):
            waiting[e] = shared[:, i * C : (i + 1) * C]
            for a in HALF1_ORDER[:PASSES4]:
                multiply(waiting[e], a, e, 1, i == 0 and a == HALF1_ORDER[0], False)
        for e in range(LATE, E):
            for a in HALF1_ORDER[PASSES4:]:
                multiply(waiting[e], a, e, 1, False, a == HALF1_ORDER[-1] and e != E - 2)
            if e < E - 2:
                silu(waiting[e], e, 1)
        for e in (E - 2, E - 1):
            silu(waiting[e], e, 1)

        part = {(h, r): keep.tile([P, T], F32, name=f"part{h}_{r}") for h in range(HALVES) for r in range(TOP) if (h, r) != LAST_PART}
        turned = [keep.tile([P, T], F32, name=f"turned{h}") for h in range(HALVES)]
        three = keep.tile([P, T], F32, name="three")
        total = [keep.tile([P, T], F32, name=f"total{h}", align_bytes=ALIGN) for h in range(HALVES)]

        def add_turned(acc, h, r, c, start, stop):
            nc.tensor.matmul(acc, part[h, r][:, c * P : (c + 1) * P], ident[:], start=start, stop=stop, is_transpose=True)

        def turn_back(back, h, c):
            nc.tensor.transpose(back, turned[h][:, c * P : (c + 1) * P], ident[:])

        tags = ["plain0", f"w8_late{E - 2}_1", "plain2", "plain3"]
        plain = {key: keep.tile([P, T], F32, name=f"plain{i}", tag=tags[i], align_bytes=ALIGN) for i, key in enumerate(ON_SCALAR)}
        runs = [slice(0, 2 * P), slice(2 * P, T)]
        for h, r in ON_SCALAR:
            nc.scalar.activation(plain[h, r][:], y[h][:].indirect(pos_sb[r][:]), COPY)
        for h, r in ((0, 0), (0, 1), (0, 2), (1, 0), (0, 3), (1, 2)):
            if (h, r) in ON_SCALAR:
                nc.vector.tensor_tensor(part[h, r][:], plain[h, r][:], gates[:, r, :], MULT)
            else:
                nc.vector.tensor_tensor(part[h, r][:], y[h][:].indirect(pos_sb[r][:]), gates[:, r, :], MULT)
        last_part = []
        for i, run in enumerate(runs):
            last_part.append(keep.tile([P, run.stop - run.start], F32, name=f"last_part{i}", tag=tags[1 + i], align_bytes=ALIGN))
            offsets = pos_sb[1][:, run.start // 16 : run.stop // 16]
            nc.vector.tensor_tensor(last_part[i][:], y[1][:].indirect(offsets), gates[:, 1, run], MULT)
            if i == 0:
                nc.vector.tensor_tensor(part[1, 3][:], plain[1, 3][:], gates[:, 3, :], MULT)
        last_bank = HALF1_BANK[E - 1]
        pieces = [(0, slice(0, T))] + [(1, run) for run in runs]
        sums = [bank(last_bank + i) for i in range(len(pieces))]
        summed = ((0, 1, 2, 3), (0, 2))
        for h, r in ((0, 0), (0, 1), (0, 2), (1, 0), (0, 3), (1, 2)):
            for (half, run), acc in zip(pieces, sums):
                chunks = range(run.start // P, run.stop // P) if half == h else ()
                for c in chunks:
                    start = r == summed[h][0] and c == chunks[0]
                    stop = r == summed[h][-1] and c == chunks[-1]
                    add_turned(acc[:, c * P - run.start : (c + 1) * P - run.start], h, r, c, start, stop)
        back = [bank(last_bank + len(pieces) + i) for i in range(len(pieces))]
        for (h, run), acc, turned_back in zip(pieces, sums, back):
            nc.scalar.copy(turned[h][:, run], acc[:, 0 : run.stop - run.start])
            for c in range(run.start // P, run.stop // P):
                turn_back(turned_back[:, c * P - run.start : (c + 1) * P - run.start], h, c)
        nc.scalar.copy(total[0][:], back[0][:])
        nc.sync.dma_start(out=out[0:P, :], in_=total[0][:])
        for i, run in enumerate(runs):
            nc.vector.tensor_tensor(three[:, run], last_part[i][:], part[1, 3][:, run], ADD)
        for run, two in zip(runs, back[1:]):
            nc.vector.tensor_tensor(total[1][:, run], three[:, run], two[:, 0 : run.stop - run.start], ADD)
            nc.sync.dma_start(out=out[P:N, run], in_=total[1][:, run])
